import numpy as np
import ml_dtypes


def mxq(x, axis, fmt="e4m3"):
    dtype, down = {"e4m3": (ml_dtypes.float8_e4m3fn, 7), "e5m2": (ml_dtypes.float8_e5m2, 14)}[fmt]
    v = np.moveaxis(np.asarray(x, np.float32).astype(ml_dtypes.bfloat16).astype(np.float64), axis, -1)
    blocks = v.reshape(v.shape[:-1] + (-1, 32))
    amax = np.abs(blocks).max(-1, keepdims=True)
    byte = np.maximum(np.where(amax > 0, np.frexp(amax)[1] - 1 + 127, 0) - down, 1)
    scale = np.exp2(byte - 127.0)
    codes = (blocks / scale).astype(np.float32).astype(dtype).astype(np.float64)
    return np.moveaxis((codes * scale).reshape(v.shape), -1, axis)


WIDE = False


def mx_kscale(k):
    if not WIDE:
        return np.ones(k)
    levels = np.array([10, -10, 5, -5, 0])
    if k % 512:
        return np.exp2(np.random.permutation(np.resize(levels, k // 32))).repeat(32)
    a = np.empty((k // 512, 16))
    for p in range(k // 512):
        a[p, :8] = np.random.permutation(np.resize(levels, 8))
        for g in range(8):
            far = levels[np.abs(levels - a[p, g]) >= 10]
            a[p, g + 8] = far[np.random.randint(len(far))]
    return np.exp2(a.ravel()).repeat(32)


def f64(x):
    return np.asarray(x).astype(np.float64)


def striped(idx):
    return np.tile(idx.reshape(-1, 16).T, (8, 1)).astype(np.uint16)


def unstriped(offs):
    return offs[:16].T.reshape(-1).astype(np.int64)


def striped8(idx):
    return np.concatenate([x.reshape(-1, 16).T for x in idx]).astype(np.uint16)


def runs(offs, k):
    lists = np.stack([offs[16 * r : 16 * r + 16].T.reshape(-1) for r in range(8)]).astype(np.int64)
    return lists[np.arange(k) % 512 // 64]


def pack_weight(w):
    k, n = w.shape
    w = f64(np.asarray(w, np.float32).astype(ml_dtypes.bfloat16)).reshape(k // 32, 32, n)
    amax = np.abs(w).max(1)
    byte = np.clip(np.where(amax > 0, np.frexp(amax)[1] - 1 + 127 - 7, 1), 1, 254)
    scaled = (w * np.exp2(127.0 - byte)[:, None, :]).reshape(k, n).astype(np.float32)
    words = np.ascontiguousarray(scaled.reshape(k // 512, 128, 4, n).transpose(0, 1, 3, 2)).astype(ml_dtypes.float8_e4m3fn).view(np.uint8)
    return words, np.ascontiguousarray(byte.astype(np.uint8).reshape(k // 512, 16, n))


def unpack_weight(words, scales):
    g, p, n, _ = words.shape
    vals = np.ascontiguousarray(words).view(ml_dtypes.float8_e4m3fn).astype(np.float64) * np.repeat(np.exp2(scales.astype(np.float64) - 127.0), 8, axis=1)[..., None]
    return vals.transpose(0, 1, 3, 2).reshape(g * 512, n)


K, T, S, N, H = 512, 2048, 512, 512, 512


def setup_inputs():
    n = np.random.standard_normal
    s = mx_kscale(K)[:, None]
    u = mx_kscale(H)
    packed_xT = pack_weight(n((K, T)) * s)
    return {
        "x_words": packed_xT[0],
        "x_scales": packed_xT[1],
        "w1": (n((K, H)) / np.sqrt(K) / s).astype(np.float32),
        "dual": n((H, S)).astype(np.float32),
        "gn": (np.random.uniform(0.5, 1.5, (H, 1)) * u[:, None]).astype(np.float32),
        "w2": (n((H, N)) / np.sqrt(H) / u[:, None]).astype(np.float32),
        "offs": striped(np.random.permutation(T)[:S]),
        "nb": striped8(np.stack([np.random.permutation(S) for _ in range(8)])),
    }


def reference(x_words, x_scales, w1, dual, gn, w2, offs, nb):
    xq = unpack_weight(x_words, x_scales)[:, unstriped(offs)]
    y = mxq(f64(w1), 0, "e4m3").T @ xq
    d = y[np.arange(H)[:, None], runs(nb, H)] - y
    z = f64(gn) * ((f64(dual) + 0.25 * d) / (0.25 * np.abs(d) + 1))
    return mxq(f64(w2), 0, "e4m3").T @ mxq(z, 0, "e4m3")

@@ -1,0 +1,202 @@
+from contextlib import ExitStack
+
+import concourse.mybir as mybir
+
+K, T, S, H, N = 512, 2048, 512, 512, 512
+FLOPS = 2 * K * H * S + 2 * H * N * S
+
+F32 = mybir.dt.float32
+BF16 = mybir.dt.bfloat16
+I32 = mybir.dt.int32
+U32 = mybir.dt.uint32
+U16 = mybir.dt.uint16
+U8 = mybir.dt.uint8
+FP8X4 = mybir.dt.float8_e4m3fn_x4
+ALU = mybir.AluOpType
+ACT = mybir.ActivationFunctionType
+
+P = 128
+PACK = 4
+HALF = S // 2
+CHUNKS = [(0, 256), (256, 128), (384, 128)]
+W1_SPLIT = 80
+W2_SPLIT = 80
+
+
+def tile_picked_tvdual_none_p_kernel(tc, x_words, x_scales, w1, dual, gn, w2, offs, nb, out):
+    nc = tc.nc
+    with ExitStack() as ctx:
+        keep = ctx.enter_context(tc.tile_pool(name="keep", bufs=1))
+        psum = ctx.enter_context(tc.psum_pool(name="psum", bufs=1))
+
+        offs_sb = keep.tile([P, S // 16], U16, name="offs_sb")
+        nb_sb = keep.tile([P, S // 16], U16, name="nb_sb")
+        w1_raw = keep.tile([P, PACK, H], F32, name="w1_raw")
+        w2_raw = keep.tile([P, PACK, N], F32, name="w2_raw")
+        dual_sb = keep.tile([P, PACK, S], F32, name="dual_sb")
+        gn_sb = keep.tile([P, PACK], F32, name="gn_sb")
+        words = keep.tile([P, T], I32, name="words")
+        bytes_win = keep.tile([P, T], U8, name="bytes_win")
+        ones = keep.tile([P, 1], F32, name="ones")
+        warm = keep.tile([P, 1], F32, name="warm")
+
+        nc.vector.memset(bytes_win[:].bitcast(I32), 0)
+        nc.vector.memset(ones[:], 1.0)
+
+        nc.sync.dma_start(offs_sb[:], offs)
+        nc.sync.dma_start(w1_raw[:], w1.rearrange("(p j) c -> p j c", j=PACK))
+        for q in range(4):
+            nc.sync.dma_start(bytes_win[32 * q : 32 * q + 4, :].bitcast(I32), x_scales[0, 4 * q : 4 * q + 4, :].bitcast(I32))
+        nc.sync.dma_start(words[:], x_words[0].rearrange("p n t -> p (n t)").bitcast(I32))
+        nc.scalar.dma_start(gn_sb[:], gn.rearrange("(p t) o -> p (t o)", t=PACK))
+        nc.sync.dma_start(nb_sb[:], nb)
+        nc.sync.dma_start(w2_raw[:], w2.rearrange("(p j) c -> p j c", j=PACK))
+        nc.sync.dma_start(dual_sb[:], dual.rearrange("(p t) n -> p t n", t=PACK))
+        nc.scalar.activation(warm[:], ones[:], ACT.Abs_reciprocal_sqrt, bias=ones[:])
+
+        w1_bf = keep.tile([P, PACK, P, PACK], BF16, name="w1_bf", align_bytes=64)
+        w1_codes = keep.tile([P, H], U32, name="w1_codes", align_bytes=64)
+        w1_scales = keep.tile([P, H], U8, name="w1_scales", align_bytes=64)
+        src = w1_raw[:].rearrange("p j (m t) -> p m t j", t=PACK)
+        dst = w1_bf[:].rearrange("p t m j -> p m t j")
+        x_bytes = keep.tile([P, S], U8, name="x_bytes", align_bytes=64)
+        nc.vector.tensor_copy(x_bytes[:], bytes_win[:].indirect(offs_sb[:]))
+        nc.vector.tensor_copy(dst[:, :W1_SPLIT], src[:, :W1_SPLIT])
+        nc.scalar.copy(dst[:, W1_SPLIT:], src[:, W1_SPLIT:])
+
+        gq = keep.tile([P, PACK], F32, name="gq")
+        gz = keep.tile([P, PACK], F32, name="gz")
+        gs = keep.tile([P, PACK], F32, name="gs")
+        ginv = keep.tile([P, PACK], F32, name="ginv")
+        nc.vector.tensor_scalar(gq[:], gn_sb[:], 0.25, None, ALU.mult)
+        nc.vector.tensor_scalar(gz[:], gn_sb[:], 0.0, None, ALU.is_equal)
+        nc.vector.tensor_tensor(gs[:], gz[:], gn_sb[:], ALU.add)
+        nc.vector.reciprocal(ginv[:], gs[:])
+
+        nc.vector.quantize_mx(out=w1_codes[:].bitcast(FP8X4), scales=w1_scales[:], in_=w1_bf[:].rearrange("p t m j -> p (t m j)"))
+
+        x_codes = [keep.tile([P, HALF], U32, name="x_codes%d" % h, align_bytes=64) for h in range(2)]
+        win = [keep.tile([P, S], F32, name="win%d" % t) for t in range(PACK)]
+        for h in range(2):
+            nc.vector.tensor_copy(x_codes[h][:], words[:].bitcast(U32).indirect(offs_sb[:, h * (HALF // 16) : (h + 1) * (HALF // 16)]))
+        for t, h in [(0, 0), (1, 0), (0, 1), (1, 1), (2, 0), (2, 1), (3, 0), (3, 1)]:
+            if True:
+                y = psum.tile([P, HALF], F32, name="y", tag="bank%d" % (PACK * h + t))
+                nc.tensor.matmul_mx(
+                    out=y[:],
+                    lhsT=w1_codes[:, t * P : (t + 1) * P].bitcast(FP8X4),
+                    lhsT_scale=w1_scales[:, t * P : (t + 1) * P],
+                    rhs=x_codes[h][:].bitcast(FP8X4),
+                    rhs_scale=x_bytes[:, h * HALF : (h + 1) * HALF],
+                    start=True,
+                    stop=True,
+                )
+                cols = slice(h * HALF, (h + 1) * HALF)
+                if h == 1 and t == 0:
+                    nc.vector.tensor_scalar(win[t][:, cols], y[:], gq[:, t : t + 1], None, ALU.mult)
+                else:
+                    nc.scalar.activation(win[t][:, cols], y[:], ACT.Copy, scale=gq[:, t : t + 1])
+
+        w2_bf = keep.tile([P, N, PACK], BF16, name="w2_bf", align_bytes=64)
+        w2_codes = keep.tile([P, N], U32, name="w2_codes", align_bytes=64)
+        w2_scales = keep.tile([P, N], U8, name="w2_scales", align_bytes=64)
+
+        def prepare_w2():
+            dst2 = w2_bf[:].rearrange("p (c i) j -> p c j i", i=2)
+            src2 = w2_raw[:].rearrange("p j (c i) -> p c j i", i=2)
+            nc.scalar.copy(dst2[:, W2_SPLIT:], src2[:, W2_SPLIT:])
+
+        def prepare_w2_rest():
+            dst2 = w2_bf[:].rearrange("p (c i) j -> p c j i", i=2)
+            src2 = w2_raw[:].rearrange("p j (c i) -> p c j i", i=2)
+            nc.vector.tensor_copy(dst2[:, :W2_SPLIT], src2[:, :W2_SPLIT])
+
+        def quantise_w2():
+            nc.vector.quantize_mx(out=w2_codes[:].bitcast(FP8X4), scales=w2_scales[:], in_=w2_bf[:].rearrange("p c j -> p (c j)"))
+
+        diff = [keep.tile([P, S], F32, name="diff%d" % t) for t in range(PACK)]
+        recip = keep.tile([P, PACK, S], F32, name="recip")
+        num = keep.tile([P, PACK, S], F32, name="num")
+        zb, zc, zs = {}, {}, {}
+
+        gots = [keep.tile([P, S], F32, name="got%d" % t) for t in range(PACK)]
+
+        def gather(t, h):
+            nc.vector.tensor_copy(gots[t][:, h * HALF : (h + 1) * HALF], win[t][:].indirect(nb_sb[:, h * (HALF // 16) : (h + 1) * (HALF // 16)]))
+
+        def subtract(t, got):
+            nc.vector.tensor_tensor(diff[t][:], got[:], win[t][:], ALU.subtract)
+
+        def reciprocal(t, pieces):
+            size = keep.tile([P, S], F32, name="size%d" % t)
+            root = keep.tile([P, S], F32, name="root%d" % t)
+            for c0, w in pieces:
+                cols = slice(c0, c0 + w)
+                nc.scalar.activation(size[:, cols], diff[t][:, cols], ACT.Abs, scale=ginv[:, t : t + 1])
+                nc.scalar.activation(root[:, cols], size[:, cols], ACT.Abs_reciprocal_sqrt, bias=ones[:])
+                nc.scalar.activation(recip[:, t, cols], root[:, cols], ACT.Square)
+
+        def numerator(t):
+            nc.vector.scalar_tensor_tensor(num[:, t, :], dual_sb[:, t, :], gn_sb[:, t : t + 1], diff[t][:], ALU.mult, ALU.add)
+
+        def quotient(c):
+            c0, w = CHUNKS[c]
+            zb[c] = keep.tile([P, w, PACK], BF16, name="zb%d" % c, align_bytes=64)
+            nc.vector.tensor_tensor(
+                zb[c][:].rearrange("p (c i) t -> p c t i", i=2),
+                num[:, :, c0 : c0 + w].rearrange("p t (c i) -> p c t i", i=2),
+                recip[:, :, c0 : c0 + w].rearrange("p t (c i) -> p c t i", i=2),
+                ALU.mult,
+            )
+
+        def quantise(c):
+            c0, w = CHUNKS[c]
+            zc[c] = keep.tile([P, w], U32, name="zc%d" % c, align_bytes=64)
+            zs[c] = keep.tile([P, w], U8, name="zs%d" % c, align_bytes=64)
+            nc.vector.quantize_mx(out=zc[c][:].bitcast(FP8X4), scales=zs[c][:], in_=zb[c][:].rearrange("p c t -> p (c t)"))
+
+        def product(c):
+            c0, w = CHUNKS[c]
+            res = keep.tile([P, PACK, w], F32, name="res%d" % c)
+            for u in range(2):
+                acc = psum.tile([P, 2, w], F32, name="acc", tag="bank%d" % (2 * c + u))
+                for v in range(2):
+                    mt = 2 * u + v
+                    nc.tensor.matmul_mx(
+                        out=acc[:, v, :],
+                        lhsT=w2_codes[:, mt * P : (mt + 1) * P].bitcast(FP8X4),
+                        lhsT_scale=w2_scales[:, mt * P : (mt + 1) * P],
+                        rhs=zc[c][:].bitcast(FP8X4),
+                        rhs_scale=zs[c][:],
+                        start=True,
+                        stop=True,
+                    )
+                if c == len(CHUNKS) - 1 and u == 1:
+                    nc.vector.tensor_copy(res[:, 2 * u : 2 * u + 2, :], acc[:])
+                else:
+                    nc.scalar.copy(res[:, 2 * u : 2 * u + 2, :], acc[:])
+            nc.sync.dma_start(out[:, c0 : c0 + w].rearrange("(mt p) n -> p mt n", p=P), res[:])
+
+        whole = [(0, S)]
+        halves = [(0, HALF), (HALF, HALF)]
+        prepare_w2()
+        gather(0, 0)
+        gather(0, 1)
+        for t in range(PACK):
+            if t + 1 < PACK:
+                gather(t + 1, 0)
+            else:
+                prepare_w2_rest()
+            subtract(t, gots[t])
+            if t + 1 < PACK:
+                gather(t + 1, 1)
+            reciprocal(t, halves if t == PACK - 1 else whole)
+        for t in range(PACK):
+            numerator(t)
+        quantise_w2()
+        quotient(0)
+        for c in range(len(CHUNKS)):
+            if c + 1 < len(CHUNKS):
+                quotient(c + 1)
+            quantise(c)
+            product(c)

@@ -20,7 +20,7 @@ PACK = 4
 HALF = S // 2
 CHUNKS = [(0, 256), (256, 128), (384, 128)]
 W1_SPLIT = 80
-W2_SPLIT = 80
+W2_SPLIT = 160
 
 
 def tile_picked_tvdual_none_p_kernel(tc, x_words, x_scales, w1, dual, gn, w2, offs, nb, out):
@@ -46,7 +46,7 @@ def tile_picked_tvdual_none_p_kernel(tc, x_words, x_scales, w1, dual, gn, w2, of
         nc.sync.dma_start(offs_sb[:], offs)
         nc.sync.dma_start(w1_raw[:], w1.rearrange("(p j) c -> p j c", j=PACK))
         for q in range(4):
-            nc.sync.dma_start(bytes_win[32 * q : 32 * q + 4, :].bitcast(I32), x_scales[0, 4 * q : 4 * q + 4, :].bitcast(I32))
+            nc.sync.dma_start(bytes_win[q:P:32, :].bitcast(I32), x_scales[0, q:16:4, :].bitcast(I32))
         nc.sync.dma_start(words[:], x_words[0].rearrange("p n t -> p (n t)").bitcast(I32))
         nc.scalar.dma_start(gn_sb[:], gn.rearrange("(p t) o -> p (t o)", t=PACK))
         nc.sync.dma_start(nb_sb[:], nb)
@@ -76,6 +76,7 @@ def tile_picked_tvdual_none_p_kernel(tc, x_words, x_scales, w1, dual, gn, w2, of
         nc.vector.quantize_mx(out=w1_codes[:].bitcast(FP8X4), scales=w1_scales[:], in_=w1_bf[:].rearrange("p t m j -> p (t m j)"))
 
         x_codes = [keep.tile([P, HALF], U32, name="x_codes%d" % h, align_bytes=64) for h in range(2)]
+        own = [keep.tile([P, S], F32, name="own%d" % t) for t in range(PACK)]
         win = [keep.tile([P, S], F32, name="win%d" % t) for t in range(PACK)]
         for h in range(2):
             nc.vector.tensor_copy(x_codes[h][:], words[:].bitcast(U32).indirect(offs_sb[:, h * (HALF // 16) : (h + 1) * (HALF // 16)]))
@@ -96,6 +97,8 @@ def tile_picked_tvdual_none_p_kernel(tc, x_words, x_scales, w1, dual, gn, w2, of
                     nc.vector.tensor_scalar(win[t][:, cols], y[:], gq[:, t : t + 1], None, ALU.mult)
                 else:
                     nc.scalar.activation(win[t][:, cols], y[:], ACT.Copy, scale=gq[:, t : t + 1])
+                if h == 0 and t < 2:
+                    nc.vector.tensor_scalar(own[t][:, cols], y[:], gq[:, t : t + 1], None, ALU.mult)
 
         w2_bf = keep.tile([P, N, PACK], BF16, name="w2_bf", align_bytes=64)
         w2_codes = keep.tile([P, N], U32, name="w2_codes", align_bytes=64)
@@ -119,13 +122,13 @@ def tile_picked_tvdual_none_p_kernel(tc, x_words, x_scales, w1, dual, gn, w2, of
         num = keep.tile([P, PACK, S], F32, name="num")
         zb, zc, zs = {}, {}, {}
 
-        gots = [keep.tile([P, S], F32, name="got%d" % t) for t in range(PACK)]
+        def duplicate(t):
+            cols = slice(HALF, S) if t < 2 else slice(0, S)
+            nc.vector.tensor_copy(own[t][:, cols], win[t][:, cols])
 
-        def gather(t, h):
-            nc.vector.tensor_copy(gots[t][:, h * HALF : (h + 1) * HALF], win[t][:].indirect(nb_sb[:, h * (HALF // 16) : (h + 1) * (HALF // 16)]))
-
-        def subtract(t, got):
-            nc.vector.tensor_tensor(diff[t][:], got[:], win[t][:], ALU.subtract)
+        def difference(t, h):
+            cols = slice(h * HALF, (h + 1) * HALF)
+            nc.vector.tensor_tensor(diff[t][:, cols], win[t][:].indirect(nb_sb[:, h * (HALF // 16) : (h + 1) * (HALF // 16)]), own[t][:, cols], ALU.subtract)
 
         def reciprocal(t, pieces):
             size = keep.tile([P, S], F32, name="size%d" % t)
@@ -180,17 +183,14 @@ def tile_picked_tvdual_none_p_kernel(tc, x_words, x_scales, w1, dual, gn, w2, of
         whole = [(0, S)]
         halves = [(0, HALF), (HALF, HALF)]
         prepare_w2()
-        gather(0, 0)
-        gather(0, 1)
+        duplicate(0)
         for t in range(PACK):
+            difference(t, 0)
             if t + 1 < PACK:
-                gather(t + 1, 0)
-            else:
-                prepare_w2_rest()
-            subtract(t, gots[t])
-            if t + 1 < PACK:
-                gather(t + 1, 1)
+                duplicate(t + 1)
+            difference(t, 1)
             reciprocal(t, halves if t == PACK - 1 else whole)
+        prepare_w2_rest()
         for t in range(PACK):
             numerator(t)
         quantise_w2()

@@ -18,9 +18,9 @@ ACT = mybir.ActivationFunctionType
 P = 128
 PACK = 4
 HALF = S // 2
-CHUNKS = [(0, 256), (256, 128), (384, 128)]
-W1_SPLIT = 80
-W2_SPLIT = 160
+CHUNKS = [(0, 128), (128, 128), (256, 128), (384, 128)]
+W1_SPLIT = 48
+W2_SPLIT = 40
 
 
 def tile_picked_tvdual_none_p_kernel(tc, x_words, x_scales, w1, dual, gn, w2, offs, nb, out):
@@ -31,7 +31,7 @@ def tile_picked_tvdual_none_p_kernel(tc, x_words, x_scales, w1, dual, gn, w2, of
 
         offs_sb = keep.tile([P, S // 16], U16, name="offs_sb")
         nb_sb = keep.tile([P, S // 16], U16, name="nb_sb")
-        w1_raw = keep.tile([P, PACK, H], F32, name="w1_raw")
+        w1_raw = [keep.tile([P, PACK, H // 2], F32, name="w1_raw%d" % u) for u in range(2)]
         w2_raw = keep.tile([P, PACK, N], F32, name="w2_raw")
         dual_sb = keep.tile([P, PACK, S], F32, name="dual_sb")
         gn_sb = keep.tile([P, PACK], F32, name="gn_sb")
@@ -44,11 +44,13 @@ def tile_picked_tvdual_none_p_kernel(tc, x_words, x_scales, w1, dual, gn, w2, of
         nc.vector.memset(ones[:], 1.0)
 
         nc.sync.dma_start(offs_sb[:], offs)
-        nc.sync.dma_start(w1_raw[:], w1.rearrange("(p j) c -> p j c", j=PACK))
+        w1_rows = w1.rearrange("(p j) c -> p j c", j=PACK)
+        nc.gpsimd.dma_start(gn_sb[:], gn.rearrange("(p t) o -> p (t o)", t=PACK))
+        nc.sync.dma_start(w1_raw[0][:], w1_rows[:, :, : H // 2])
         for q in range(4):
             nc.sync.dma_start(bytes_win[q:P:32, :].bitcast(I32), x_scales[0, q:16:4, :].bitcast(I32))
+        nc.sync.dma_start(w1_raw[1][:], w1_rows[:, :, H // 2 :])
         nc.sync.dma_start(words[:], x_words[0].rearrange("p n t -> p (n t)").bitcast(I32))
-        nc.scalar.dma_start(gn_sb[:], gn.rearrange("(p t) o -> p (t o)", t=PACK))
         nc.sync.dma_start(nb_sb[:], nb)
         nc.sync.dma_start(w2_raw[:], w2.rearrange("(p j) c -> p j c", j=PACK))
         nc.sync.dma_start(dual_sb[:], dual.rearrange("(p t) n -> p t n", t=PACK))
@@ -57,27 +59,30 @@ def tile_picked_tvdual_none_p_kernel(tc, x_words, x_scales, w1, dual, gn, w2, of
         w1_bf = keep.tile([P, PACK, P, PACK], BF16, name="w1_bf", align_bytes=64)
         w1_codes = keep.tile([P, H], U32, name="w1_codes", align_bytes=64)
         w1_scales = keep.tile([P, H], U8, name="w1_scales", align_bytes=64)
-        src = w1_raw[:].rearrange("p j (m t) -> p m t j", t=PACK)
+        src = [w1_raw[u][:].rearrange("p j (m t) -> p m t j", t=PACK) for u in range(2)]
         dst = w1_bf[:].rearrange("p t m j -> p m t j")
         x_bytes = keep.tile([P, S], U8, name="x_bytes", align_bytes=64)
         nc.vector.tensor_copy(x_bytes[:], bytes_win[:].indirect(offs_sb[:]))
-        nc.vector.tensor_copy(dst[:, :W1_SPLIT], src[:, :W1_SPLIT])
-        nc.scalar.copy(dst[:, W1_SPLIT:], src[:, W1_SPLIT:])
+        nc.scalar.copy(dst[:, :64], src[0])
+        nc.vector.tensor_copy(dst[:, 64 : 64 + W1_SPLIT], src[1][:, :W1_SPLIT])
+        nc.scalar.copy(dst[:, 64 + W1_SPLIT :], src[1][:, W1_SPLIT:])
 
         gq = keep.tile([P, PACK], F32, name="gq")
         gz = keep.tile([P, PACK], F32, name="gz")
         gs = keep.tile([P, PACK], F32, name="gs")
         ginv = keep.tile([P, PACK], F32, name="ginv")
-        nc.vector.tensor_scalar(gq[:], gn_sb[:], 0.25, None, ALU.mult)
-        nc.vector.tensor_scalar(gz[:], gn_sb[:], 0.0, None, ALU.is_equal)
-        nc.vector.tensor_tensor(gs[:], gz[:], gn_sb[:], ALU.add)
+        nc.gpsimd.tensor_scalar(gq[:], gn_sb[:], 0.25, None, ALU.mult)
+        nc.gpsimd.tensor_scalar(gz[:], gn_sb[:], 0.0, None, ALU.is_equal)
+        nc.gpsimd.tensor_tensor(gs[:], gz[:], gn_sb[:], ALU.add)
         nc.vector.reciprocal(ginv[:], gs[:])
 
         nc.vector.quantize_mx(out=w1_codes[:].bitcast(FP8X4), scales=w1_scales[:], in_=w1_bf[:].rearrange("p t m j -> p (t m j)"))
 
         x_codes = [keep.tile([P, HALF], U32, name="x_codes%d" % h, align_bytes=64) for h in range(2)]
         own = [keep.tile([P, S], F32, name="own%d" % t) for t in range(PACK)]
-        win = [keep.tile([P, S], F32, name="win%d" % t) for t in range(PACK)]
+        win = [keep.tile([P, S if t == 0 else 2 * S], F32, name="win%d" % t) for t in range(PACK)]
+        for t in range(1, PACK):
+            nc.vector.memset(win[t][:, S:], 0.0)
         for h in range(2):
             nc.vector.tensor_copy(x_codes[h][:], words[:].bitcast(U32).indirect(offs_sb[:, h * (HALF // 16) : (h + 1) * (HALF // 16)]))
         for t, h in [(0, 0), (1, 0), (0, 1), (1, 1), (2, 0), (2, 1), (3, 0), (3, 1)]:
@@ -118,7 +123,7 @@ def tile_picked_tvdual_none_p_kernel(tc, x_words, x_scales, w1, dual, gn, w2, of
             nc.vector.quantize_mx(out=w2_codes[:].bitcast(FP8X4), scales=w2_scales[:], in_=w2_bf[:].rearrange("p c j -> p (c j)"))
 
         diff = [keep.tile([P, S], F32, name="diff%d" % t) for t in range(PACK)]
-        recip = keep.tile([P, PACK, S], F32, name="recip")
+        recip = keep.tile([P, 2, PACK, HALF], F32, name="recip")
         num = keep.tile([P, PACK, S], F32, name="num")
         zb, zc, zs = {}, {}, {}
 
@@ -126,18 +131,20 @@ def tile_picked_tvdual_none_p_kernel(tc, x_words, x_scales, w1, dual, gn, w2, of
             cols = slice(HALF, S) if t < 2 else slice(0, S)
             nc.vector.tensor_copy(own[t][:, cols], win[t][:, cols])
 
-        def difference(t, h):
-            cols = slice(h * HALF, (h + 1) * HALF)
-            nc.vector.tensor_tensor(diff[t][:, cols], win[t][:].indirect(nb_sb[:, h * (HALF // 16) : (h + 1) * (HALF // 16)]), own[t][:, cols], ALU.subtract)
+        def difference(t, c0, w):
+            cols = slice(c0, c0 + w)
+            nc.vector.tensor_tensor(diff[t][:, cols], win[t][:].indirect(nb_sb[:, c0 // 16 : (c0 + w) // 16]), own[t][:, cols], ALU.subtract)
+
+        sizes = [keep.tile([P, S], F32, name="size%d" % t) for t in range(PACK)]
+        roots = [keep.tile([P, S], F32, name="root%d" % t) for t in range(PACK)]
 
         def reciprocal(t, pieces):
-            size = keep.tile([P, S], F32, name="size%d" % t)
-            root = keep.tile([P, S], F32, name="root%d" % t)
+            size, root = sizes[t], roots[t]
             for c0, w in pieces:
                 cols = slice(c0, c0 + w)
                 nc.scalar.activation(size[:, cols], diff[t][:, cols], ACT.Abs, scale=ginv[:, t : t + 1])
                 nc.scalar.activation(root[:, cols], size[:, cols], ACT.Abs_reciprocal_sqrt, bias=ones[:])
-                nc.scalar.activation(recip[:, t, cols], root[:, cols], ACT.Square)
+                nc.scalar.activation(recip[:, c0 // HALF : (c0 + w) // HALF, t, :], root[:, cols].rearrange("p (h n) -> p h n", n=HALF), ACT.Square)
 
         def numerator(t):
             nc.vector.scalar_tensor_tensor(num[:, t, :], dual_sb[:, t, :], gn_sb[:, t : t + 1], diff[t][:], ALU.mult, ALU.add)
@@ -148,7 +155,7 @@ def tile_picked_tvdual_none_p_kernel(tc, x_words, x_scales, w1, dual, gn, w2, of
             nc.vector.tensor_tensor(
                 zb[c][:].rearrange("p (c i) t -> p c t i", i=2),
                 num[:, :, c0 : c0 + w].rearrange("p t (c i) -> p c t i", i=2),
-                recip[:, :, c0 : c0 + w].rearrange("p t (c i) -> p c t i", i=2),
+                recip[:, c0 // HALF, :, c0 % HALF : c0 % HALF + w].rearrange("p t (c i) -> p c t i", i=2),
                 ALU.mult,
             )
 
@@ -178,18 +185,29 @@ def tile_picked_tvdual_none_p_kernel(tc, x_words, x_scales, w1, dual, gn, w2, of
                     nc.vector.tensor_copy(res[:, 2 * u : 2 * u + 2, :], acc[:])
                 else:
                     nc.scalar.copy(res[:, 2 * u : 2 * u + 2, :], acc[:])
-            nc.sync.dma_start(out[:, c0 : c0 + w].rearrange("(mt p) n -> p mt n", p=P), res[:])
+                if c == len(CHUNKS) - 1:
+                    nc.sync.dma_start(out[2 * u * P : (2 * u + 2) * P, c0 : c0 + w].rearrange("(mt p) n -> p mt n", p=P), res[:, 2 * u : 2 * u + 2, :])
+            if c < len(CHUNKS) - 1:
+                nc.sync.dma_start(out[:, c0 : c0 + w].rearrange("(mt p) n -> p mt n", p=P), res[:])
 
         whole = [(0, S)]
         halves = [(0, HALF), (HALF, HALF)]
         prepare_w2()
+        difference(0, 0, HALF)
         duplicate(0)
-        for t in range(PACK):
-            difference(t, 0)
-            if t + 1 < PACK:
-                duplicate(t + 1)
-            difference(t, 1)
-            reciprocal(t, halves if t == PACK - 1 else whole)
+        duplicate(1)
+        difference(0, HALF, HALF)
+        reciprocal(0, whole)
+        difference(1, 0, S)
+        reciprocal(1, whole)
+        duplicate(2)
+        duplicate(3)
+        difference(2, 0, S)
+        reciprocal(2, halves[:1])
+        difference(3, 0, S)
+        reciprocal(3, halves[:1])
+        reciprocal(2, halves[1:])
+        reciprocal(3, halves[1:])
         prepare_w2_rest()
         for t in range(PACK):
             numerator(t)

@@ -18,9 +18,9 @@ ACT = mybir.ActivationFunctionType
 P = 128
 PACK = 4
 HALF = S // 2
-CHUNKS = [(0, 128), (128, 128), (256, 128), (384, 128)]
-W1_SPLIT = 48
-W2_SPLIT = 40
+MH = P // 2
+CHUNK = 128
+W2_ON_VECTOR = 120
 
 
 def tile_picked_tvdual_none_p_kernel(tc, x_words, x_scales, w1, dual, gn, w2, offs, nb, out):
@@ -49,23 +49,28 @@ def tile_picked_tvdual_none_p_kernel(tc, x_words, x_scales, w1, dual, gn, w2, of
         nc.sync.dma_start(w1_raw[0][:], w1_rows[:, :, : H // 2])
         for q in range(4):
             nc.sync.dma_start(bytes_win[q:P:32, :].bitcast(I32), x_scales[0, q:16:4, :].bitcast(I32))
-        nc.sync.dma_start(w1_raw[1][:], w1_rows[:, :, H // 2 :])
         nc.sync.dma_start(words[:], x_words[0].rearrange("p n t -> p (n t)").bitcast(I32))
+        nc.sync.dma_start(w1_raw[1][:], w1_rows[:, :, H // 2 :])
         nc.sync.dma_start(nb_sb[:], nb)
         nc.sync.dma_start(w2_raw[:], w2.rearrange("(p j) c -> p j c", j=PACK))
         nc.sync.dma_start(dual_sb[:], dual.rearrange("(p t) n -> p t n", t=PACK))
         nc.scalar.activation(warm[:], ones[:], ACT.Abs_reciprocal_sqrt, bias=ones[:])
 
-        w1_bf = keep.tile([P, PACK, P, PACK], BF16, name="w1_bf", align_bytes=64)
-        w1_codes = keep.tile([P, H], U32, name="w1_codes", align_bytes=64)
-        w1_scales = keep.tile([P, H], U8, name="w1_scales", align_bytes=64)
+        w1_bf = [[keep.tile([P, 2, MH, PACK], BF16, name="w1_bf%d%d" % (u, g), align_bytes=64) for g in range(2)] for u in range(2)]
+        w1_codes = [keep.tile([P, P], U32, name="w1_codes%d" % t, align_bytes=64) for t in range(PACK)]
+        w1_scales = [keep.tile([P, P], U8, name="w1_scales%d" % t, align_bytes=64) for t in range(PACK)]
         src = [w1_raw[u][:].rearrange("p j (m t) -> p m t j", t=PACK) for u in range(2)]
-        dst = w1_bf[:].rearrange("p t m j -> p m t j")
+        dst = [[w1_bf[u][g][:].rearrange("p t m j -> p m t j") for g in range(2)] for u in range(2)]
+
+        def quantise_w1(t, u):
+            cols = slice(u * MH, (u + 1) * MH)
+            nc.vector.quantize_mx(out=w1_codes[t][:, cols].bitcast(FP8X4), scales=w1_scales[t][:, cols], in_=w1_bf[u][t // 2][:, t % 2].rearrange("p m j -> p (m j)"))
+
         x_bytes = keep.tile([P, S], U8, name="x_bytes", align_bytes=64)
+        x_codes = keep.tile([P, S], U32, name="x_codes", align_bytes=64)
         nc.vector.tensor_copy(x_bytes[:], bytes_win[:].indirect(offs_sb[:]))
-        nc.scalar.copy(dst[:, :64], src[0])
-        nc.vector.tensor_copy(dst[:, 64 : 64 + W1_SPLIT], src[1][:, :W1_SPLIT])
-        nc.scalar.copy(dst[:, 64 + W1_SPLIT :], src[1][:, W1_SPLIT:])
+        for g in range(2):
+            nc.scalar.copy(dst[0][g], src[0][:, :, 2 * g : 2 * g + 2])
 
         gq = keep.tile([P, PACK], F32, name="gq")
         gz = keep.tile([P, PACK], F32, name="gz")
@@ -74,50 +79,60 @@ def tile_picked_tvdual_none_p_kernel(tc, x_words, x_scales, w1, dual, gn, w2, of
         nc.gpsimd.tensor_scalar(gq[:], gn_sb[:], 0.25, None, ALU.mult)
         nc.gpsimd.tensor_scalar(gz[:], gn_sb[:], 0.0, None, ALU.is_equal)
         nc.gpsimd.tensor_tensor(gs[:], gz[:], gn_sb[:], ALU.add)
-        nc.vector.reciprocal(ginv[:], gs[:])
 
-        nc.vector.quantize_mx(out=w1_codes[:].bitcast(FP8X4), scales=w1_scales[:], in_=w1_bf[:].rearrange("p t m j -> p (t m j)"))
-
-        x_codes = [keep.tile([P, HALF], U32, name="x_codes%d" % h, align_bytes=64) for h in range(2)]
         own = [keep.tile([P, S], F32, name="own%d" % t) for t in range(PACK)]
         win = [keep.tile([P, S if t == 0 else 2 * S], F32, name="win%d" % t) for t in range(PACK)]
         for t in range(1, PACK):
             nc.vector.memset(win[t][:, S:], 0.0)
-        for h in range(2):
-            nc.vector.tensor_copy(x_codes[h][:], words[:].bitcast(U32).indirect(offs_sb[:, h * (HALF // 16) : (h + 1) * (HALF // 16)]))
-        for t, h in [(0, 0), (1, 0), (0, 1), (1, 1), (2, 0), (2, 1), (3, 0), (3, 1)]:
-            if True:
-                y = psum.tile([P, HALF], F32, name="y", tag="bank%d" % (PACK * h + t))
-                nc.tensor.matmul_mx(
-                    out=y[:],
-                    lhsT=w1_codes[:, t * P : (t + 1) * P].bitcast(FP8X4),
-                    lhsT_scale=w1_scales[:, t * P : (t + 1) * P],
-                    rhs=x_codes[h][:].bitcast(FP8X4),
-                    rhs_scale=x_bytes[:, h * HALF : (h + 1) * HALF],
-                    start=True,
-                    stop=True,
-                )
-                cols = slice(h * HALF, (h + 1) * HALF)
-                if h == 1 and t == 0:
-                    nc.vector.tensor_scalar(win[t][:, cols], y[:], gq[:, t : t + 1], None, ALU.mult)
-                else:
-                    nc.scalar.activation(win[t][:, cols], y[:], ACT.Copy, scale=gq[:, t : t + 1])
-                if h == 0 and t < 2:
-                    nc.vector.tensor_scalar(own[t][:, cols], y[:], gq[:, t : t + 1], None, ALU.mult)
+        for t in range(PACK):
+            quantise_w1(t, 0)
+        nc.vector.reciprocal(ginv[:], gs[:])
+        nc.vector.tensor_copy(x_codes[:], words[:].bitcast(U32).indirect(offs_sb[:]))
+        nc.vector.tensor_copy(dst[1][0], src[1][:, :, 0:2])
+        nc.scalar.copy(dst[1][1], src[1][:, :, 2:4])
+        for t in range(PACK):
+            quantise_w1(t, 1)
+
+        def first_product(t, c0, w, bank):
+            y = psum.tile([P, w], F32, name="y", tag="bank%d" % bank)
+            nc.tensor.matmul_mx(
+                out=y[:],
+                lhsT=w1_codes[t][:].bitcast(FP8X4),
+                lhsT_scale=w1_scales[t][:],
+                rhs=x_codes[:, c0 : c0 + w].bitcast(FP8X4),
+                rhs_scale=x_bytes[:, c0 : c0 + w],
+                start=True,
+                stop=True,
+            )
+            return y
+
+        def out_scalar(dst_tile, t, c0, w, y):
+            nc.scalar.activation(dst_tile[:, c0 : c0 + w], y[:], ACT.Copy, scale=gq[:, t : t + 1])
+
+        def out_vector(dst_tile, t, c0, w, y):
+            nc.vector.tensor_scalar(dst_tile[:, c0 : c0 + w], y[:], gq[:, t : t + 1], None, ALU.mult)
+
+        y00 = first_product(0, 0, HALF, 0)
+        y01 = first_product(0, HALF, HALF, 1)
+        ys = [first_product(t, 0, S, t + 1) for t in range(1, PACK)]
+        out_scalar(win[0], 0, 0, HALF, y00)
+        out_scalar(own[0], 0, 0, HALF, y00)
+        out_vector(win[0], 0, HALF, HALF, y01)
+        out_vector(own[0], 0, HALF, HALF, y01)
+        for t in range(1, PACK):
+            out_scalar(win[t], t, 0, S, ys[t - 1])
 
         w2_bf = keep.tile([P, N, PACK], BF16, name="w2_bf", align_bytes=64)
         w2_codes = keep.tile([P, N], U32, name="w2_codes", align_bytes=64)
         w2_scales = keep.tile([P, N], U8, name="w2_scales", align_bytes=64)
+        dst2 = w2_bf[:].rearrange("p (c i) j -> p c j i", i=2)
+        src2 = w2_raw[:].rearrange("p j (c i) -> p c j i", i=2)
 
-        def prepare_w2():
-            dst2 = w2_bf[:].rearrange("p (c i) j -> p c j i", i=2)
-            src2 = w2_raw[:].rearrange("p j (c i) -> p c j i", i=2)
-            nc.scalar.copy(dst2[:, W2_SPLIT:], src2[:, W2_SPLIT:])
+        def cast_w2_scalar():
+            nc.scalar.copy(dst2[:, W2_ON_VECTOR:], src2[:, W2_ON_VECTOR:])
 
-        def prepare_w2_rest():
-            dst2 = w2_bf[:].rearrange("p (c i) j -> p c j i", i=2)
-            src2 = w2_raw[:].rearrange("p j (c i) -> p c j i", i=2)
-            nc.vector.tensor_copy(dst2[:, :W2_SPLIT], src2[:, :W2_SPLIT])
+        def cast_w2_vector():
+            nc.vector.tensor_copy(dst2[:, :W2_ON_VECTOR], src2[:, :W2_ON_VECTOR])
 
         def quantise_w2():
             nc.vector.quantize_mx(out=w2_codes[:].bitcast(FP8X4), scales=w2_scales[:], in_=w2_bf[:].rearrange("p c j -> p (c j)"))
@@ -127,9 +142,8 @@ def tile_picked_tvdual_none_p_kernel(tc, x_words, x_scales, w1, dual, gn, w2, of
         num = keep.tile([P, PACK, S], F32, name="num")
         zb, zc, zs = {}, {}, {}
 
-        def duplicate(t):
-            cols = slice(HALF, S) if t < 2 else slice(0, S)
-            nc.vector.tensor_copy(own[t][:, cols], win[t][:, cols])
+        def duplicate(t, c0=0, w=S):
+            nc.vector.tensor_copy(own[t][:, c0 : c0 + w], win[t][:, c0 : c0 + w])
 
         def difference(t, c0, w):
             cols = slice(c0, c0 + w)
@@ -138,19 +152,35 @@ def tile_picked_tvdual_none_p_kernel(tc, x_words, x_scales, w1, dual, gn, w2, of
         sizes = [keep.tile([P, S], F32, name="size%d" % t) for t in range(PACK)]
         roots = [keep.tile([P, S], F32, name="root%d" % t) for t in range(PACK)]
 
-        def reciprocal(t, pieces):
-            size, root = sizes[t], roots[t]
-            for c0, w in pieces:
-                cols = slice(c0, c0 + w)
-                nc.scalar.activation(size[:, cols], diff[t][:, cols], ACT.Abs, scale=ginv[:, t : t + 1])
-                nc.scalar.activation(root[:, cols], size[:, cols], ACT.Abs_reciprocal_sqrt, bias=ones[:])
-                nc.scalar.activation(recip[:, c0 // HALF : (c0 + w) // HALF, t, :], root[:, cols].rearrange("p (h n) -> p h n", n=HALF), ACT.Square)
+        def absolute(t, c0, w):
+            nc.scalar.activation(sizes[t][:, c0 : c0 + w], diff[t][:, c0 : c0 + w], ACT.Abs, scale=ginv[:, t : t + 1])
+
+        def root(t, c0, w):
+            nc.scalar.activation(roots[t][:, c0 : c0 + w], sizes[t][:, c0 : c0 + w], ACT.Abs_reciprocal_sqrt, bias=ones[:])
+
+        def square(t, c0, w):
+            nc.scalar.activation(recip[:, c0 // HALF : (c0 + w) // HALF, t, :], roots[t][:, c0 : c0 + w].rearrange("p (h n) -> p h n", n=HALF), ACT.Square)
+
+        def reciprocal(t, c0, w):
+            absolute(t, c0, w)
+            root(t, c0, w)
+            square(t, c0, w)
+
+        size23 = keep.tile([P, 2, 2, HALF], F32, name="size23")
+        root23 = keep.tile([P, 2, 2, HALF], F32, name="root23")
+
+        def absolute23(t, h):
+            nc.scalar.activation(size23[:, h, t - 2, :], diff[t][:, h * HALF : (h + 1) * HALF], ACT.Abs, scale=ginv[:, t : t + 1])
+
+        def inverse23(h):
+            nc.scalar.activation(root23[:, h], size23[:, h], ACT.Abs_reciprocal_sqrt, bias=ones[:])
+            nc.scalar.activation(recip[:, h, 2:4, :], root23[:, h], ACT.Square)
 
         def numerator(t):
             nc.vector.scalar_tensor_tensor(num[:, t, :], dual_sb[:, t, :], gn_sb[:, t : t + 1], diff[t][:], ALU.mult, ALU.add)
 
         def quotient(c):
-            c0, w = CHUNKS[c]
+            c0, w = c * CHUNK, CHUNK
             zb[c] = keep.tile([P, w, PACK], BF16, name="zb%d" % c, align_bytes=64)
             nc.vector.tensor_tensor(
                 zb[c][:].rearrange("p (c i) t -> p c t i", i=2),
@@ -160,16 +190,17 @@ def tile_picked_tvdual_none_p_kernel(tc, x_words, x_scales, w1, dual, gn, w2, of
             )
 
         def quantise(c):
-            c0, w = CHUNKS[c]
-            zc[c] = keep.tile([P, w], U32, name="zc%d" % c, align_bytes=64)
-            zs[c] = keep.tile([P, w], U8, name="zs%d" % c, align_bytes=64)
+            zc[c] = keep.tile([P, CHUNK], U32, name="zc%d" % c, align_bytes=64)
+            zs[c] = keep.tile([P, CHUNK], U8, name="zs%d" % c, align_bytes=64)
             nc.vector.quantize_mx(out=zc[c][:].bitcast(FP8X4), scales=zs[c][:], in_=zb[c][:].rearrange("p c t -> p (c t)"))
 
+        last = S // CHUNK - 1
+
         def product(c):
-            c0, w = CHUNKS[c]
+            c0, w = c * CHUNK, CHUNK
             res = keep.tile([P, PACK, w], F32, name="res%d" % c)
             for u in range(2):
-                acc = psum.tile([P, 2, w], F32, name="acc", tag="bank%d" % (2 * c + u))
+                acc = psum.tile([P, 2, w], F32, name="acc", tag="bank%d" % ((2 * c + u + 5) % 8))
                 for v in range(2):
                     mt = 2 * u + v
                     nc.tensor.matmul_mx(
@@ -181,40 +212,39 @@ def tile_picked_tvdual_none_p_kernel(tc, x_words, x_scales, w1, dual, gn, w2, of
                         start=True,
                         stop=True,
                     )
-                if c == len(CHUNKS) - 1 and u == 1:
+                if c == last and u == 1:
                     nc.vector.tensor_copy(res[:, 2 * u : 2 * u + 2, :], acc[:])
                 else:
                     nc.scalar.copy(res[:, 2 * u : 2 * u + 2, :], acc[:])
-                if c == len(CHUNKS) - 1:
+                if c == last:
                     nc.sync.dma_start(out[2 * u * P : (2 * u + 2) * P, c0 : c0 + w].rearrange("(mt p) n -> p mt n", p=P), res[:, 2 * u : 2 * u + 2, :])
-            if c < len(CHUNKS) - 1:
+            if c < last:
                 nc.sync.dma_start(out[:, c0 : c0 + w].rearrange("(mt p) n -> p mt n", p=P), res[:])
 
-        whole = [(0, S)]
-        halves = [(0, HALF), (HALF, HALF)]
-        prepare_w2()
         difference(0, 0, HALF)
-        duplicate(0)
-        duplicate(1)
         difference(0, HALF, HALF)
-        reciprocal(0, whole)
-        difference(1, 0, S)
-        reciprocal(1, whole)
+        reciprocal(0, 0, S)
+        duplicate(1)
         duplicate(2)
+        difference(1, 0, S)
+        reciprocal(1, 0, S)
         duplicate(3)
         difference(2, 0, S)
-        reciprocal(2, halves[:1])
+        absolute23(2, 0)
+        absolute23(2, 1)
         difference(3, 0, S)
-        reciprocal(3, halves[:1])
-        reciprocal(2, halves[1:])
-        reciprocal(3, halves[1:])
-        prepare_w2_rest()
+        absolute23(3, 0)
+        inverse23(0)
+        absolute23(3, 1)
+        inverse23(1)
+        cast_w2_scalar()
         for t in range(PACK):
             numerator(t)
-        quantise_w2()
+        cast_w2_vector()
         quotient(0)
-        for c in range(len(CHUNKS)):
-            if c + 1 < len(CHUNKS):
+        quantise_w2()
+        for c in range(last + 1):
+            if c < last:
                 quotient(c + 1)
             quantise(c)
             product(c)

@@ -43,10 +43,10 @@ def tile_picked_tvdual_none_p_kernel(tc, x_words, x_scales, w1, dual, gn, w2, of
         nc.vector.memset(bytes_win[:].bitcast(I32), 0)
         nc.vector.memset(ones[:], 1.0)
 
-        nc.sync.dma_start(offs_sb[:], offs)
         w1_rows = w1.rearrange("(p j) c -> p j c", j=PACK)
         nc.gpsimd.dma_start(gn_sb[:], gn.rearrange("(p t) o -> p (t o)", t=PACK))
         nc.sync.dma_start(w1_raw[0][:], w1_rows[:, :, : H // 2])
+        nc.sync.dma_start(offs_sb[:], offs)
         for q in range(4):
             nc.sync.dma_start(bytes_win[q:P:32, :].bitcast(I32), x_scales[0, q:16:4, :].bitcast(I32))
         nc.sync.dma_start(words[:], x_words[0].rearrange("p n t -> p (n t)").bitcast(I32))
@@ -115,10 +115,10 @@ def tile_picked_tvdual_none_p_kernel(tc, x_words, x_scales, w1, dual, gn, w2, of
         y00 = first_product(0, 0, HALF, 0)
         y01 = first_product(0, HALF, HALF, 1)
         ys = [first_product(t, 0, S, t + 1) for t in range(1, PACK)]
-        out_scalar(win[0], 0, 0, HALF, y00)
-        out_scalar(own[0], 0, 0, HALF, y00)
-        out_vector(win[0], 0, HALF, HALF, y01)
-        out_vector(own[0], 0, HALF, HALF, y01)
+        out_vector(win[0], 0, 0, HALF, y00)
+        out_vector(own[0], 0, 0, HALF, y00)
+        out_scalar(win[0], 0, HALF, HALF, y01)
+        out_scalar(own[0], 0, HALF, HALF, y01)
         for t in range(1, PACK):
             out_scalar(win[t], t, 0, S, ys[t - 1])
 
@@ -199,10 +199,12 @@ def tile_picked_tvdual_none_p_kernel(tc, x_words, x_scales, w1, dual, gn, w2, of
         def product(c):
             c0, w = c * CHUNK, CHUNK
             res = keep.tile([P, PACK, w], F32, name="res%d" % c)
-            for u in range(2):
-                acc = psum.tile([P, 2, w], F32, name="acc", tag="bank%d" % ((2 * c + u + 5) % 8))
-                for v in range(2):
-                    mt = 2 * u + v
+            per = 1 if c == last else 2
+            for u in range(PACK // per):
+                bank = (2 * c + u + 5) % 8
+                acc = psum.tile([P, per, w], F32, name="acc", tag="bank%d" % bank)
+                for v in range(per):
+                    mt = per * u + v
                     nc.tensor.matmul_mx(
                         out=acc[:, v, :],
                         lhsT=w2_codes[:, mt * P : (mt + 1) * P].bitcast(FP8X4),
@@ -212,12 +214,12 @@ def tile_picked_tvdual_none_p_kernel(tc, x_words, x_scales, w1, dual, gn, w2, of
                         start=True,
                         stop=True,
                     )
-                if c == last and u == 1:
-                    nc.vector.tensor_copy(res[:, 2 * u : 2 * u + 2, :], acc[:])
+                rows = slice(per * u, per * (u + 1))
+                if c == last and u % 2 == 1:
+                    nc.vector.tensor_copy(res[:, rows, :], acc[:])
+                    nc.sync.dma_start(out[(u - 1) * P : (u + 1) * P, c0 : c0 + w].rearrange("(mt p) n -> p mt n", p=P), res[:, u - 1 : u + 1, :])
                 else:
-                    nc.scalar.copy(res[:, 2 * u : 2 * u + 2, :], acc[:])
-                if c == last:
-                    nc.sync.dma_start(out[2 * u * P : (2 * u + 2) * P, c0 : c0 + w].rearrange("(mt p) n -> p mt n", p=P), res[:, 2 * u : 2 * u + 2, :])
+                    nc.scalar.copy(res[:, rows, :], acc[:])
             if c < last:
                 nc.sync.dma_start(out[:, c0 : c0 + w].rearrange("(mt p) n -> p mt n", p=P), res[:])
 

@@ -20,7 +20,7 @@ PACK = 4
 HALF = S // 2
 MH = P // 2
 CHUNK = 128
-W2_ON_VECTOR = 120
+W2_ON_VECTOR = 148
 
 
 def tile_picked_tvdual_none_p_kernel(tc, x_words, x_scales, w1, dual, gn, w2, offs, nb, out):
@@ -139,7 +139,7 @@ def tile_picked_tvdual_none_p_kernel(tc, x_words, x_scales, w1, dual, gn, w2, of
 
         diff = [keep.tile([P, S], F32, name="diff%d" % t) for t in range(PACK)]
         recip = keep.tile([P, 2, PACK, HALF], F32, name="recip")
-        num = keep.tile([P, PACK, S], F32, name="num")
+        nums = {}
         zb, zc, zs = {}, {}, {}
 
         def duplicate(t, c0=0, w=S):
@@ -149,42 +149,29 @@ def tile_picked_tvdual_none_p_kernel(tc, x_words, x_scales, w1, dual, gn, w2, of
             cols = slice(c0, c0 + w)
             nc.vector.tensor_tensor(diff[t][:, cols], win[t][:].indirect(nb_sb[:, c0 // 16 : (c0 + w) // 16]), own[t][:, cols], ALU.subtract)
 
-        sizes = [keep.tile([P, S], F32, name="size%d" % t) for t in range(PACK)]
-        roots = [keep.tile([P, S], F32, name="root%d" % t) for t in range(PACK)]
+        def inverse(turn, *pieces):
+            sizes = [keep.tile([P, HALF], F32, name="size", tag="work%d%d" % (i, turn)) for i in range(2)]
+            roots = [keep.tile([P, HALF], F32, name="root", tag="work%d%d" % (i, 1 - turn)) for i in range(2)]
+            for i, (t, h) in enumerate(pieces):
+                nc.scalar.activation(sizes[i][:], diff[t][:, h * HALF : (h + 1) * HALF], ACT.Abs, scale=ginv[:, t : t + 1])
+            for i in range(2):
+                nc.scalar.activation(roots[i][:], sizes[i][:], ACT.Abs_reciprocal_sqrt, bias=ones[:])
+            for i, (t, h) in enumerate(pieces):
+                nc.scalar.activation(recip[:, h, t, :], roots[i][:], ACT.Square)
 
-        def absolute(t, c0, w):
-            nc.scalar.activation(sizes[t][:, c0 : c0 + w], diff[t][:, c0 : c0 + w], ACT.Abs, scale=ginv[:, t : t + 1])
-
-        def root(t, c0, w):
-            nc.scalar.activation(roots[t][:, c0 : c0 + w], sizes[t][:, c0 : c0 + w], ACT.Abs_reciprocal_sqrt, bias=ones[:])
-
-        def square(t, c0, w):
-            nc.scalar.activation(recip[:, c0 // HALF : (c0 + w) // HALF, t, :], roots[t][:, c0 : c0 + w].rearrange("p (h n) -> p h n", n=HALF), ACT.Square)
-
-        def reciprocal(t, c0, w):
-            absolute(t, c0, w)
-            root(t, c0, w)
-            square(t, c0, w)
-
-        size23 = keep.tile([P, 2, 2, HALF], F32, name="size23")
-        root23 = keep.tile([P, 2, 2, HALF], F32, name="root23")
-
-        def absolute23(t, h):
-            nc.scalar.activation(size23[:, h, t - 2, :], diff[t][:, h * HALF : (h + 1) * HALF], ACT.Abs, scale=ginv[:, t : t + 1])
-
-        def inverse23(h):
-            nc.scalar.activation(root23[:, h], size23[:, h], ACT.Abs_reciprocal_sqrt, bias=ones[:])
-            nc.scalar.activation(recip[:, h, 2:4, :], root23[:, h], ACT.Square)
-
-        def numerator(t):
-            nc.vector.scalar_tensor_tensor(num[:, t, :], dual_sb[:, t, :], gn_sb[:, t : t + 1], diff[t][:], ALU.mult, ALU.add)
+        def numerators(c0, w, tag):
+            num = keep.tile([P, PACK, w], F32, name="num", tag=tag, align_bytes=64)
+            for t in range(PACK):
+                nc.vector.scalar_tensor_tensor(num[:, t, :], dual_sb[:, t, c0 : c0 + w], gn_sb[:, t : t + 1], diff[t][:, c0 : c0 + w], ALU.mult, ALU.add)
+            for c in range(c0 // CHUNK, (c0 + w) // CHUNK):
+                nums[c] = num[:, :, c * CHUNK - c0 : (c + 1) * CHUNK - c0]
 
         def quotient(c):
             c0, w = c * CHUNK, CHUNK
-            zb[c] = keep.tile([P, w, PACK], BF16, name="zb%d" % c, align_bytes=64)
+            zb[c] = keep.tile([P, w, PACK], BF16, name="zb%d" % c, tag="zb%d" % c, align_bytes=64)
             nc.vector.tensor_tensor(
                 zb[c][:].rearrange("p (c i) t -> p c t i", i=2),
-                num[:, :, c0 : c0 + w].rearrange("p t (c i) -> p c t i", i=2),
+                nums[c].rearrange("p t (c i) -> p c t i", i=2),
                 recip[:, c0 // HALF, :, c0 % HALF : c0 % HALF + w].rearrange("p t (c i) -> p c t i", i=2),
                 ALU.mult,
             )
@@ -225,28 +212,28 @@ def tile_picked_tvdual_none_p_kernel(tc, x_words, x_scales, w1, dual, gn, w2, of
 
         difference(0, 0, HALF)
         difference(0, HALF, HALF)
-        reciprocal(0, 0, S)
+        inverse(0, (0, 0), (0, 1))
         duplicate(1)
         duplicate(2)
         difference(1, 0, S)
-        reciprocal(1, 0, S)
+        inverse(1, (1, 0), (1, 1))
         duplicate(3)
         difference(2, 0, S)
-        absolute23(2, 0)
-        absolute23(2, 1)
         difference(3, 0, S)
-        absolute23(3, 0)
-        inverse23(0)
-        absolute23(3, 1)
-        inverse23(1)
+        inverse(0, (2, 0), (3, 0))
+        inverse(1, (2, 1), (3, 1))
         cast_w2_scalar()
-        for t in range(PACK):
-            numerator(t)
+        numerators(0, HALF, "num")
         cast_w2_vector()
         quotient(0)
         quantise_w2()
-        for c in range(last + 1):
-            if c < last:
-                quotient(c + 1)
-            quantise(c)
-            product(c)
+        quotient(1)
+        quantise(0)
+        product(0)
+        for c in range(2, last + 1):
+            numerators(c * CHUNK, CHUNK, "zb%d" % (c - 2))
+            quantise(c - 1)
+            product(c - 1)
+            quotient(c)
+        quantise(last)
+        product(last)

@@ -20,7 +20,6 @@ PACK = 4
 HALF = S // 2
 MH = P // 2
 CHUNK = 128
-W2_ON_VECTOR = 148
 
 
 def tile_picked_tvdual_none_p_kernel(tc, x_words, x_scales, w1, dual, gn, w2, offs, nb, out):
@@ -77,13 +76,12 @@ def tile_picked_tvdual_none_p_kernel(tc, x_words, x_scales, w1, dual, gn, w2, of
         gs = keep.tile([P, PACK], F32, name="gs")
         ginv = keep.tile([P, PACK], F32, name="ginv")
         nc.gpsimd.tensor_scalar(gq[:], gn_sb[:], 0.25, None, ALU.mult)
+        ngq = keep.tile([P, PACK], F32, name="ngq")
+        nc.gpsimd.tensor_scalar(ngq[:], gn_sb[:], -0.25, None, ALU.mult)
         nc.gpsimd.tensor_scalar(gz[:], gn_sb[:], 0.0, None, ALU.is_equal)
         nc.gpsimd.tensor_tensor(gs[:], gz[:], gn_sb[:], ALU.add)
 
-        own = [keep.tile([P, S], F32, name="own%d" % t) for t in range(PACK)]
-        win = [keep.tile([P, S if t == 0 else 2 * S], F32, name="win%d" % t) for t in range(PACK)]
-        for t in range(1, PACK):
-            nc.vector.memset(win[t][:, S:], 0.0)
+        win = [keep.tile([P, S], F32, name="win%d" % t) for t in range(PACK)]
         for t in range(PACK):
             quantise_w1(t, 0)
         nc.vector.reciprocal(ginv[:], gs[:])
@@ -116,38 +114,42 @@ def tile_picked_tvdual_none_p_kernel(tc, x_words, x_scales, w1, dual, gn, w2, of
         y01 = first_product(0, HALF, HALF, 1)
         ys = [first_product(t, 0, S, t + 1) for t in range(1, PACK)]
         out_vector(win[0], 0, 0, HALF, y00)
-        out_vector(own[0], 0, 0, HALF, y00)
         out_scalar(win[0], 0, HALF, HALF, y01)
-        out_scalar(own[0], 0, HALF, HALF, y01)
         for t in range(1, PACK):
             out_scalar(win[t], t, 0, S, ys[t - 1])
+        y_half = {(0, 0): y00[:], (0, 1): y01[:]}
+        for t in range(1, PACK):
+            for h in range(2):
+                y_half[t, h] = ys[t - 1][:, h * HALF : (h + 1) * HALF]
 
         w2_bf = keep.tile([P, N, PACK], BF16, name="w2_bf", align_bytes=64)
         w2_codes = keep.tile([P, N], U32, name="w2_codes", align_bytes=64)
         w2_scales = keep.tile([P, N], U8, name="w2_scales", align_bytes=64)
-        dst2 = w2_bf[:].rearrange("p (c i) j -> p c j i", i=2)
-        src2 = w2_raw[:].rearrange("p j (c i) -> p c j i", i=2)
 
-        def cast_w2_scalar():
-            nc.scalar.copy(dst2[:, W2_ON_VECTOR:], src2[:, W2_ON_VECTOR:])
-
-        def cast_w2_vector():
-            nc.vector.tensor_copy(dst2[:, :W2_ON_VECTOR], src2[:, :W2_ON_VECTOR])
+        def cast_w2():
+            nc.gpsimd.tensor_scalar(w2_bf[:], w2_raw[:].rearrange("p j c -> p c j"), 1.0, 0.0, ALU.mult, ALU.add)
 
         def quantise_w2():
             nc.vector.quantize_mx(out=w2_codes[:].bitcast(FP8X4), scales=w2_scales[:], in_=w2_bf[:].rearrange("p c j -> p (c j)"))
 
         diff = [keep.tile([P, S], F32, name="diff%d" % t) for t in range(PACK)]
         recip = keep.tile([P, 2, PACK, HALF], F32, name="recip")
-        nums = {}
+        fetched = {(t, h): keep.tile([P, HALF], F32, name="fetched%d%d" % (t, h)) for t in range(PACK) for h in range(2)}
+        gained = [keep.tile([P, S], F32, name="gained%d" % t) for t in range(2)]
+        num = keep.tile([P, 2, PACK, HALF], F32, name="num")
         zb, zc, zs = {}, {}, {}
 
-        def duplicate(t, c0=0, w=S):
-            nc.vector.tensor_copy(own[t][:, c0 : c0 + w], win[t][:, c0 : c0 + w])
+        def fetch(t, h):
+            nc.vector.tensor_copy(fetched[t, h][:], win[t][:].indirect(nb_sb[:, h * HALF // 16 : (h + 1) * HALF // 16]))
 
-        def difference(t, c0, w):
-            cols = slice(c0, c0 + w)
-            nc.vector.tensor_tensor(diff[t][:, cols], win[t][:].indirect(nb_sb[:, c0 // 16 : (c0 + w) // 16]), own[t][:, cols], ALU.subtract)
+        def difference(t, h):
+            nc.vector.scalar_tensor_tensor(diff[t][:, h * HALF : (h + 1) * HALF], y_half[t, h], ngq[:, t : t + 1], fetched[t, h][:], ALU.mult, ALU.add)
+
+        def differences(*pieces):
+            for t, h in pieces:
+                fetch(t, h)
+            for t, h in pieces:
+                difference(t, h)
 
         def inverse(turn, *pieces):
             sizes = [keep.tile([P, HALF], F32, name="size", tag="work%d%d" % (i, turn)) for i in range(2)]
@@ -159,20 +161,21 @@ def tile_picked_tvdual_none_p_kernel(tc, x_words, x_scales, w1, dual, gn, w2, of
             for i, (t, h) in enumerate(pieces):
                 nc.scalar.activation(recip[:, h, t, :], roots[i][:], ACT.Square)
 
-        def numerators(c0, w, tag):
-            num = keep.tile([P, PACK, w], F32, name="num", tag=tag, align_bytes=64)
-            for t in range(PACK):
-                nc.vector.scalar_tensor_tensor(num[:, t, :], dual_sb[:, t, c0 : c0 + w], gn_sb[:, t : t + 1], diff[t][:, c0 : c0 + w], ALU.mult, ALU.add)
-            for c in range(c0 // CHUNK, (c0 + w) // CHUNK):
-                nums[c] = num[:, :, c * CHUNK - c0 : (c + 1) * CHUNK - c0]
+        def numerator_gpsimd(t):
+            nc.gpsimd.tensor_scalar(gained[t][:], dual_sb[:, t, :], gn_sb[:, t : t + 1], 0.0, ALU.mult, ALU.add)
+            nc.gpsimd.tensor_tensor(num[:, :, t, :], gained[t][:].rearrange("p (h c) -> p h c", h=2), diff[t][:].rearrange("p (h c) -> p h c", h=2), ALU.add)
+
+        def numerator_vector(t, h):
+            cols = slice(h * HALF, (h + 1) * HALF)
+            nc.vector.scalar_tensor_tensor(num[:, h, t, :], dual_sb[:, t, cols], gn_sb[:, t : t + 1], diff[t][:, cols], ALU.mult, ALU.add)
 
         def quotient(c):
-            c0, w = c * CHUNK, CHUNK
-            zb[c] = keep.tile([P, w, PACK], BF16, name="zb%d" % c, tag="zb%d" % c, align_bytes=64)
+            h, cols = c * CHUNK // HALF, slice(c * CHUNK % HALF, c * CHUNK % HALF + CHUNK)
+            zb[c] = keep.tile([P, CHUNK, PACK], BF16, name="zb%d" % c, tag="zb%d" % c, align_bytes=64)
             nc.vector.tensor_tensor(
                 zb[c][:].rearrange("p (c i) t -> p c t i", i=2),
-                nums[c].rearrange("p t (c i) -> p c t i", i=2),
-                recip[:, c0 // HALF, :, c0 % HALF : c0 % HALF + w].rearrange("p t (c i) -> p c t i", i=2),
+                num[:, h, :, cols].rearrange("p t (c i) -> p c t i", i=2),
+                recip[:, h, :, cols].rearrange("p t (c i) -> p c t i", i=2),
                 ALU.mult,
             )
 
@@ -210,30 +213,31 @@ def tile_picked_tvdual_none_p_kernel(tc, x_words, x_scales, w1, dual, gn, w2, of
             if c < last:
                 nc.sync.dma_start(out[:, c0 : c0 + w].rearrange("(mt p) n -> p mt n", p=P), res[:])
 
-        difference(0, 0, HALF)
-        difference(0, HALF, HALF)
+        cast_w2()
+        differences((0, 0), (0, 1))
         inverse(0, (0, 0), (0, 1))
-        duplicate(1)
-        duplicate(2)
-        difference(1, 0, S)
+        differences((1, 0), (1, 1))
         inverse(1, (1, 0), (1, 1))
-        duplicate(3)
-        difference(2, 0, S)
-        difference(3, 0, S)
+        numerator_gpsimd(0)
+        numerator_gpsimd(1)
+        differences((2, 0), (3, 0))
         inverse(0, (2, 0), (3, 0))
+        differences((2, 1), (3, 1))
         inverse(1, (2, 1), (3, 1))
-        cast_w2_scalar()
-        numerators(0, HALF, "num")
-        cast_w2_vector()
-        quotient(0)
+        numerator_vector(2, 0)
+        numerator_vector(3, 0)
         quantise_w2()
+        quotient(0)
+        numerator_vector(2, 1)
         quotient(1)
         quantise(0)
         product(0)
-        for c in range(2, last + 1):
-            numerators(c * CHUNK, CHUNK, "zb%d" % (c - 2))
-            quantise(c - 1)
-            product(c - 1)
-            quotient(c)
-        quantise(last)
-        product(last)
+        numerator_vector(3, 1)
+        quantise(1)
+        product(1)
+        quotient(2)
+        quotient(3)
+        quantise(2)
+        product(2)
+        quantise(3)
+        product(3)

@@ -123,58 +123,75 @@ def tile_picked_tvdual_none_p_kernel(tc, x_words, x_scales, w1, dual, gn, w2, of
                 y_half[t, h] = ys[t - 1][:, h * HALF : (h + 1) * HALF]
 
         w2_bf = keep.tile([P, N, PACK], BF16, name="w2_bf", align_bytes=64)
-        w2_codes = keep.tile([P, N], U32, name="w2_codes", align_bytes=64)
+        last_root = keep.tile([P, HALF], F32, name="last_root", tag="w2_codes", align_bytes=64)
         w2_scales = keep.tile([P, N], U8, name="w2_scales", align_bytes=64)
 
         def cast_w2():
             nc.gpsimd.tensor_scalar(w2_bf[:], w2_raw[:].rearrange("p j c -> p c j"), 1.0, 0.0, ALU.mult, ALU.add)
 
-        def quantise_w2():
+        def quantise_w2(w2_codes):
             nc.vector.quantize_mx(out=w2_codes[:].bitcast(FP8X4), scales=w2_scales[:], in_=w2_bf[:].rearrange("p c j -> p (c j)"))
 
         diff = [keep.tile([P, S], F32, name="diff%d" % t) for t in range(PACK)]
         recip = keep.tile([P, 2, PACK, HALF], F32, name="recip")
-        fetched = {(t, h): keep.tile([P, HALF], F32, name="fetched%d%d" % (t, h)) for t in range(PACK) for h in range(2)}
+        fetched = {}
         gained = [keep.tile([P, S], F32, name="gained%d" % t) for t in range(2)]
-        num = keep.tile([P, 2, PACK, HALF], F32, name="num")
+        num_row = keep.tile([P, PACK * S], F32, name="num_row", align_bytes=64)
+        num = num_row[:].rearrange("p (c t n) -> p c t n", t=PACK, n=CHUNK)
         zb, zc, zs = {}, {}, {}
 
-        def fetch(t, h):
+        def fetch(i, t, h):
+            fetched[t, h] = keep.tile([P, HALF], F32, name="fetched", tag="fetched%d" % i)
             nc.vector.tensor_copy(fetched[t, h][:], win[t][:].indirect(nb_sb[:, h * HALF // 16 : (h + 1) * HALF // 16]))
 
         def difference(t, h):
             nc.vector.scalar_tensor_tensor(diff[t][:, h * HALF : (h + 1) * HALF], y_half[t, h], ngq[:, t : t + 1], fetched[t, h][:], ALU.mult, ALU.add)
 
         def differences(*pieces):
-            for t, h in pieces:
-                fetch(t, h)
+            for i, (t, h) in enumerate(pieces):
+                fetch(i, t, h)
             for t, h in pieces:
                 difference(t, h)
 
-        def inverse(turn, *pieces):
-            sizes = [keep.tile([P, HALF], F32, name="size", tag="work%d%d" % (i, turn)) for i in range(2)]
-            roots = [keep.tile([P, HALF], F32, name="root", tag="work%d%d" % (i, 1 - turn)) for i in range(2)]
-            for i, (t, h) in enumerate(pieces):
-                nc.scalar.activation(sizes[i][:], diff[t][:, h * HALF : (h + 1) * HALF], ACT.Abs, scale=ginv[:, t : t + 1])
-            for i in range(2):
-                nc.scalar.activation(roots[i][:], sizes[i][:], ACT.Abs_reciprocal_sqrt, bias=ones[:])
-            for i, (t, h) in enumerate(pieces):
-                nc.scalar.activation(recip[:, h, t, :], roots[i][:], ACT.Square)
+        work = keep.tile([P, 5 * HALF], F32, name="work")
+
+        def span(first):
+            return work[:, first : first + HALF]
+
+        def inverse(pieces, sizes, roots):
+            for (t, h), size in zip(pieces, sizes):
+                nc.scalar.activation(size, diff[t][:, h * HALF : (h + 1) * HALF], ACT.Abs, scale=ginv[:, t : t + 1])
+            for size, root in zip(sizes, roots):
+                nc.scalar.activation(root, size, ACT.Abs_reciprocal_sqrt, bias=ones[:])
+            for (t, h), root in zip(pieces, roots):
+                nc.scalar.activation(recip[:, h, t, :], root, ACT.Square)
 
         def numerator_gpsimd(t):
             nc.gpsimd.tensor_scalar(gained[t][:], dual_sb[:, t, :], gn_sb[:, t : t + 1], 0.0, ALU.mult, ALU.add)
-            nc.gpsimd.tensor_tensor(num[:, :, t, :], gained[t][:].rearrange("p (h c) -> p h c", h=2), diff[t][:].rearrange("p (h c) -> p h c", h=2), ALU.add)
+            nc.gpsimd.tensor_tensor(num[:, :, t, :], gained[t][:].rearrange("p (c n) -> p c n", n=CHUNK), diff[t][:].rearrange("p (c n) -> p c n", n=CHUNK), ALU.add)
 
-        def numerator_vector(t, h):
-            cols = slice(h * HALF, (h + 1) * HALF)
-            nc.vector.scalar_tensor_tensor(num[:, h, t, :], dual_sb[:, t, cols], gn_sb[:, t : t + 1], diff[t][:, cols], ALU.mult, ALU.add)
+        def numerators_vector(c0, n):
+            cols = slice(c0 * CHUNK, (c0 + n) * CHUNK)
+            for t in range(2, PACK):
+                nc.vector.scalar_tensor_tensor(
+                    num[:, c0 : c0 + n, t, :],
+                    dual_sb[:, t, cols].rearrange("p (c n) -> p c n", n=CHUNK),
+                    gn_sb[:, t : t + 1],
+                    diff[t][:, cols].rearrange("p (c n) -> p c n", n=CHUNK),
+                    ALU.mult,
+                    ALU.add,
+                )
 
         def quotient(c):
             h, cols = c * CHUNK // HALF, slice(c * CHUNK % HALF, c * CHUNK % HALF + CHUNK)
-            zb[c] = keep.tile([P, CHUNK, PACK], BF16, name="zb%d" % c, tag="zb%d" % c, align_bytes=64)
+            if c < 2:
+                first = ((c + 2) * PACK + 2) * CHUNK
+                zb[c] = num_row[:, first : first + 2 * CHUNK].bitcast(BF16)
+            else:
+                zb[c] = keep.tile([P, CHUNK * PACK], BF16, name="zb%d" % c, align_bytes=64)[:]
             nc.vector.tensor_tensor(
-                zb[c][:].rearrange("p (c i) t -> p c t i", i=2),
-                num[:, h, :, cols].rearrange("p t (c i) -> p c t i", i=2),
+                zb[c].rearrange("p (c i t) -> p c t i", i=2, t=PACK),
+                num[:, c].rearrange("p t (c i) -> p c t i", i=2),
                 recip[:, h, :, cols].rearrange("p t (c i) -> p c t i", i=2),
                 ALU.mult,
             )
@@ -182,7 +199,7 @@ def tile_picked_tvdual_none_p_kernel(tc, x_words, x_scales, w1, dual, gn, w2, of
         def quantise(c):
             zc[c] = keep.tile([P, CHUNK], U32, name="zc%d" % c, align_bytes=64)
             zs[c] = keep.tile([P, CHUNK], U8, name="zs%d" % c, align_bytes=64)
-            nc.vector.quantize_mx(out=zc[c][:].bitcast(FP8X4), scales=zs[c][:], in_=zb[c][:].rearrange("p c t -> p (c t)"))
+            nc.vector.quantize_mx(out=zc[c][:].bitcast(FP8X4), scales=zs[c][:], in_=zb[c])
 
         last = S // CHUNK - 1
 
@@ -215,29 +232,26 @@ def tile_picked_tvdual_none_p_kernel(tc, x_words, x_scales, w1, dual, gn, w2, of
 
         cast_w2()
         differences((0, 0), (0, 1))
-        inverse(0, (0, 0), (0, 1))
+        inverse([(0, 0), (0, 1)], [span(0), span(HALF)], [span(2 * HALF), span(3 * HALF)])
         differences((1, 0), (1, 1))
-        inverse(1, (1, 0), (1, 1))
+        inverse([(1, 0), (1, 1)], [span(2 * HALF), span(3 * HALF)], [span(0), span(HALF)])
         numerator_gpsimd(0)
         numerator_gpsimd(1)
         differences((2, 0), (3, 0))
-        inverse(0, (2, 0), (3, 0))
+        inverse([(2, 0), (3, 0)], [span(0), span(HALF)], [span(2 * HALF), last_root[:]])
         differences((2, 1), (3, 1))
-        inverse(1, (2, 1), (3, 1))
-        numerator_vector(2, 0)
-        numerator_vector(3, 0)
-        quantise_w2()
+        inverse([(2, 1), (3, 1)], [span(3 * HALF // 2), span(5 * HALF // 2)], [span(0), span(4 * HALF)])
+        numerators_vector(0, 2)
         quotient(0)
-        numerator_vector(2, 1)
-        quotient(1)
+        w2_codes = keep.tile([P, N], U32, name="w2_codes", tag="w2_codes", align_bytes=64)
+        quantise_w2(w2_codes)
         quantise(0)
         product(0)
-        numerator_vector(3, 1)
-        quantise(1)
-        product(1)
-        quotient(2)
-        quotient(3)
-        quantise(2)
-        product(2)
-        quantise(3)
-        product(3)
+        for c in range(1, last):
+            quotient(c)
+            numerators_vector(c + 1, 1)
+            quantise(c)
+            product(c)
+        quotient(last)
+        quantise(last)
+        product(last)

@@ -135,7 +135,7 @@ def tile_picked_tvdual_none_p_kernel(tc, x_words, x_scales, w1, dual, gn, w2, of
         diff = [keep.tile([P, S], F32, name="diff%d" % t) for t in range(PACK)]
         recip = keep.tile([P, 2, PACK, HALF], F32, name="recip")
         fetched = {}
-        gained = [keep.tile([P, S], F32, name="gained%d" % t) for t in range(2)]
+        gained = [keep.tile([P, S], F32, name="gained%d" % t) for t in range(3)]
         num_row = keep.tile([P, PACK * S], F32, name="num_row", align_bytes=64)
         num = num_row[:].rearrange("p (c t n) -> p c t n", t=PACK, n=CHUNK)
         zb, zc, zs = {}, {}, {}
@@ -166,13 +166,13 @@ def tile_picked_tvdual_none_p_kernel(tc, x_words, x_scales, w1, dual, gn, w2, of
             for (t, h), root in zip(pieces, roots):
                 nc.scalar.activation(recip[:, h, t, :], root, ACT.Square)
 
-        def numerator_gpsimd(t):
-            nc.gpsimd.tensor_scalar(gained[t][:], dual_sb[:, t, :], gn_sb[:, t : t + 1], 0.0, ALU.mult, ALU.add)
-            nc.gpsimd.tensor_tensor(num[:, :, t, :], gained[t][:].rearrange("p (c n) -> p c n", n=CHUNK), diff[t][:].rearrange("p (c n) -> p c n", n=CHUNK), ALU.add)
+        def numerator_gpsimd(t, w):
+            nc.gpsimd.tensor_scalar(gained[t][:, :w], dual_sb[:, t, :w], gn_sb[:, t : t + 1], 0.0, ALU.mult, ALU.add)
+            nc.gpsimd.tensor_tensor(num[:, : w // CHUNK, t, :], gained[t][:, :w].rearrange("p (c n) -> p c n", n=CHUNK), diff[t][:, :w].rearrange("p (c n) -> p c n", n=CHUNK), ALU.add)
 
-        def numerators_vector(c0, n):
+        def numerators_vector(c0, n, t0=2):
             cols = slice(c0 * CHUNK, (c0 + n) * CHUNK)
-            for t in range(2, PACK):
+            for t in range(t0, PACK):
                 nc.vector.scalar_tensor_tensor(
                     num[:, c0 : c0 + n, t, :],
                     dual_sb[:, t, cols].rearrange("p (c n) -> p c n", n=CHUNK),
@@ -235,13 +235,14 @@ def tile_picked_tvdual_none_p_kernel(tc, x_words, x_scales, w1, dual, gn, w2, of
         inverse([(0, 0), (0, 1)], [span(0), span(HALF)], [span(2 * HALF), span(3 * HALF)])
         differences((1, 0), (1, 1))
         inverse([(1, 0), (1, 1)], [span(2 * HALF), span(3 * HALF)], [span(0), span(HALF)])
-        numerator_gpsimd(0)
-        numerator_gpsimd(1)
+        numerator_gpsimd(0, S)
+        numerator_gpsimd(1, S)
         differences((2, 0), (3, 0))
         inverse([(2, 0), (3, 0)], [span(0), span(HALF)], [span(2 * HALF), last_root[:]])
         differences((2, 1), (3, 1))
         inverse([(2, 1), (3, 1)], [span(3 * HALF // 2), span(5 * HALF // 2)], [span(0), span(4 * HALF)])
-        numerators_vector(0, 2)
+        numerator_gpsimd(2, HALF)
+        numerators_vector(0, 2, 3)
         quotient(0)
         w2_codes = keep.tile([P, N], U32, name="w2_codes", tag="w2_codes", align_bytes=64)
         quantise_w2(w2_codes)

@@ -20,6 +20,7 @@ PACK = 4
 HALF = S // 2
 MH = P // 2
 CHUNK = 128
+W2_ON_SCALAR = 64
 
 
 def tile_picked_tvdual_none_p_kernel(tc, x_words, x_scales, w1, dual, gn, w2, offs, nb, out):
@@ -58,8 +59,8 @@ def tile_picked_tvdual_none_p_kernel(tc, x_words, x_scales, w1, dual, gn, w2, of
         w1_bf = [[keep.tile([P, 2, MH, PACK], BF16, name="w1_bf%d%d" % (u, g), align_bytes=64) for g in range(2)] for u in range(2)]
         w1_codes = [keep.tile([P, P], U32, name="w1_codes%d" % t, align_bytes=64) for t in range(PACK)]
         w1_scales = [keep.tile([P, P], U8, name="w1_scales%d" % t, align_bytes=64) for t in range(PACK)]
-        src = [w1_raw[u][:].rearrange("p j (m t) -> p m t j", t=PACK) for u in range(2)]
-        dst = [[w1_bf[u][g][:].rearrange("p t m j -> p m t j") for g in range(2)] for u in range(2)]
+        src = [w1_raw[u][:].rearrange("p j (m t) -> p m j t", t=PACK) for u in range(2)]
+        dst = [[w1_bf[u][g][:].rearrange("p t m j -> p m j t") for g in range(2)] for u in range(2)]
 
         def quantise_w1(t, u):
             cols = slice(u * MH, (u + 1) * MH)
@@ -69,7 +70,7 @@ def tile_picked_tvdual_none_p_kernel(tc, x_words, x_scales, w1, dual, gn, w2, of
         x_codes = keep.tile([P, S], U32, name="x_codes", align_bytes=64)
         nc.vector.tensor_copy(x_bytes[:], bytes_win[:].indirect(offs_sb[:]))
         for g in range(2):
-            nc.scalar.copy(dst[0][g], src[0][:, :, 2 * g : 2 * g + 2])
+            nc.scalar.copy(dst[0][g], src[0][:, :, :, 2 * g : 2 * g + 2])
 
         gq = keep.tile([P, PACK], F32, name="gq")
         gz = keep.tile([P, PACK], F32, name="gz")
@@ -86,8 +87,8 @@ def tile_picked_tvdual_none_p_kernel(tc, x_words, x_scales, w1, dual, gn, w2, of
             quantise_w1(t, 0)
         nc.vector.reciprocal(ginv[:], gs[:])
         nc.vector.tensor_copy(x_codes[:], words[:].bitcast(U32).indirect(offs_sb[:]))
-        nc.vector.tensor_copy(dst[1][0], src[1][:, :, 0:2])
-        nc.scalar.copy(dst[1][1], src[1][:, :, 2:4])
+        nc.vector.tensor_copy(dst[1][0], src[1][:, :, :, 0:2])
+        nc.scalar.copy(dst[1][1], src[1][:, :, :, 2:4])
         for t in range(PACK):
             quantise_w1(t, 1)
 
@@ -115,19 +116,23 @@ def tile_picked_tvdual_none_p_kernel(tc, x_words, x_scales, w1, dual, gn, w2, of
         ys = [first_product(t, 0, S, t + 1) for t in range(1, PACK)]
         out_vector(win[0], 0, 0, HALF, y00)
         out_scalar(win[0], 0, HALF, HALF, y01)
+        w2_bf = keep.tile([P, N, PACK], BF16, name="w2_bf", align_bytes=64)
         for t in range(1, PACK):
             out_scalar(win[t], t, 0, S, ys[t - 1])
+        nc.scalar.copy(
+            w2_bf[:, :W2_ON_SCALAR, :].rearrange("p (c i) j -> p c j i", i=2),
+            w2_raw[:, :, :W2_ON_SCALAR].rearrange("p j (c i) -> p c j i", i=2),
+        )
         y_half = {(0, 0): y00[:], (0, 1): y01[:]}
         for t in range(1, PACK):
             for h in range(2):
                 y_half[t, h] = ys[t - 1][:, h * HALF : (h + 1) * HALF]
 
-        w2_bf = keep.tile([P, N, PACK], BF16, name="w2_bf", align_bytes=64)
         last_root = keep.tile([P, HALF], F32, name="last_root", tag="w2_codes", align_bytes=64)
         w2_scales = keep.tile([P, N], U8, name="w2_scales", align_bytes=64)
 
         def cast_w2():
-            nc.gpsimd.tensor_scalar(w2_bf[:], w2_raw[:].rearrange("p j c -> p c j"), 1.0, 0.0, ALU.mult, ALU.add)
+            nc.gpsimd.tensor_scalar(w2_bf[:, W2_ON_SCALAR:, :], w2_raw[:, :, W2_ON_SCALAR:].rearrange("p j c -> p c j"), 1.0, 0.0, ALU.mult, ALU.add)
 
         def quantise_w2(w2_codes):
             nc.vector.quantize_mx(out=w2_codes[:].bitcast(FP8X4), scales=w2_scales[:], in_=w2_bf[:].rearrange("p c j -> p (c j)"))

@@ -20,6 +20,7 @@ PACK = 4
 HALF = S // 2
 MH = P // 2
 CHUNK = 128
+W1_ON_SCALAR = 20
 W2_ON_SCALAR = 64
 
 
@@ -56,7 +57,7 @@ def tile_picked_tvdual_none_p_kernel(tc, x_words, x_scales, w1, dual, gn, w2, of
         nc.sync.dma_start(dual_sb[:], dual.rearrange("(p t) n -> p t n", t=PACK))
         nc.scalar.activation(warm[:], ones[:], ACT.Abs_reciprocal_sqrt, bias=ones[:])
 
-        w1_bf = [[keep.tile([P, 2, MH, PACK], BF16, name="w1_bf%d%d" % (u, g), align_bytes=64) for g in range(2)] for u in range(2)]
+        w1_bf = [[keep.tile([P, 2, MH, PACK], BF16, name="w1_bf%d%d" % (u, g), tag="rounded%d%d" % (u, g), align_bytes=64) for g in range(2)] for u in range(2)]
         w1_codes = [keep.tile([P, P], U32, name="w1_codes%d" % t, align_bytes=64) for t in range(PACK)]
         w1_scales = [keep.tile([P, P], U8, name="w1_scales%d" % t, align_bytes=64) for t in range(PACK)]
         src = [w1_raw[u][:].rearrange("p j (m t) -> p m j t", t=PACK) for u in range(2)]
@@ -75,7 +76,6 @@ def tile_picked_tvdual_none_p_kernel(tc, x_words, x_scales, w1, dual, gn, w2, of
         gq = keep.tile([P, PACK], F32, name="gq")
         gz = keep.tile([P, PACK], F32, name="gz")
         gs = keep.tile([P, PACK], F32, name="gs")
-        ginv = keep.tile([P, PACK], F32, name="ginv")
         nc.gpsimd.tensor_scalar(gq[:], gn_sb[:], 0.25, None, ALU.mult)
         ngq = keep.tile([P, PACK], F32, name="ngq")
         nc.gpsimd.tensor_scalar(ngq[:], gn_sb[:], -0.25, None, ALU.mult)
@@ -85,12 +85,14 @@ def tile_picked_tvdual_none_p_kernel(tc, x_words, x_scales, w1, dual, gn, w2, of
         win = [keep.tile([P, S], F32, name="win%d" % t) for t in range(PACK)]
         for t in range(PACK):
             quantise_w1(t, 0)
-        nc.vector.reciprocal(ginv[:], gs[:])
         nc.vector.tensor_copy(x_codes[:], words[:].bitcast(U32).indirect(offs_sb[:]))
-        nc.vector.tensor_copy(dst[1][0], src[1][:, :, :, 0:2])
+        nc.scalar.copy(dst[1][0][:, :W1_ON_SCALAR], src[1][:, :W1_ON_SCALAR, :, 0:2])
+        nc.vector.tensor_copy(dst[1][0][:, W1_ON_SCALAR:], src[1][:, W1_ON_SCALAR:, :, 0:2])
         nc.scalar.copy(dst[1][1], src[1][:, :, :, 2:4])
         for t in range(PACK):
             quantise_w1(t, 1)
+        ginv = keep.tile([P, PACK], F32, name="ginv", tag="rounded11", align_bytes=64)
+        nc.vector.reciprocal(ginv[:], gs[:])
 
         def first_product(t, c0, w, bank):
             y = psum.tile([P, w], F32, name="y", tag="bank%d" % bank)
@@ -152,9 +154,9 @@ def tile_picked_tvdual_none_p_kernel(tc, x_words, x_scales, w1, dual, gn, w2, of
         def difference(t, h):
             nc.vector.scalar_tensor_tensor(diff[t][:, h * HALF : (h + 1) * HALF], y_half[t, h], ngq[:, t : t + 1], fetched[t, h][:], ALU.mult, ALU.add)
 
-        def differences(*pieces):
+        def differences(slot, *pieces):
             for i, (t, h) in enumerate(pieces):
-                fetch(i, t, h)
+                fetch(slot + i, t, h)
             for t, h in pieces:
                 difference(t, h)
 
@@ -187,67 +189,78 @@ def tile_picked_tvdual_none_p_kernel(tc, x_words, x_scales, w1, dual, gn, w2, of
                     ALU.add,
                 )
 
-        def quotient(c):
-            h, cols = c * CHUNK // HALF, slice(c * CHUNK % HALF, c * CHUNK % HALF + CHUNK)
+        last = S // CHUNK - 1
+
+        def rounded_tile(c):
             if c < 2:
                 first = ((c + 2) * PACK + 2) * CHUNK
                 zb[c] = num_row[:, first : first + 2 * CHUNK].bitcast(BF16)
             else:
                 zb[c] = keep.tile([P, CHUNK * PACK], BF16, name="zb%d" % c, align_bytes=64)[:]
+            zc[c] = keep.tile([P, CHUNK], U32, name="zc%d" % c, align_bytes=64)
+            zs[c] = keep.tile([P, CHUNK], U8, name="zs%d" % c, align_bytes=64)
+
+        def quotient(c, lo=0, hi=CHUNK):
+            h, r0 = c * CHUNK // HALF, c * CHUNK % HALF
             nc.vector.tensor_tensor(
-                zb[c].rearrange("p (c i t) -> p c t i", i=2, t=PACK),
-                num[:, c].rearrange("p t (c i) -> p c t i", i=2),
-                recip[:, h, :, cols].rearrange("p t (c i) -> p c t i", i=2),
+                zb[c][:, lo * PACK : hi * PACK].rearrange("p (c i t) -> p c t i", i=2, t=PACK),
+                num[:, c, :, lo:hi].rearrange("p t (c i) -> p c t i", i=2),
+                recip[:, h, :, r0 + lo : r0 + hi].rearrange("p t (c i) -> p c t i", i=2),
                 ALU.mult,
             )
 
-        def quantise(c):
-            zc[c] = keep.tile([P, CHUNK], U32, name="zc%d" % c, align_bytes=64)
-            zs[c] = keep.tile([P, CHUNK], U8, name="zs%d" % c, align_bytes=64)
-            nc.vector.quantize_mx(out=zc[c][:].bitcast(FP8X4), scales=zs[c][:], in_=zb[c])
+        def quantise(c, lo=0, hi=CHUNK):
+            nc.vector.quantize_mx(out=zc[c][:, lo:hi].bitcast(FP8X4), scales=zs[c][:, lo:hi], in_=zb[c][:, lo * PACK : hi * PACK])
 
-        last = S // CHUNK - 1
+        def second_product(c, mt, acc):
+            nc.tensor.matmul_mx(
+                out=acc,
+                lhsT=w2_codes[:, mt * P : (mt + 1) * P].bitcast(FP8X4),
+                lhsT_scale=w2_scales[:, mt * P : (mt + 1) * P],
+                rhs=zc[c][:].bitcast(FP8X4),
+                rhs_scale=zs[c][:],
+                start=True,
+                stop=True,
+            )
+
+        def out_rows(mt0, n, c):
+            return out[mt0 * P : (mt0 + n) * P, c * CHUNK : (c + 1) * CHUNK].rearrange("(mt p) n -> p mt n", p=P)
 
         def product(c):
-            c0, w = c * CHUNK, CHUNK
-            res = keep.tile([P, PACK, w], F32, name="res%d" % c)
-            per = 1 if c == last else 2
-            for u in range(PACK // per):
-                bank = (2 * c + u + 5) % 8
-                acc = psum.tile([P, per, w], F32, name="acc", tag="bank%d" % bank)
-                for v in range(per):
-                    mt = per * u + v
-                    nc.tensor.matmul_mx(
-                        out=acc[:, v, :],
-                        lhsT=w2_codes[:, mt * P : (mt + 1) * P].bitcast(FP8X4),
-                        lhsT_scale=w2_scales[:, mt * P : (mt + 1) * P],
-                        rhs=zc[c][:].bitcast(FP8X4),
-                        rhs_scale=zs[c][:],
-                        start=True,
-                        stop=True,
-                    )
-                rows = slice(per * u, per * (u + 1))
-                if c == last and u % 2 == 1:
-                    nc.vector.tensor_copy(res[:, rows, :], acc[:])
-                    nc.sync.dma_start(out[(u - 1) * P : (u + 1) * P, c0 : c0 + w].rearrange("(mt p) n -> p mt n", p=P), res[:, u - 1 : u + 1, :])
+            res = keep.tile([P, PACK, CHUNK], F32, name="res%d" % c)
+            for u in range(2):
+                acc = psum.tile([P, 2, CHUNK], F32, name="acc", tag="bank%d" % ((2 * c + u + 5) % 8))
+                for v in range(2):
+                    second_product(c, 2 * u + v, acc[:, v, :])
+                nc.scalar.copy(res[:, 2 * u : 2 * u + 2, :], acc[:])
+            nc.sync.dma_start(out_rows(0, PACK, c), res[:])
+
+        def last_product():
+            res = keep.tile([P, PACK, CHUNK], F32, name="res_last")
+            for mt in range(PACK):
+                acc = psum.tile([P, CHUNK], F32, name="acc", tag="bank%d" % (mt + 3))
+                second_product(last, mt, acc[:])
+                if mt % 2 == 0:
+                    nc.scalar.copy(res[:, mt, :], acc[:])
                 else:
-                    nc.scalar.copy(res[:, rows, :], acc[:])
-            if c < last:
-                nc.sync.dma_start(out[:, c0 : c0 + w].rearrange("(mt p) n -> p mt n", p=P), res[:])
+                    nc.vector.tensor_copy(res[:, mt, :], acc[:])
+                    nc.sync.dma_start(out_rows(mt - 1, 2, last), res[:, mt - 1 : mt + 1, :])
 
         cast_w2()
-        differences((0, 0), (0, 1))
+        differences(0, (0, 0), (0, 1))
         inverse([(0, 0), (0, 1)], [span(0), span(HALF)], [span(2 * HALF), span(3 * HALF)])
-        differences((1, 0), (1, 1))
+        differences(0, (1, 0), (1, 1))
         inverse([(1, 0), (1, 1)], [span(2 * HALF), span(3 * HALF)], [span(0), span(HALF)])
         numerator_gpsimd(0, S)
         numerator_gpsimd(1, S)
-        differences((2, 0), (3, 0))
+        differences(0, (2, 0), (3, 0))
         inverse([(2, 0), (3, 0)], [span(0), span(HALF)], [span(2 * HALF), last_root[:]])
-        differences((2, 1), (3, 1))
+        differences(0, (2, 1), (3, 1))
         inverse([(2, 1), (3, 1)], [span(3 * HALF // 2), span(5 * HALF // 2)], [span(0), span(4 * HALF)])
         numerator_gpsimd(2, HALF)
         numerators_vector(0, 2, 3)
+        for c in range(last + 1):
+            rounded_tile(c)
         quotient(0)
         w2_codes = keep.tile([P, N], U32, name="w2_codes", tag="w2_codes", align_bytes=64)
         quantise_w2(w2_codes)
@@ -258,6 +271,8 @@ def tile_picked_tvdual_none_p_kernel(tc, x_words, x_scales, w1, dual, gn, w2, of
             numerators_vector(c + 1, 1)
             quantise(c)
             product(c)
-        quotient(last)
-        quantise(last)
-        product(last)
+        for lo in (0, CHUNK // 2):
+            quotient(last, lo, lo + CHUNK // 2)
+        for lo in (0, CHUNK // 2):
+            quantise(last, lo, lo + CHUNK // 2)
+        last_product()

@@ -91,7 +91,7 @@ def tile_picked_tvdual_none_p_kernel(tc, x_words, x_scales, w1, dual, gn, w2, of
         nc.scalar.copy(dst[1][1], src[1][:, :, :, 2:4])
         for t in range(PACK):
             quantise_w1(t, 1)
-        ginv = keep.tile([P, PACK], F32, name="ginv", tag="rounded11", align_bytes=64)
+        ginv = keep.tile([P, PACK], F32, name="ginv", tag="rounded10", align_bytes=64)
         nc.vector.reciprocal(ginv[:], gs[:])
 
         def first_product(t, c0, w, bank):
@@ -118,7 +118,7 @@ def tile_picked_tvdual_none_p_kernel(tc, x_words, x_scales, w1, dual, gn, w2, of
         ys = [first_product(t, 0, S, t + 1) for t in range(1, PACK)]
         out_vector(win[0], 0, 0, HALF, y00)
         out_scalar(win[0], 0, HALF, HALF, y01)
-        w2_bf = keep.tile([P, N, PACK], BF16, name="w2_bf", align_bytes=64)
+        w2_bf = keep.tile([P, N, PACK], BF16, name="w2_bf", tag="rounded11", align_bytes=64)
         for t in range(1, PACK):
             out_scalar(win[t], t, 0, S, ys[t - 1])
         nc.scalar.copy(

@@ -20,8 +20,7 @@ PACK = 4
 HALF = S // 2
 MH = P // 2
 CHUNK = 128
-W1_ON_SCALAR = 20
-W2_ON_SCALAR = 64
+W2_ON_SCALAR = 112
 
 
 def tile_picked_tvdual_none_p_kernel(tc, x_words, x_scales, w1, dual, gn, w2, offs, nb, out):
@@ -36,7 +35,7 @@ def tile_picked_tvdual_none_p_kernel(tc, x_words, x_scales, w1, dual, gn, w2, of
         w2_raw = keep.tile([P, PACK, N], F32, name="w2_raw")
         dual_sb = keep.tile([P, PACK, S], F32, name="dual_sb")
         gn_sb = keep.tile([P, PACK], F32, name="gn_sb")
-        words = keep.tile([P, T], I32, name="words")
+        words = keep.tile([P, T], I32, name="words", tag="words", align_bytes=64)
         bytes_win = keep.tile([P, T], U8, name="bytes_win")
         ones = keep.tile([P, 1], F32, name="ones")
         warm = keep.tile([P, 1], F32, name="warm")
@@ -57,15 +56,16 @@ def tile_picked_tvdual_none_p_kernel(tc, x_words, x_scales, w1, dual, gn, w2, of
         nc.sync.dma_start(dual_sb[:], dual.rearrange("(p t) n -> p t n", t=PACK))
         nc.scalar.activation(warm[:], ones[:], ACT.Abs_reciprocal_sqrt, bias=ones[:])
 
-        w1_bf = [[keep.tile([P, 2, MH, PACK], BF16, name="w1_bf%d%d" % (u, g), tag="rounded%d%d" % (u, g), align_bytes=64) for g in range(2)] for u in range(2)]
-        w1_codes = [keep.tile([P, P], U32, name="w1_codes%d" % t, align_bytes=64) for t in range(PACK)]
-        w1_scales = [keep.tile([P, P], U8, name="w1_scales%d" % t, align_bytes=64) for t in range(PACK)]
+        early_bf = [keep.tile([P, 2, MH, PACK], BF16, name="early_bf%d" % u, tag="early_bf%d" % u, align_bytes=64) for u in range(2)]
+        late_bf = keep.tile([P, 2, P, PACK], BF16, name="late_bf", tag="late_bf", align_bytes=64)
+        early_codes = [keep.tile([P, P], U32, name="early_codes%d" % t, align_bytes=64) for t in range(2)]
+        early_scales = [keep.tile([P, P], U8, name="early_scales%d" % t, align_bytes=64) for t in range(2)]
         src = [w1_raw[u][:].rearrange("p j (m t) -> p m j t", t=PACK) for u in range(2)]
-        dst = [[w1_bf[u][g][:].rearrange("p t m j -> p m j t") for g in range(2)] for u in range(2)]
+        dst = [[early_bf[u][:].rearrange("p t m j -> p m j t"), late_bf[:, :, u * MH : (u + 1) * MH, :].rearrange("p t m j -> p m j t")] for u in range(2)]
 
-        def quantise_w1(t, u):
+        def quantise_early(t, u):
             cols = slice(u * MH, (u + 1) * MH)
-            nc.vector.quantize_mx(out=w1_codes[t][:, cols].bitcast(FP8X4), scales=w1_scales[t][:, cols], in_=w1_bf[u][t // 2][:, t % 2].rearrange("p m j -> p (m j)"))
+            nc.vector.quantize_mx(out=early_codes[t][:, cols].bitcast(FP8X4), scales=early_scales[t][:, cols], in_=early_bf[u][:, t].rearrange("p m j -> p (m j)"))
 
         x_bytes = keep.tile([P, S], U8, name="x_bytes", align_bytes=64)
         x_codes = keep.tile([P, S], U32, name="x_codes", align_bytes=64)
@@ -83,23 +83,27 @@ def tile_picked_tvdual_none_p_kernel(tc, x_words, x_scales, w1, dual, gn, w2, of
         nc.gpsimd.tensor_tensor(gs[:], gz[:], gn_sb[:], ALU.add)
 
         win = [keep.tile([P, S], F32, name="win%d" % t) for t in range(PACK)]
-        for t in range(PACK):
-            quantise_w1(t, 0)
+        for t in range(2):
+            quantise_early(t, 0)
         nc.vector.tensor_copy(x_codes[:], words[:].bitcast(U32).indirect(offs_sb[:]))
-        nc.scalar.copy(dst[1][0][:, :W1_ON_SCALAR], src[1][:, :W1_ON_SCALAR, :, 0:2])
-        nc.vector.tensor_copy(dst[1][0][:, W1_ON_SCALAR:], src[1][:, W1_ON_SCALAR:, :, 0:2])
-        nc.scalar.copy(dst[1][1], src[1][:, :, :, 2:4])
-        for t in range(PACK):
-            quantise_w1(t, 1)
-        ginv = keep.tile([P, PACK], F32, name="ginv", tag="rounded10", align_bytes=64)
+        nc.scalar.copy(dst[1][0], src[1][:, :, :, 0:2])
+        nc.vector.tensor_copy(dst[1][1], src[1][:, :, :, 2:4])
+        for t in range(2):
+            quantise_early(t, 1)
+        late_codes = keep.tile([P, 2 * P], U32, name="late_codes", tag="early_bf1", align_bytes=64)
+        late_scales = keep.tile([P, 2 * P], U8, name="late_scales", align_bytes=64)
+        nc.vector.quantize_mx(out=late_codes[:].bitcast(FP8X4), scales=late_scales[:], in_=late_bf[:].rearrange("p t m j -> p (t m j)"))
+        w1_codes = [early_codes[0][:], early_codes[1][:], late_codes[:, :P], late_codes[:, P:]]
+        w1_scales = [early_scales[0][:], early_scales[1][:], late_scales[:, :P], late_scales[:, P:]]
+        ginv = keep.tile([P, PACK], F32, name="ginv", tag="words", align_bytes=64)
         nc.vector.reciprocal(ginv[:], gs[:])
 
         def first_product(t, c0, w, bank):
             y = psum.tile([P, w], F32, name="y", tag="bank%d" % bank)
             nc.tensor.matmul_mx(
                 out=y[:],
-                lhsT=w1_codes[t][:].bitcast(FP8X4),
-                lhsT_scale=w1_scales[t][:],
+                lhsT=w1_codes[t].bitcast(FP8X4),
+                lhsT_scale=w1_scales[t],
                 rhs=x_codes[:, c0 : c0 + w].bitcast(FP8X4),
                 rhs_scale=x_bytes[:, c0 : c0 + w],
                 start=True,
@@ -118,7 +122,7 @@ def tile_picked_tvdual_none_p_kernel(tc, x_words, x_scales, w1, dual, gn, w2, of
         ys = [first_product(t, 0, S, t + 1) for t in range(1, PACK)]
         out_vector(win[0], 0, 0, HALF, y00)
         out_scalar(win[0], 0, HALF, HALF, y01)
-        w2_bf = keep.tile([P, N, PACK], BF16, name="w2_bf", tag="rounded11", align_bytes=64)
+        w2_bf = keep.tile([P, N, PACK], BF16, name="w2_bf", tag="late_bf", align_bytes=64)
         for t in range(1, PACK):
             out_scalar(win[t], t, 0, S, ys[t - 1])
         nc.scalar.copy(

@@ -18,8 +18,8 @@ ACT = mybir.ActivationFunctionType
 P = 128
 PACK = 4
 HALF = S // 2
-MH = P // 2
 CHUNK = 128
+W1_ON_VECTOR = (84, 40)
 W2_ON_SCALAR = 112
 
 
@@ -31,72 +31,62 @@ def tile_picked_tvdual_none_p_kernel(tc, x_words, x_scales, w1, dual, gn, w2, of
 
         offs_sb = keep.tile([P, S // 16], U16, name="offs_sb")
         nb_sb = keep.tile([P, S // 16], U16, name="nb_sb")
-        w1_raw = [keep.tile([P, PACK, H // 2], F32, name="w1_raw%d" % u) for u in range(2)]
+        w1_raw = keep.tile([P, PACK, H], F32, name="w1_raw")
         w2_raw = keep.tile([P, PACK, N], F32, name="w2_raw")
         dual_sb = keep.tile([P, PACK, S], F32, name="dual_sb")
         gn_sb = keep.tile([P, PACK], F32, name="gn_sb")
         words = keep.tile([P, T], I32, name="words", tag="words", align_bytes=64)
-        bytes_win = keep.tile([P, T], U8, name="bytes_win")
+        bytes_win = keep.tile([P, T], U8, name="bytes_win", tag="bytes_win", align_bytes=64)
         ones = keep.tile([P, 1], F32, name="ones")
         warm = keep.tile([P, 1], F32, name="warm")
 
         nc.vector.memset(bytes_win[:].bitcast(I32), 0)
         nc.vector.memset(ones[:], 1.0)
 
-        w1_rows = w1.rearrange("(p j) c -> p j c", j=PACK)
         nc.gpsimd.dma_start(gn_sb[:], gn.rearrange("(p t) o -> p (t o)", t=PACK))
-        nc.sync.dma_start(w1_raw[0][:], w1_rows[:, :, : H // 2])
+        word_rows = x_words[0].rearrange("p n t -> p (n t)").bitcast(I32)
+        nc.sync.dma_start(words[:, : T // 2], word_rows[:, : T // 2])
         nc.sync.dma_start(offs_sb[:], offs)
         for q in range(4):
             nc.sync.dma_start(bytes_win[q:P:32, :].bitcast(I32), x_scales[0, q:16:4, :].bitcast(I32))
-        nc.sync.dma_start(words[:], x_words[0].rearrange("p n t -> p (n t)").bitcast(I32))
-        nc.sync.dma_start(w1_raw[1][:], w1_rows[:, :, H // 2 :])
+        nc.sync.dma_start(words[:, T // 2 :], word_rows[:, T // 2 :])
+        nc.sync.dma_start(w1_raw[:], w1.rearrange("(p j) c -> p j c", j=PACK))
         nc.sync.dma_start(nb_sb[:], nb)
         nc.sync.dma_start(w2_raw[:], w2.rearrange("(p j) c -> p j c", j=PACK))
         nc.sync.dma_start(dual_sb[:], dual.rearrange("(p t) n -> p t n", t=PACK))
         nc.scalar.activation(warm[:], ones[:], ACT.Abs_reciprocal_sqrt, bias=ones[:])
 
-        early_bf = [keep.tile([P, 2, MH, PACK], BF16, name="early_bf%d" % u, tag="early_bf%d" % u, align_bytes=64) for u in range(2)]
-        late_bf = keep.tile([P, 2, P, PACK], BF16, name="late_bf", tag="late_bf", align_bytes=64)
-        early_codes = [keep.tile([P, P], U32, name="early_codes%d" % t, align_bytes=64) for t in range(2)]
-        early_scales = [keep.tile([P, P], U8, name="early_scales%d" % t, align_bytes=64) for t in range(2)]
-        src = [w1_raw[u][:].rearrange("p j (m t) -> p m j t", t=PACK) for u in range(2)]
-        dst = [[early_bf[u][:].rearrange("p t m j -> p m j t"), late_bf[:, :, u * MH : (u + 1) * MH, :].rearrange("p t m j -> p m j t")] for u in range(2)]
-
-        def quantise_early(t, u):
-            cols = slice(u * MH, (u + 1) * MH)
-            nc.vector.quantize_mx(out=early_codes[t][:, cols].bitcast(FP8X4), scales=early_scales[t][:, cols], in_=early_bf[u][:, t].rearrange("p m j -> p (m j)"))
-
         x_bytes = keep.tile([P, S], U8, name="x_bytes", align_bytes=64)
         x_codes = keep.tile([P, S], U32, name="x_codes", align_bytes=64)
         nc.vector.tensor_copy(x_bytes[:], bytes_win[:].indirect(offs_sb[:]))
-        for g in range(2):
-            nc.scalar.copy(dst[0][g], src[0][:, :, :, 2 * g : 2 * g + 2])
+        nc.vector.tensor_copy(x_codes[:], words[:].bitcast(U32).indirect(offs_sb[:]))
 
         gq = keep.tile([P, PACK], F32, name="gq")
+        ngq = keep.tile([P, PACK], F32, name="ngq")
         gz = keep.tile([P, PACK], F32, name="gz")
         gs = keep.tile([P, PACK], F32, name="gs")
         nc.gpsimd.tensor_scalar(gq[:], gn_sb[:], 0.25, None, ALU.mult)
-        ngq = keep.tile([P, PACK], F32, name="ngq")
         nc.gpsimd.tensor_scalar(ngq[:], gn_sb[:], -0.25, None, ALU.mult)
         nc.gpsimd.tensor_scalar(gz[:], gn_sb[:], 0.0, None, ALU.is_equal)
         nc.gpsimd.tensor_tensor(gs[:], gz[:], gn_sb[:], ALU.add)
-
-        win = [keep.tile([P, S], F32, name="win%d" % t) for t in range(PACK)]
-        for t in range(2):
-            quantise_early(t, 0)
-        nc.vector.tensor_copy(x_codes[:], words[:].bitcast(U32).indirect(offs_sb[:]))
-        nc.scalar.copy(dst[1][0], src[1][:, :, :, 0:2])
-        nc.vector.tensor_copy(dst[1][1], src[1][:, :, :, 2:4])
-        for t in range(2):
-            quantise_early(t, 1)
-        late_codes = keep.tile([P, 2 * P], U32, name="late_codes", tag="early_bf1", align_bytes=64)
-        late_scales = keep.tile([P, 2 * P], U8, name="late_scales", align_bytes=64)
-        nc.vector.quantize_mx(out=late_codes[:].bitcast(FP8X4), scales=late_scales[:], in_=late_bf[:].rearrange("p t m j -> p (t m j)"))
-        w1_codes = [early_codes[0][:], early_codes[1][:], late_codes[:, :P], late_codes[:, P:]]
-        w1_scales = [early_scales[0][:], early_scales[1][:], late_scales[:, :P], late_scales[:, P:]]
         ginv = keep.tile([P, PACK], F32, name="ginv", tag="words", align_bytes=64)
         nc.vector.reciprocal(ginv[:], gs[:])
+
+        w1_bf = [keep.tile([P, 2 * P * PACK], BF16, name="w1_bf%d" % g, tag="w1_bf%d" % g, align_bytes=64) for g in range(2)]
+        src = w1_raw[:].rearrange("p j (m t) -> p m j t", t=PACK)
+        for g in range(2):
+            dst = w1_bf[g][:].rearrange("p (t m j) -> p m j t", t=2, j=PACK)
+            nc.vector.tensor_copy(dst[:, : W1_ON_VECTOR[g]], src[:, : W1_ON_VECTOR[g], :, 2 * g : 2 * g + 2])
+            nc.scalar.copy(dst[:, W1_ON_VECTOR[g] :], src[:, W1_ON_VECTOR[g] :, :, 2 * g : 2 * g + 2])
+        early_codes = [keep.tile([P, P], U32, name="early_codes%d" % t, align_bytes=64) for t in range(2)]
+        early_scales = [keep.tile([P, P], U8, name="early_scales%d" % t, align_bytes=64) for t in range(2)]
+        for t in range(2):
+            nc.vector.quantize_mx(out=early_codes[t][:].bitcast(FP8X4), scales=early_scales[t][:], in_=w1_bf[0][:, t * H : (t + 1) * H])
+        late_codes = keep.tile([P, 2 * P], U32, name="late_codes", tag="w1_bf0", align_bytes=64)
+        late_scales = keep.tile([P, 2 * P], U8, name="late_scales", align_bytes=64)
+        nc.vector.quantize_mx(out=late_codes[:].bitcast(FP8X4), scales=late_scales[:], in_=w1_bf[1][:])
+        w1_codes = [early_codes[0][:], early_codes[1][:], late_codes[:, :P], late_codes[:, P:]]
+        w1_scales = [early_scales[0][:], early_scales[1][:], late_scales[:, :P], late_scales[:, P:]]
 
         def first_product(t, c0, w, bank):
             y = psum.tile([P, w], F32, name="y", tag="bank%d" % bank)
@@ -111,58 +101,42 @@ def tile_picked_tvdual_none_p_kernel(tc, x_words, x_scales, w1, dual, gn, w2, of
             )
             return y
 
-        def out_scalar(dst_tile, t, c0, w, y):
-            nc.scalar.activation(dst_tile[:, c0 : c0 + w], y[:], ACT.Copy, scale=gq[:, t : t + 1])
-
-        def out_vector(dst_tile, t, c0, w, y):
-            nc.vector.tensor_scalar(dst_tile[:, c0 : c0 + w], y[:], gq[:, t : t + 1], None, ALU.mult)
-
+        win = [keep.tile([P, S], F32, name="win%d" % t) for t in range(PACK)]
         y00 = first_product(0, 0, HALF, 0)
         y01 = first_product(0, HALF, HALF, 1)
         ys = [first_product(t, 0, S, t + 1) for t in range(1, PACK)]
-        out_vector(win[0], 0, 0, HALF, y00)
-        out_scalar(win[0], 0, HALF, HALF, y01)
-        w2_bf = keep.tile([P, N, PACK], BF16, name="w2_bf", tag="late_bf", align_bytes=64)
+        nc.vector.tensor_scalar(win[0][:, :HALF], y00[:], gq[:, 0:1], None, ALU.mult)
+        nc.scalar.activation(win[0][:, HALF:], y01[:], ACT.Copy, scale=gq[:, 0:1])
         for t in range(1, PACK):
-            out_scalar(win[t], t, 0, S, ys[t - 1])
-        nc.scalar.copy(
-            w2_bf[:, :W2_ON_SCALAR, :].rearrange("p (c i) j -> p c j i", i=2),
-            w2_raw[:, :, :W2_ON_SCALAR].rearrange("p j (c i) -> p c j i", i=2),
-        )
+            nc.scalar.activation(win[t][:], ys[t - 1][:], ACT.Copy, scale=gq[:, t : t + 1])
         y_half = {(0, 0): y00[:], (0, 1): y01[:]}
         for t in range(1, PACK):
             for h in range(2):
                 y_half[t, h] = ys[t - 1][:, h * HALF : (h + 1) * HALF]
 
+        w2_bf = keep.tile([P, N, PACK], BF16, name="w2_bf", tag="w1_bf1", align_bytes=64)
+        nc.scalar.copy(
+            w2_bf[:, :W2_ON_SCALAR, :].rearrange("p (c i) j -> p c j i", i=2),
+            w2_raw[:, :, :W2_ON_SCALAR].rearrange("p j (c i) -> p c j i", i=2),
+        )
+        nc.gpsimd.tensor_scalar(w2_bf[:, W2_ON_SCALAR:, :], w2_raw[:, :, W2_ON_SCALAR:].rearrange("p j c -> p c j"), 1.0, 0.0, ALU.mult, ALU.add)
         last_root = keep.tile([P, HALF], F32, name="last_root", tag="w2_codes", align_bytes=64)
         w2_scales = keep.tile([P, N], U8, name="w2_scales", align_bytes=64)
-
-        def cast_w2():
-            nc.gpsimd.tensor_scalar(w2_bf[:, W2_ON_SCALAR:, :], w2_raw[:, :, W2_ON_SCALAR:].rearrange("p j c -> p c j"), 1.0, 0.0, ALU.mult, ALU.add)
-
-        def quantise_w2(w2_codes):
-            nc.vector.quantize_mx(out=w2_codes[:].bitcast(FP8X4), scales=w2_scales[:], in_=w2_bf[:].rearrange("p c j -> p (c j)"))
 
         diff = [keep.tile([P, S], F32, name="diff%d" % t) for t in range(PACK)]
         recip = keep.tile([P, 2, PACK, HALF], F32, name="recip")
         fetched = {}
-        gained = [keep.tile([P, S], F32, name="gained%d" % t) for t in range(3)]
+        gained = [keep.tile([P, S], F32, name="gained%d" % t) for t in range(PACK)]
         num_row = keep.tile([P, PACK * S], F32, name="num_row", align_bytes=64)
         num = num_row[:].rearrange("p (c t n) -> p c t n", t=PACK, n=CHUNK)
         zb, zc, zs = {}, {}, {}
 
-        def fetch(i, t, h):
-            fetched[t, h] = keep.tile([P, HALF], F32, name="fetched", tag="fetched%d" % i)
-            nc.vector.tensor_copy(fetched[t, h][:], win[t][:].indirect(nb_sb[:, h * HALF // 16 : (h + 1) * HALF // 16]))
-
-        def difference(t, h):
-            nc.vector.scalar_tensor_tensor(diff[t][:, h * HALF : (h + 1) * HALF], y_half[t, h], ngq[:, t : t + 1], fetched[t, h][:], ALU.mult, ALU.add)
-
-        def differences(slot, *pieces):
+        def differences(*pieces):
             for i, (t, h) in enumerate(pieces):
-                fetch(slot + i, t, h)
+                fetched[t, h] = keep.tile([P, HALF], F32, name="fetched", tag="fetched%d" % i)
+                nc.vector.tensor_copy(fetched[t, h][:], win[t][:].indirect(nb_sb[:, h * HALF // 16 : (h + 1) * HALF // 16]))
             for t, h in pieces:
-                difference(t, h)
+                nc.vector.scalar_tensor_tensor(diff[t][:, h * HALF : (h + 1) * HALF], y_half[t, h], ngq[:, t : t + 1], fetched[t, h][:], ALU.mult, ALU.add)
 
         work = keep.tile([P, 5 * HALF], F32, name="work")
 
@@ -181,17 +155,10 @@ def tile_picked_tvdual_none_p_kernel(tc, x_words, x_scales, w1, dual, gn, w2, of
             nc.gpsimd.tensor_scalar(gained[t][:, :w], dual_sb[:, t, :w], gn_sb[:, t : t + 1], 0.0, ALU.mult, ALU.add)
             nc.gpsimd.tensor_tensor(num[:, : w // CHUNK, t, :], gained[t][:, :w].rearrange("p (c n) -> p c n", n=CHUNK), diff[t][:, :w].rearrange("p (c n) -> p c n", n=CHUNK), ALU.add)
 
-        def numerators_vector(c0, n, t0=2):
-            cols = slice(c0 * CHUNK, (c0 + n) * CHUNK)
-            for t in range(t0, PACK):
-                nc.vector.scalar_tensor_tensor(
-                    num[:, c0 : c0 + n, t, :],
-                    dual_sb[:, t, cols].rearrange("p (c n) -> p c n", n=CHUNK),
-                    gn_sb[:, t : t + 1],
-                    diff[t][:, cols].rearrange("p (c n) -> p c n", n=CHUNK),
-                    ALU.mult,
-                    ALU.add,
-                )
+        def numerators_vector(c):
+            cols = slice(c * CHUNK, (c + 1) * CHUNK)
+            for t in range(1, PACK):
+                nc.vector.scalar_tensor_tensor(num[:, c, t, :], dual_sb[:, t, cols], gn_sb[:, t : t + 1], diff[t][:, cols], ALU.mult, ALU.add)
 
         last = S // CHUNK - 1
 
@@ -250,29 +217,27 @@ def tile_picked_tvdual_none_p_kernel(tc, x_words, x_scales, w1, dual, gn, w2, of
                     nc.vector.tensor_copy(res[:, mt, :], acc[:])
                     nc.sync.dma_start(out_rows(mt - 1, 2, last), res[:, mt - 1 : mt + 1, :])
 
-        cast_w2()
-        differences(0, (0, 0), (0, 1))
+        differences((0, 0), (0, 1))
         inverse([(0, 0), (0, 1)], [span(0), span(HALF)], [span(2 * HALF), span(3 * HALF)])
-        differences(0, (1, 0), (1, 1))
-        inverse([(1, 0), (1, 1)], [span(2 * HALF), span(3 * HALF)], [span(0), span(HALF)])
+        differences((1, 0), (2, 0))
+        inverse([(1, 0), (2, 0)], [span(2 * HALF), span(3 * HALF)], [span(0), span(HALF)])
         numerator_gpsimd(0, S)
-        numerator_gpsimd(1, S)
-        differences(0, (2, 0), (3, 0))
-        inverse([(2, 0), (3, 0)], [span(0), span(HALF)], [span(2 * HALF), last_root[:]])
-        differences(0, (2, 1), (3, 1))
+        differences((3, 0), (1, 1))
+        inverse([(3, 0), (1, 1)], [span(0), span(HALF)], [last_root[:], span(3 * HALF)])
+        for t in range(1, PACK):
+            numerator_gpsimd(t, HALF)
+        differences((2, 1), (3, 1))
         inverse([(2, 1), (3, 1)], [span(3 * HALF // 2), span(5 * HALF // 2)], [span(0), span(4 * HALF)])
-        numerator_gpsimd(2, HALF)
-        numerators_vector(0, 2, 3)
         for c in range(last + 1):
             rounded_tile(c)
         quotient(0)
         w2_codes = keep.tile([P, N], U32, name="w2_codes", tag="w2_codes", align_bytes=64)
-        quantise_w2(w2_codes)
+        nc.vector.quantize_mx(out=w2_codes[:].bitcast(FP8X4), scales=w2_scales[:], in_=w2_bf[:].rearrange("p c j -> p (c j)"))
         quantise(0)
         product(0)
         for c in range(1, last):
             quotient(c)
-            numerators_vector(c + 1, 1)
+            numerators_vector(c + 1)
             quantise(c)
             product(c)
         for lo in (0, CHUNK // 2):

@@ -19,8 +19,8 @@ P = 128
 PACK = 4
 HALF = S // 2
 CHUNK = 128
-W1_ON_VECTOR = (84, 40)
-W2_ON_SCALAR = 112
+MH = P // 2
+W2_ON_SCALAR = 80
 
 
 def tile_picked_tvdual_none_p_kernel(tc, x_words, x_scales, w1, dual, gn, w2, offs, nb, out):
@@ -31,9 +31,9 @@ def tile_picked_tvdual_none_p_kernel(tc, x_words, x_scales, w1, dual, gn, w2, of
 
         offs_sb = keep.tile([P, S // 16], U16, name="offs_sb")
         nb_sb = keep.tile([P, S // 16], U16, name="nb_sb")
-        w1_raw = keep.tile([P, PACK, H], F32, name="w1_raw")
+        w1_raw = [keep.tile([P, PACK, H // 2], F32, name="w1_raw%d" % u) for u in range(2)]
         w2_raw = keep.tile([P, PACK, N], F32, name="w2_raw")
-        dual_sb = keep.tile([P, PACK, S], F32, name="dual_sb")
+        dual_row = keep.tile([P, PACK * S], F32, name="dual_row")
         gn_sb = keep.tile([P, PACK], F32, name="gn_sb")
         words = keep.tile([P, T], I32, name="words", tag="words", align_bytes=64)
         bytes_win = keep.tile([P, T], U8, name="bytes_win", tag="bytes_win", align_bytes=64)
@@ -44,22 +44,22 @@ def tile_picked_tvdual_none_p_kernel(tc, x_words, x_scales, w1, dual, gn, w2, of
         nc.vector.memset(ones[:], 1.0)
 
         nc.gpsimd.dma_start(gn_sb[:], gn.rearrange("(p t) o -> p (t o)", t=PACK))
-        word_rows = x_words[0].rearrange("p n t -> p (n t)").bitcast(I32)
-        nc.sync.dma_start(words[:, : T // 2], word_rows[:, : T // 2])
+        w1_rows = w1.rearrange("(p j) c -> p j c", j=PACK)
+        nc.sync.dma_start(w1_raw[0][:], w1_rows[:, :, : H // 2])
         nc.sync.dma_start(offs_sb[:], offs)
         for q in range(4):
             nc.sync.dma_start(bytes_win[q:P:32, :].bitcast(I32), x_scales[0, q:16:4, :].bitcast(I32))
-        nc.sync.dma_start(words[:, T // 2 :], word_rows[:, T // 2 :])
-        nc.sync.dma_start(w1_raw[:], w1.rearrange("(p j) c -> p j c", j=PACK))
+        nc.sync.dma_start(words[:], x_words[0].rearrange("p n t -> p (n t)").bitcast(I32))
+        nc.sync.dma_start(w1_raw[1][:], w1_rows[:, :, H // 2 :])
         nc.sync.dma_start(nb_sb[:], nb)
         nc.sync.dma_start(w2_raw[:], w2.rearrange("(p j) c -> p j c", j=PACK))
-        nc.sync.dma_start(dual_sb[:], dual.rearrange("(p t) n -> p t n", t=PACK))
+        nc.sync.dma_start(dual_row[:], dual.rearrange("(p t) n -> p (t n)", t=PACK))
+        dual_sb = [dual_row[:, t * S : (t + 1) * S] for t in range(PACK)]
         nc.scalar.activation(warm[:], ones[:], ACT.Abs_reciprocal_sqrt, bias=ones[:])
 
         x_bytes = keep.tile([P, S], U8, name="x_bytes", align_bytes=64)
         x_codes = keep.tile([P, S], U32, name="x_codes", align_bytes=64)
         nc.vector.tensor_copy(x_bytes[:], bytes_win[:].indirect(offs_sb[:]))
-        nc.vector.tensor_copy(x_codes[:], words[:].bitcast(U32).indirect(offs_sb[:]))
 
         gq = keep.tile([P, PACK], F32, name="gq")
         ngq = keep.tile([P, PACK], F32, name="ngq")
@@ -69,24 +69,35 @@ def tile_picked_tvdual_none_p_kernel(tc, x_words, x_scales, w1, dual, gn, w2, of
         nc.gpsimd.tensor_scalar(ngq[:], gn_sb[:], -0.25, None, ALU.mult)
         nc.gpsimd.tensor_scalar(gz[:], gn_sb[:], 0.0, None, ALU.is_equal)
         nc.gpsimd.tensor_tensor(gs[:], gz[:], gn_sb[:], ALU.add)
-        ginv = keep.tile([P, PACK], F32, name="ginv", tag="words", align_bytes=64)
-        nc.vector.reciprocal(ginv[:], gs[:])
 
-        w1_bf = [keep.tile([P, 2 * P * PACK], BF16, name="w1_bf%d" % g, tag="w1_bf%d" % g, align_bytes=64) for g in range(2)]
-        src = w1_raw[:].rearrange("p j (m t) -> p m j t", t=PACK)
-        for g in range(2):
-            dst = w1_bf[g][:].rearrange("p (t m j) -> p m j t", t=2, j=PACK)
-            nc.vector.tensor_copy(dst[:, : W1_ON_VECTOR[g]], src[:, : W1_ON_VECTOR[g], :, 2 * g : 2 * g + 2])
-            nc.scalar.copy(dst[:, W1_ON_VECTOR[g] :], src[:, W1_ON_VECTOR[g] :, :, 2 * g : 2 * g + 2])
+        early_bf = [keep.tile([P, 2, MH, PACK], BF16, name="early_bf%d" % u, tag="early_bf%d" % u, align_bytes=64) for u in range(2)]
+        late_row = keep.tile([P, (PACK + 2) * HALF], F32, name="late_row", align_bytes=64)
+        late_bf = late_row[:, HALF : HALF + P * PACK].bitcast(BF16).rearrange("p (t m j) -> p t m j", t=2, j=PACK)
         early_codes = [keep.tile([P, P], U32, name="early_codes%d" % t, align_bytes=64) for t in range(2)]
         early_scales = [keep.tile([P, P], U8, name="early_scales%d" % t, align_bytes=64) for t in range(2)]
+        src = [w1_raw[u][:].rearrange("p j (m t) -> p m j t", t=PACK) for u in range(2)]
+        dst = [[early_bf[u][:].rearrange("p t m j -> p m j t"), late_bf[:, :, u * MH : (u + 1) * MH, :].rearrange("p t m j -> p m j t")] for u in range(2)]
+
+        def quantise_early(t, u):
+            cols = slice(u * MH, (u + 1) * MH)
+            nc.vector.quantize_mx(out=early_codes[t][:, cols].bitcast(FP8X4), scales=early_scales[t][:, cols], in_=early_bf[u][:, t].rearrange("p m j -> p (m j)"))
+
+        for g in range(2):
+            nc.scalar.copy(dst[0][g], src[0][:, :, :, 2 * g : 2 * g + 2])
         for t in range(2):
-            nc.vector.quantize_mx(out=early_codes[t][:].bitcast(FP8X4), scales=early_scales[t][:], in_=w1_bf[0][:, t * H : (t + 1) * H])
-        late_codes = keep.tile([P, 2 * P], U32, name="late_codes", tag="w1_bf0", align_bytes=64)
+            quantise_early(t, 0)
+        nc.vector.tensor_copy(x_codes[:], words[:].bitcast(U32).indirect(offs_sb[:]))
+        nc.scalar.copy(dst[1][0], src[1][:, :, :, 0:2])
+        nc.vector.tensor_copy(dst[1][1], src[1][:, :, :, 2:4])
+        for t in range(2):
+            quantise_early(t, 1)
+        late_codes = keep.tile([P, 2 * P], U32, name="late_codes", tag="early_bf1", align_bytes=64)
         late_scales = keep.tile([P, 2 * P], U8, name="late_scales", align_bytes=64)
-        nc.vector.quantize_mx(out=late_codes[:].bitcast(FP8X4), scales=late_scales[:], in_=w1_bf[1][:])
+        nc.vector.quantize_mx(out=late_codes[:].bitcast(FP8X4), scales=late_scales[:], in_=late_row[:, HALF : HALF + P * PACK].bitcast(BF16))
         w1_codes = [early_codes[0][:], early_codes[1][:], late_codes[:, :P], late_codes[:, P:]]
         w1_scales = [early_scales[0][:], early_scales[1][:], late_scales[:, :P], late_scales[:, P:]]
+        ginv = keep.tile([P, PACK], F32, name="ginv", tag="words", align_bytes=64)
+        nc.vector.reciprocal(ginv[:], gs[:])
 
         def first_product(t, c0, w, bank):
             y = psum.tile([P, w], F32, name="y", tag="bank%d" % bank)
@@ -102,70 +113,81 @@ def tile_picked_tvdual_none_p_kernel(tc, x_words, x_scales, w1, dual, gn, w2, of
             return y
 
         win = [keep.tile([P, S], F32, name="win%d" % t) for t in range(PACK)]
-        y00 = first_product(0, 0, HALF, 0)
-        y01 = first_product(0, HALF, HALF, 1)
-        ys = [first_product(t, 0, S, t + 1) for t in range(1, PACK)]
-        nc.vector.tensor_scalar(win[0][:, :HALF], y00[:], gq[:, 0:1], None, ALU.mult)
-        nc.scalar.activation(win[0][:, HALF:], y01[:], ACT.Copy, scale=gq[:, 0:1])
-        for t in range(1, PACK):
-            nc.scalar.activation(win[t][:], ys[t - 1][:], ACT.Copy, scale=gq[:, t : t + 1])
-        y_half = {(0, 0): y00[:], (0, 1): y01[:]}
-        for t in range(1, PACK):
+        y_half = {}
+        for t in range(2):
             for h in range(2):
-                y_half[t, h] = ys[t - 1][:, h * HALF : (h + 1) * HALF]
+                y_half[t, h] = first_product(t, h * HALF, HALF, 2 * t + h)[:]
+        whole = {t: first_product(t, 0, S, t + 2) for t in range(2, PACK)}
+        for t in range(2):
+            nc.vector.tensor_scalar(win[t][:, :HALF], y_half[t, 0], gq[:, t : t + 1], None, ALU.mult)
+            nc.scalar.activation(win[t][:, HALF:], y_half[t, 1], ACT.Copy, scale=gq[:, t : t + 1])
+        for t in range(2, PACK):
+            nc.scalar.activation(win[t][:], whole[t][:], ACT.Copy, scale=gq[:, t : t + 1])
+            for h in range(2):
+                y_half[t, h] = whole[t][:, h * HALF : (h + 1) * HALF]
 
-        w2_bf = keep.tile([P, N, PACK], BF16, name="w2_bf", tag="w1_bf1", align_bytes=64)
+        w2_flat = late_row[:, HALF : HALF + N * PACK // 2].bitcast(BF16)
+        w2_bf = w2_flat.rearrange("p (c j) -> p c j", j=PACK)
         nc.scalar.copy(
             w2_bf[:, :W2_ON_SCALAR, :].rearrange("p (c i) j -> p c j i", i=2),
             w2_raw[:, :, :W2_ON_SCALAR].rearrange("p j (c i) -> p c j i", i=2),
         )
         nc.gpsimd.tensor_scalar(w2_bf[:, W2_ON_SCALAR:, :], w2_raw[:, :, W2_ON_SCALAR:].rearrange("p j c -> p c j"), 1.0, 0.0, ALU.mult, ALU.add)
-        last_root = keep.tile([P, HALF], F32, name="last_root", tag="w2_codes", align_bytes=64)
+        shared = keep.tile([P, S], F32, name="shared", tag="w2_codes", align_bytes=64)
         w2_scales = keep.tile([P, N], U8, name="w2_scales", align_bytes=64)
 
         diff = [keep.tile([P, S], F32, name="diff%d" % t) for t in range(PACK)]
         recip = keep.tile([P, 2, PACK, HALF], F32, name="recip")
         fetched = {}
-        gained = [keep.tile([P, S], F32, name="gained%d" % t) for t in range(PACK)]
-        num_row = keep.tile([P, PACK * S], F32, name="num_row", align_bytes=64)
-        num = num_row[:].rearrange("p (c t n) -> p c t n", t=PACK, n=CHUNK)
+        gained = [keep.tile([P, HALF], F32, name="gained%d" % t) for t in range(PACK - 1)]
+        early_row = keep.tile([P, PACK * HALF], F32, name="early_row")
+        num = [row[:, : PACK * HALF].rearrange("p (t n) -> p t n", t=PACK) for row in (early_row, late_row)]
         zb, zc, zs = {}, {}, {}
+        piece = {(t, h): diff[t][:, h * HALF : (h + 1) * HALF] for t in range(PACK) for h in range(2)}
 
         def differences(*pieces):
             for i, (t, h) in enumerate(pieces):
                 fetched[t, h] = keep.tile([P, HALF], F32, name="fetched", tag="fetched%d" % i)
                 nc.vector.tensor_copy(fetched[t, h][:], win[t][:].indirect(nb_sb[:, h * HALF // 16 : (h + 1) * HALF // 16]))
             for t, h in pieces:
-                nc.vector.scalar_tensor_tensor(diff[t][:, h * HALF : (h + 1) * HALF], y_half[t, h], ngq[:, t : t + 1], fetched[t, h][:], ALU.mult, ALU.add)
+                nc.vector.scalar_tensor_tensor(piece[t, h], y_half[t, h], ngq[:, t : t + 1], fetched[t, h][:], ALU.mult, ALU.add)
 
         work = keep.tile([P, 5 * HALF], F32, name="work")
 
         def span(first):
             return work[:, first : first + HALF]
 
-        def inverse(pieces, sizes, roots):
+        def sizes_and_roots(pieces, sizes, roots):
             for (t, h), size in zip(pieces, sizes):
-                nc.scalar.activation(size, diff[t][:, h * HALF : (h + 1) * HALF], ACT.Abs, scale=ginv[:, t : t + 1])
+                nc.scalar.activation(size, piece[t, h], ACT.Abs, scale=ginv[:, t : t + 1])
             for size, root in zip(sizes, roots):
                 nc.scalar.activation(root, size, ACT.Abs_reciprocal_sqrt, bias=ones[:])
+
+        def square(t, h, root):
+            nc.scalar.activation(recip[:, h, t, :], root, ACT.Square)
+
+        def inverse(pieces, sizes, roots):
+            sizes_and_roots(pieces, sizes, roots)
             for (t, h), root in zip(pieces, roots):
-                nc.scalar.activation(recip[:, h, t, :], root, ACT.Square)
+                square(t, h, root)
 
-        def numerator_gpsimd(t, w):
-            nc.gpsimd.tensor_scalar(gained[t][:, :w], dual_sb[:, t, :w], gn_sb[:, t : t + 1], 0.0, ALU.mult, ALU.add)
-            nc.gpsimd.tensor_tensor(num[:, : w // CHUNK, t, :], gained[t][:, :w].rearrange("p (c n) -> p c n", n=CHUNK), diff[t][:, :w].rearrange("p (c n) -> p c n", n=CHUNK), ALU.add)
+        def add_gpsimd(t, h, scaled):
+            nc.gpsimd.tensor_tensor(num[h][:, t, :], scaled, piece[t, h], ALU.add)
 
-        def numerators_vector(c):
-            cols = slice(c * CHUNK, (c + 1) * CHUNK)
-            for t in range(1, PACK):
-                nc.vector.scalar_tensor_tensor(num[:, c, t, :], dual_sb[:, t, cols], gn_sb[:, t : t + 1], diff[t][:, cols], ALU.mult, ALU.add)
+        def numerator_gpsimd(t):
+            nc.gpsimd.tensor_scalar(gained[t][:], dual_sb[t][:, :HALF], gn_sb[:, t : t + 1], 0.0, ALU.mult, ALU.add)
+            add_gpsimd(t, 0, gained[t][:])
+
+        def numerator_vector(t, lo, hi):
+            cols = slice(HALF + lo, HALF + hi)
+            nc.vector.scalar_tensor_tensor(num[1][:, t, lo:hi], dual_sb[t][:, cols], gn_sb[:, t : t + 1], diff[t][:, cols], ALU.mult, ALU.add)
 
         last = S // CHUNK - 1
+        third_row = keep.tile([P, PACK * CHUNK], F32, name="third_row", align_bytes=64)
 
         def rounded_tile(c):
-            if c < 2:
-                first = ((c + 2) * PACK + 2) * CHUNK
-                zb[c] = num_row[:, first : first + 2 * CHUNK].bitcast(BF16)
+            if c == last:
+                zb[c] = third_row[:, 2 * CHUNK :].bitcast(BF16)
             else:
                 zb[c] = keep.tile([P, CHUNK * PACK], BF16, name="zb%d" % c, align_bytes=64)[:]
             zc[c] = keep.tile([P, CHUNK], U32, name="zc%d" % c, align_bytes=64)
@@ -175,7 +197,7 @@ def tile_picked_tvdual_none_p_kernel(tc, x_words, x_scales, w1, dual, gn, w2, of
             h, r0 = c * CHUNK // HALF, c * CHUNK % HALF
             nc.vector.tensor_tensor(
                 zb[c][:, lo * PACK : hi * PACK].rearrange("p (c i t) -> p c t i", i=2, t=PACK),
-                num[:, c, :, lo:hi].rearrange("p t (c i) -> p c t i", i=2),
+                num[h][:, :, r0 + lo : r0 + hi].rearrange("p t (c i) -> p c t i", i=2),
                 recip[:, h, :, r0 + lo : r0 + hi].rearrange("p t (c i) -> p c t i", i=2),
                 ALU.mult,
             )
@@ -197,19 +219,24 @@ def tile_picked_tvdual_none_p_kernel(tc, x_words, x_scales, w1, dual, gn, w2, of
         def out_rows(mt0, n, c):
             return out[mt0 * P : (mt0 + n) * P, c * CHUNK : (c + 1) * CHUNK].rearrange("(mt p) n -> p mt n", p=P)
 
-        def product(c):
-            res = keep.tile([P, PACK, CHUNK], F32, name="res%d" % c)
-            for u in range(2):
-                acc = psum.tile([P, 2, CHUNK], F32, name="acc", tag="bank%d" % ((2 * c + u + 5) % 8))
-                for v in range(2):
-                    second_product(c, 2 * u + v, acc[:, v, :])
-                nc.scalar.copy(res[:, 2 * u : 2 * u + 2, :], acc[:])
-            nc.sync.dma_start(out_rows(0, PACK, c), res[:])
+        def early_product(c, res):
+            acc = psum.tile([P, PACK * CHUNK], F32, name="acc", tag="bank%d" % (6 + c))
+            for mt in range(PACK):
+                second_product(c, mt, acc[:, mt * CHUNK : (mt + 1) * CHUNK])
+            nc.scalar.copy(res, acc[:])
+            nc.sync.dma_start(out_rows(0, PACK, c), res.rearrange("p (m n) -> p m n", n=CHUNK))
+
+        def third_product(c):
+            res = third_row[:].rearrange("p (m n) -> p m n", n=CHUNK)
+            banks = [psum.tile([P, 2, CHUNK], F32, name="acc", tag="bank%d" % (5 * u)) for u in range(2)]
+            for mt in range(PACK):
+                second_product(c, mt, banks[mt // 2][:, mt % 2, :])
+            return res, banks
 
         def last_product():
             res = keep.tile([P, PACK, CHUNK], F32, name="res_last")
             for mt in range(PACK):
-                acc = psum.tile([P, CHUNK], F32, name="acc", tag="bank%d" % (mt + 3))
+                acc = psum.tile([P, CHUNK], F32, name="acc", tag="bank%d" % (mt + 1))
                 second_product(last, mt, acc[:])
                 if mt % 2 == 0:
                     nc.scalar.copy(res[:, mt, :], acc[:])
@@ -217,31 +244,43 @@ def tile_picked_tvdual_none_p_kernel(tc, x_words, x_scales, w1, dual, gn, w2, of
                     nc.vector.tensor_copy(res[:, mt, :], acc[:])
                     nc.sync.dma_start(out_rows(mt - 1, 2, last), res[:, mt - 1 : mt + 1, :])
 
-        differences((0, 0), (0, 1))
-        inverse([(0, 0), (0, 1)], [span(0), span(HALF)], [span(2 * HALF), span(3 * HALF)])
-        differences((1, 0), (2, 0))
-        inverse([(1, 0), (2, 0)], [span(2 * HALF), span(3 * HALF)], [span(0), span(HALF)])
-        numerator_gpsimd(0, S)
-        differences((3, 0), (1, 1))
-        inverse([(3, 0), (1, 1)], [span(0), span(HALF)], [last_root[:], span(3 * HALF)])
-        for t in range(1, PACK):
-            numerator_gpsimd(t, HALF)
+        differences((0, 0), (1, 0))
+        inverse([(0, 0), (1, 0)], [span(0), span(HALF)], [span(4 * HALF), shared[:, :HALF]])
+        nc.scalar.activation(span(4 * HALF), dual_sb[3][:, :HALF], ACT.Copy, scale=gn_sb[:, 3:4])
+        nc.scalar.activation(shared[:, :HALF], dual_sb[0][:, HALF:], ACT.Copy, scale=gn_sb[:, 0:1])
+        differences((2, 0), (3, 0))
+        inverse([(2, 0), (3, 0)], [dual_sb[3][:, :HALF], dual_sb[0][:, HALF:]], [span(HALF // 2), shared[:, HALF:]])
+        for t in range(PACK - 1):
+            numerator_gpsimd(t)
+        add_gpsimd(3, 0, span(4 * HALF))
+        differences((0, 1), (1, 1))
+        inverse([(0, 1), (1, 1)], [span(0), span(HALF)], [span(2 * HALF), span(3 * HALF)])
+        add_gpsimd(0, 1, shared[:, :HALF])
         differences((2, 1), (3, 1))
-        inverse([(2, 1), (3, 1)], [span(3 * HALF // 2), span(5 * HALF // 2)], [span(0), span(4 * HALF)])
         for c in range(last + 1):
             rounded_tile(c)
         quotient(0)
         w2_codes = keep.tile([P, N], U32, name="w2_codes", tag="w2_codes", align_bytes=64)
-        nc.vector.quantize_mx(out=w2_codes[:].bitcast(FP8X4), scales=w2_scales[:], in_=w2_bf[:].rearrange("p c j -> p (c j)"))
+        nc.vector.quantize_mx(out=w2_codes[:].bitcast(FP8X4), scales=w2_scales[:], in_=w2_flat)
+        inverse([(2, 1), (3, 1)], [span(2 * HALF), span(3 * HALF)], [span(0), late_row[:, PACK * HALF - CHUNK : PACK * HALF + CHUNK]])
         quantise(0)
-        product(0)
-        for c in range(1, last):
-            quotient(c)
-            numerators_vector(c + 1)
-            quantise(c)
-            product(c)
+        early_product(0, work[:, : PACK * CHUNK])
+        quotient(1)
+        numerator_vector(1, 0, HALF)
+        quantise(1)
+        early_product(1, late_row[:, PACK * HALF :])
+        numerator_vector(2, 0, CHUNK)
+        numerator_vector(3, 0, CHUNK)
+        numerator_vector(2, CHUNK, HALF)
+        quotient(2)
+        numerator_vector(3, CHUNK, HALF)
+        quantise(2)
+        res, banks = third_product(2)
+        nc.scalar.copy(res[:, :2, :], banks[0][:])
         for lo in (0, CHUNK // 2):
             quotient(last, lo, lo + CHUNK // 2)
         for lo in (0, CHUNK // 2):
             quantise(last, lo, lo + CHUNK // 2)
+        nc.vector.tensor_copy(res[:, 2:, :], banks[1][:])
+        nc.sync.dma_start(out_rows(0, PACK, 2), res)
         last_product()

@@ -32,34 +32,35 @@ def tile_picked_tvdual_none_p_kernel(tc, x_words, x_scales, w1, dual, gn, w2, of
         offs_sb = keep.tile([P, S // 16], U16, name="offs_sb")
         nb_sb = keep.tile([P, S // 16], U16, name="nb_sb")
         w1_raw = [keep.tile([P, PACK, H // 2], F32, name="w1_raw%d" % u) for u in range(2)]
-        w2_raw = keep.tile([P, PACK, N], F32, name="w2_raw")
-        dual_row = keep.tile([P, PACK * S], F32, name="dual_row")
         gn_sb = keep.tile([P, PACK], F32, name="gn_sb")
         words = keep.tile([P, T], I32, name="words", tag="words", align_bytes=64)
         bytes_win = keep.tile([P, T], U8, name="bytes_win", tag="bytes_win", align_bytes=64)
         ones = keep.tile([P, 1], F32, name="ones")
         warm = keep.tile([P, 1], F32, name="warm")
 
-        nc.vector.memset(bytes_win[:].bitcast(I32), 0)
+        for lo, hi in ((0, 16), (32, 64), (64, P)):
+            nc.vector.memset(bytes_win[lo:hi, :].bitcast(I32), 0)
         nc.vector.memset(ones[:], 1.0)
+        x_bytes = keep.tile([P, S], U8, name="x_bytes", align_bytes=64)
+        nc.vector.memset(x_bytes[:].bitcast(I32), 0)
 
         nc.gpsimd.dma_start(gn_sb[:], gn.rearrange("(p t) o -> p (t o)", t=PACK))
         w1_rows = w1.rearrange("(p j) c -> p j c", j=PACK)
-        nc.sync.dma_start(w1_raw[0][:], w1_rows[:, :, : H // 2])
         nc.sync.dma_start(offs_sb[:], offs)
-        for q in range(4):
-            nc.sync.dma_start(bytes_win[q:P:32, :].bitcast(I32), x_scales[0, q:16:4, :].bitcast(I32))
+        nc.sync.dma_start(bytes_win[16:32, :].bitcast(I32), x_scales[0].bitcast(I32))
+        nc.sync.dma_start(w1_raw[0][:], w1_rows[:, :, : H // 2])
         nc.sync.dma_start(words[:], x_words[0].rearrange("p n t -> p (n t)").bitcast(I32))
         nc.sync.dma_start(w1_raw[1][:], w1_rows[:, :, H // 2 :])
         nc.sync.dma_start(nb_sb[:], nb)
-        nc.sync.dma_start(w2_raw[:], w2.rearrange("(p j) c -> p j c", j=PACK))
-        nc.sync.dma_start(dual_row[:], dual.rearrange("(p t) n -> p (t n)", t=PACK))
-        dual_sb = [dual_row[:, t * S : (t + 1) * S] for t in range(PACK)]
         nc.scalar.activation(warm[:], ones[:], ACT.Abs_reciprocal_sqrt, bias=ones[:])
 
-        x_bytes = keep.tile([P, S], U8, name="x_bytes", align_bytes=64)
+        picked = keep.tile([P, S], U8, name="picked", align_bytes=64)
         x_codes = keep.tile([P, S], U32, name="x_codes", align_bytes=64)
-        nc.vector.tensor_copy(x_bytes[:], bytes_win[:].indirect(offs_sb[:]))
+        nc.vector.tensor_copy(picked[:], bytes_win[:].indirect(offs_sb[:]))
+        for q in range(4):
+            nc.sync.dma_start(x_bytes[32 * q : 32 * q + 4, :].bitcast(I32), picked[16 + 4 * q : 20 + 4 * q, :].bitcast(I32))
+        w2_raw = keep.tile([P, PACK, N], F32, name="w2_raw", tag="bytes_win", align_bytes=64)
+        nc.sync.dma_start(w2_raw[:], w2.rearrange("(p j) c -> p j c", j=PACK))
 
         gq = keep.tile([P, PACK], F32, name="gq")
         ngq = keep.tile([P, PACK], F32, name="ngq")
@@ -86,6 +87,9 @@ def tile_picked_tvdual_none_p_kernel(tc, x_words, x_scales, w1, dual, gn, w2, of
             nc.scalar.copy(dst[0][g], src[0][:, :, :, 2 * g : 2 * g + 2])
         for t in range(2):
             quantise_early(t, 0)
+        dual_row = keep.tile([P, PACK * S], F32, name="dual_row", tag="early_bf0", align_bytes=64)
+        nc.sync.dma_start(dual_row[:], dual.rearrange("(p t) n -> p (t n)", t=PACK))
+        dual_sb = [dual_row[:, t * S : (t + 1) * S] for t in range(PACK)]
         nc.vector.tensor_copy(x_codes[:], words[:].bitcast(U32).indirect(offs_sb[:]))
         nc.scalar.copy(dst[1][0], src[1][:, :, :, 0:2])
         nc.vector.tensor_copy(dst[1][1], src[1][:, :, :, 2:4])

@@ -31,7 +31,7 @@ def tile_picked_tvdual_none_p_kernel(tc, x_words, x_scales, w1, dual, gn, w2, of
 
         offs_sb = keep.tile([P, S // 16], U16, name="offs_sb")
         nb_sb = keep.tile([P, S // 16], U16, name="nb_sb")
-        w1_raw = [keep.tile([P, PACK, H // 2], F32, name="w1_raw%d" % u) for u in range(2)]
+        w1_raw = [keep.tile([P, PACK, H // 2], F32, name="w1_raw%d" % u, tag="w1_raw%d" % u) for u in range(2)]
         gn_sb = keep.tile([P, PACK], F32, name="gn_sb")
         words = keep.tile([P, T], I32, name="words", tag="words", align_bytes=64)
         bytes_win = keep.tile([P, T], U8, name="bytes_win", tag="bytes_win", align_bytes=64)
@@ -54,13 +54,14 @@ def tile_picked_tvdual_none_p_kernel(tc, x_words, x_scales, w1, dual, gn, w2, of
         nc.sync.dma_start(nb_sb[:], nb)
         nc.scalar.activation(warm[:], ones[:], ACT.Abs_reciprocal_sqrt, bias=ones[:])
 
-        picked = keep.tile([P, S], U8, name="picked", align_bytes=64)
+        picked = keep.tile([P, S], U8, name="picked", tag="picked", align_bytes=64)
         x_codes = keep.tile([P, S], U32, name="x_codes", align_bytes=64)
         nc.vector.tensor_copy(picked[:], bytes_win[:].indirect(offs_sb[:]))
         for q in range(4):
             nc.sync.dma_start(x_bytes[32 * q : 32 * q + 4, :].bitcast(I32), picked[16 + 4 * q : 20 + 4 * q, :].bitcast(I32))
-        w2_raw = keep.tile([P, PACK, N], F32, name="w2_raw", tag="bytes_win", align_bytes=64)
-        nc.sync.dma_start(w2_raw[:], w2.rearrange("(p j) c -> p j c", j=PACK))
+        dual_rows = dual.rearrange("(p t) n -> p (t n)", t=PACK)
+        dual_lo = keep.tile([P, S], F32, name="dual_lo", tag="bytes_win", align_bytes=64)
+        nc.sync.dma_start(dual_lo[:], dual_rows[:, :S])
 
         gq = keep.tile([P, PACK], F32, name="gq")
         ngq = keep.tile([P, PACK], F32, name="ngq")
@@ -73,7 +74,8 @@ def tile_picked_tvdual_none_p_kernel(tc, x_words, x_scales, w1, dual, gn, w2, of
 
         early_bf = [keep.tile([P, 2, MH, PACK], BF16, name="early_bf%d" % u, tag="early_bf%d" % u, align_bytes=64) for u in range(2)]
         late_row = keep.tile([P, (PACK + 2) * HALF], F32, name="late_row", align_bytes=64)
-        late_bf = late_row[:, HALF : HALF + P * PACK].bitcast(BF16).rearrange("p (t m j) -> p t m j", t=2, j=PACK)
+        gained = keep.tile([P, 7 * HALF], F32, name="gained", tag="w2_codes", align_bytes=64)
+        late_bf = gained[:, : P * PACK].bitcast(BF16).rearrange("p (t m j) -> p t m j", t=2, j=PACK)
         early_codes = [keep.tile([P, P], U32, name="early_codes%d" % t, align_bytes=64) for t in range(2)]
         early_scales = [keep.tile([P, P], U8, name="early_scales%d" % t, align_bytes=64) for t in range(2)]
         src = [w1_raw[u][:].rearrange("p j (m t) -> p m j t", t=PACK) for u in range(2)]
@@ -87,20 +89,22 @@ def tile_picked_tvdual_none_p_kernel(tc, x_words, x_scales, w1, dual, gn, w2, of
             nc.scalar.copy(dst[0][g], src[0][:, :, :, 2 * g : 2 * g + 2])
         for t in range(2):
             quantise_early(t, 0)
-        dual_row = keep.tile([P, PACK * S], F32, name="dual_row", tag="early_bf0", align_bytes=64)
-        nc.sync.dma_start(dual_row[:], dual.rearrange("(p t) n -> p (t n)", t=PACK))
-        dual_sb = [dual_row[:, t * S : (t + 1) * S] for t in range(PACK)]
+        w2_raw = keep.tile([P, PACK, N], F32, name="w2_raw", tag="early_bf0", align_bytes=64)
+        nc.sync.dma_start(w2_raw[:], w2.rearrange("(p j) c -> p j c", j=PACK))
         nc.vector.tensor_copy(x_codes[:], words[:].bitcast(U32).indirect(offs_sb[:]))
+        dual_hi = keep.tile([P, 3 * S], F32, name="dual_hi", tag="words", align_bytes=64)
+        nc.sync.dma_start(dual_hi[:], dual_rows[:, S:])
+        dual_sb = [dual_lo[:]] + [dual_hi[:, i * S : (i + 1) * S] for i in range(3)]
         nc.scalar.copy(dst[1][0], src[1][:, :, :, 0:2])
         nc.vector.tensor_copy(dst[1][1], src[1][:, :, :, 2:4])
         for t in range(2):
             quantise_early(t, 1)
         late_codes = keep.tile([P, 2 * P], U32, name="late_codes", tag="early_bf1", align_bytes=64)
         late_scales = keep.tile([P, 2 * P], U8, name="late_scales", align_bytes=64)
-        nc.vector.quantize_mx(out=late_codes[:].bitcast(FP8X4), scales=late_scales[:], in_=late_row[:, HALF : HALF + P * PACK].bitcast(BF16))
+        nc.vector.quantize_mx(out=late_codes[:].bitcast(FP8X4), scales=late_scales[:], in_=gained[:, : P * PACK].bitcast(BF16))
         w1_codes = [early_codes[0][:], early_codes[1][:], late_codes[:, :P], late_codes[:, P:]]
         w1_scales = [early_scales[0][:], early_scales[1][:], late_scales[:, :P], late_scales[:, P:]]
-        ginv = keep.tile([P, PACK], F32, name="ginv", tag="words", align_bytes=64)
+        ginv = keep.tile([P, PACK], F32, name="ginv", tag="picked", align_bytes=64)
         nc.vector.reciprocal(ginv[:], gs[:])
 
         def first_product(t, c0, w, bank):
@@ -130,24 +134,17 @@ def tile_picked_tvdual_none_p_kernel(tc, x_words, x_scales, w1, dual, gn, w2, of
             for h in range(2):
                 y_half[t, h] = whole[t][:, h * HALF : (h + 1) * HALF]
 
-        w2_flat = late_row[:, HALF : HALF + N * PACK // 2].bitcast(BF16)
+        w2_flat = late_row[:, 2 * HALF : 2 * HALF + N * PACK // 2].bitcast(BF16)
         w2_bf = w2_flat.rearrange("p (c j) -> p c j", j=PACK)
-        nc.scalar.copy(
-            w2_bf[:, :W2_ON_SCALAR, :].rearrange("p (c i) j -> p c j i", i=2),
-            w2_raw[:, :, :W2_ON_SCALAR].rearrange("p j (c i) -> p c j i", i=2),
-        )
-        nc.gpsimd.tensor_scalar(w2_bf[:, W2_ON_SCALAR:, :], w2_raw[:, :, W2_ON_SCALAR:].rearrange("p j c -> p c j"), 1.0, 0.0, ALU.mult, ALU.add)
-        shared = keep.tile([P, S], F32, name="shared", tag="w2_codes", align_bytes=64)
         w2_scales = keep.tile([P, N], U8, name="w2_scales", align_bytes=64)
 
-        diff = [keep.tile([P, S], F32, name="diff%d" % t) for t in range(PACK)]
+        diff = keep.tile([P, PACK * S], F32, name="diff")
         recip = keep.tile([P, 2, PACK, HALF], F32, name="recip")
         fetched = {}
-        gained = [keep.tile([P, HALF], F32, name="gained%d" % t) for t in range(PACK - 1)]
         early_row = keep.tile([P, PACK * HALF], F32, name="early_row")
         num = [row[:, : PACK * HALF].rearrange("p (t n) -> p t n", t=PACK) for row in (early_row, late_row)]
         zb, zc, zs = {}, {}, {}
-        piece = {(t, h): diff[t][:, h * HALF : (h + 1) * HALF] for t in range(PACK) for h in range(2)}
+        piece = {(t, h): diff[:, (h * PACK + t) * HALF : (h * PACK + t + 1) * HALF] for t in range(PACK) for h in range(2)}
 
         def differences(*pieces):
             for i, (t, h) in enumerate(pieces):
@@ -175,16 +172,24 @@ def tile_picked_tvdual_none_p_kernel(tc, x_words, x_scales, w1, dual, gn, w2, of
             for (t, h), root in zip(pieces, roots):
                 square(t, h, root)
 
-        def add_gpsimd(t, h, scaled):
-            nc.gpsimd.tensor_tensor(num[h][:, t, :], scaled, piece[t, h], ALU.add)
+        def gain_gpsimd(t, halves):
+            both = gained[:, : 2 * PACK * HALF - HALF]
+            if halves == 1:
+                to = late_row[:, :HALF]
+                src_t = dual_sb[t][:, :HALF]
+            else:
+                to = both[:, t * HALF : (t + 5) * HALF].rearrange("p (h n) -> p h n", n=HALF)[:, 0:5:4, :]
+                src_t = dual_sb[t].rearrange("p (h n) -> p h n", n=HALF)
+            nc.gpsimd.tensor_scalar(to, src_t, gn_sb[:, t : t + 1], 0.0, ALU.mult, ALU.add)
 
-        def numerator_gpsimd(t):
-            nc.gpsimd.tensor_scalar(gained[t][:], dual_sb[t][:, :HALF], gn_sb[:, t : t + 1], 0.0, ALU.mult, ALU.add)
-            add_gpsimd(t, 0, gained[t][:])
+        def add_gpsimd(t, h, planes):
+            cols = slice((h * PACK + t) * HALF, (h * PACK + t + planes) * HALF)
+            row = (early_row, late_row)[h]
+            nc.gpsimd.tensor_tensor(row[:, t * HALF : (t + planes) * HALF], late_row[:, : 2 * HALF] if t == 2 else gained[:, cols], diff[:, cols], ALU.add)
 
         def numerator_vector(t, lo, hi):
             cols = slice(HALF + lo, HALF + hi)
-            nc.vector.scalar_tensor_tensor(num[1][:, t, lo:hi], dual_sb[t][:, cols], gn_sb[:, t : t + 1], diff[t][:, cols], ALU.mult, ALU.add)
+            nc.vector.scalar_tensor_tensor(num[1][:, t, lo:hi], dual_sb[t][:, cols], gn_sb[:, t : t + 1], piece[t, 1][:, lo:hi], ALU.mult, ALU.add)
 
         last = S // CHUNK - 1
         third_row = keep.tile([P, PACK * CHUNK], F32, name="third_row", align_bytes=64)
@@ -248,18 +253,27 @@ def tile_picked_tvdual_none_p_kernel(tc, x_words, x_scales, w1, dual, gn, w2, of
                     nc.vector.tensor_copy(res[:, mt, :], acc[:])
                     nc.sync.dma_start(out_rows(mt - 1, 2, last), res[:, mt - 1 : mt + 1, :])
 
+        gain_gpsimd(0, 2)
+        nc.scalar.copy(
+            w2_bf[:, :W2_ON_SCALAR, :].rearrange("p (c i) j -> p c j i", i=2),
+            w2_raw[:, :, :W2_ON_SCALAR].rearrange("p j (c i) -> p c j i", i=2),
+        )
+        nc.gpsimd.tensor_scalar(w2_bf[:, W2_ON_SCALAR:, :], w2_raw[:, :, W2_ON_SCALAR:].rearrange("p j c -> p c j"), 1.0, 0.0, ALU.mult, ALU.add)
+        gain_gpsimd(1, 2)
         differences((0, 0), (1, 0))
-        inverse([(0, 0), (1, 0)], [span(0), span(HALF)], [span(4 * HALF), shared[:, :HALF]])
-        nc.scalar.activation(span(4 * HALF), dual_sb[3][:, :HALF], ACT.Copy, scale=gn_sb[:, 3:4])
-        nc.scalar.activation(shared[:, :HALF], dual_sb[0][:, HALF:], ACT.Copy, scale=gn_sb[:, 0:1])
+        add_gpsimd(0, 0, 2)
+        held = [late_row[:, i * HALF : (i + 1) * HALF] for i in range(2)]
+        sizes_and_roots([(0, 0), (1, 0)], held, [span(4 * HALF), span(3 * HALF)])
+        for t in range(2, PACK):
+            nc.scalar.activation(held[t - 2], dual_sb[t][:, :HALF], ACT.Copy, scale=gn_sb[:, t : t + 1])
+        square(0, 0, span(4 * HALF))
+        square(1, 0, span(3 * HALF))
         differences((2, 0), (3, 0))
-        inverse([(2, 0), (3, 0)], [dual_sb[3][:, :HALF], dual_sb[0][:, HALF:]], [span(HALF // 2), shared[:, HALF:]])
-        for t in range(PACK - 1):
-            numerator_gpsimd(t)
-        add_gpsimd(3, 0, span(4 * HALF))
+        inverse([(2, 0), (3, 0)], [dual_sb[2][:, :HALF], dual_sb[3][:, :HALF]], [span(HALF // 2), gained[:, 6 * HALF :]])
+        add_gpsimd(2, 0, 2)
         differences((0, 1), (1, 1))
         inverse([(0, 1), (1, 1)], [span(0), span(HALF)], [span(2 * HALF), span(3 * HALF)])
-        add_gpsimd(0, 1, shared[:, :HALF])
+        add_gpsimd(0, 1, 2)
         differences((2, 1), (3, 1))
         for c in range(last + 1):
             rounded_tile(c)
@@ -270,10 +284,9 @@ def tile_picked_tvdual_none_p_kernel(tc, x_words, x_scales, w1, dual, gn, w2, of
         quantise(0)
         early_product(0, work[:, : PACK * CHUNK])
         quotient(1)
-        numerator_vector(1, 0, HALF)
+        numerator_vector(2, 0, CHUNK)
         quantise(1)
         early_product(1, late_row[:, PACK * HALF :])
-        numerator_vector(2, 0, CHUNK)
         numerator_vector(3, 0, CHUNK)
         numerator_vector(2, CHUNK, HALF)
         quotient(2)

@@ -195,10 +195,7 @@ def tile_picked_tvdual_none_p_kernel(tc, x_words, x_scales, w1, dual, gn, w2, of
         third_row = keep.tile([P, PACK * CHUNK], F32, name="third_row", align_bytes=64)
 
         def rounded_tile(c):
-            if c == last:
-                zb[c] = third_row[:, 2 * CHUNK :].bitcast(BF16)
-            else:
-                zb[c] = keep.tile([P, CHUNK * PACK], BF16, name="zb%d" % c, align_bytes=64)[:]
+            zb[c] = keep.tile([P, CHUNK * PACK], BF16, name="zb%d" % c, align_bytes=64)[:]
             zc[c] = keep.tile([P, CHUNK], U32, name="zc%d" % c, align_bytes=64)
             zs[c] = keep.tile([P, CHUNK], U8, name="zs%d" % c, align_bytes=64)
 
@@ -280,24 +277,24 @@ def tile_picked_tvdual_none_p_kernel(tc, x_words, x_scales, w1, dual, gn, w2, of
         quotient(0)
         w2_codes = keep.tile([P, N], U32, name="w2_codes", tag="w2_codes", align_bytes=64)
         nc.vector.quantize_mx(out=w2_codes[:].bitcast(FP8X4), scales=w2_scales[:], in_=w2_flat)
-        inverse([(2, 1), (3, 1)], [span(2 * HALF), span(3 * HALF)], [span(0), late_row[:, PACK * HALF - CHUNK : PACK * HALF + CHUNK]])
+        inverse([(2, 1), (3, 1)], [span(2 * HALF), span(3 * HALF)], [span(0), late_row[:, PACK * HALF : (PACK + 1) * HALF]])
         quantise(0)
         early_product(0, work[:, : PACK * CHUNK])
+        for t in range(2, PACK):
+            numerator_vector(t, 0, CHUNK)
         quotient(1)
-        numerator_vector(2, 0, CHUNK)
+        for t in range(2, PACK):
+            numerator_vector(t, CHUNK, HALF)
         quantise(1)
         early_product(1, late_row[:, PACK * HALF :])
-        numerator_vector(3, 0, CHUNK)
-        numerator_vector(2, CHUNK, HALF)
         quotient(2)
-        numerator_vector(3, CHUNK, HALF)
+        quotient(last, 0, CHUNK // 2)
         quantise(2)
         res, banks = third_product(2)
-        nc.scalar.copy(res[:, :2, :], banks[0][:])
-        for lo in (0, CHUNK // 2):
-            quotient(last, lo, lo + CHUNK // 2)
+        for u in range(2):
+            nc.scalar.copy(res[:, 2 * u : 2 * u + 2, :], banks[u][:])
+            nc.sync.dma_start(out_rows(2 * u, 2, 2), res[:, 2 * u : 2 * u + 2, :])
+        quotient(last, CHUNK // 2, CHUNK)
         for lo in (0, CHUNK // 2):
             quantise(last, lo, lo + CHUNK // 2)
-        nc.vector.tensor_copy(res[:, 2:, :], banks[1][:])
-        nc.sync.dma_start(out_rows(0, PACK, 2), res)
         last_product()

@@ -225,12 +225,15 @@ def tile_picked_tvdual_none_p_kernel(tc, x_words, x_scales, w1, dual, gn, w2, of
         def out_rows(mt0, n, c):
             return out[mt0 * P : (mt0 + n) * P, c * CHUNK : (c + 1) * CHUNK].rearrange("(mt p) n -> p mt n", p=P)
 
-        def early_product(c, res):
+        def early_product(c, res, pieces):
             acc = psum.tile([P, PACK * CHUNK], F32, name="acc", tag="bank%d" % (6 + c))
             for mt in range(PACK):
                 second_product(c, mt, acc[:, mt * CHUNK : (mt + 1) * CHUNK])
-            nc.scalar.copy(res, acc[:])
-            nc.sync.dma_start(out_rows(0, PACK, c), res.rearrange("p (m n) -> p m n", n=CHUNK))
+            tiles = PACK // pieces
+            for mt in range(0, PACK, tiles):
+                cols = slice(mt * CHUNK, (mt + tiles) * CHUNK)
+                nc.scalar.copy(res[:, cols], acc[:, cols])
+                nc.sync.dma_start(out_rows(mt, tiles, c), res[:, cols].rearrange("p (m n) -> p m n", n=CHUNK))
 
         def third_product(c):
             res = third_row[:].rearrange("p (m n) -> p m n", n=CHUNK)
@@ -240,15 +243,18 @@ def tile_picked_tvdual_none_p_kernel(tc, x_words, x_scales, w1, dual, gn, w2, of
             return res, banks
 
         def last_product():
-            res = keep.tile([P, PACK, CHUNK], F32, name="res_last")
-            for mt in range(PACK):
+            res = keep.tile([P, 2, CHUNK], F32, name="res_last")
+            for mt in (2, 3, 0, 1):
                 acc = psum.tile([P, CHUNK], F32, name="acc", tag="bank%d" % (mt + 1))
                 second_product(last, mt, acc[:])
+                to = res[:, mt, :] if mt < 2 else joint[:, mt - 2, CHUNK:]
                 if mt % 2 == 0:
-                    nc.scalar.copy(res[:, mt, :], acc[:])
+                    nc.scalar.copy(to, acc[:])
                 else:
-                    nc.vector.tensor_copy(res[:, mt, :], acc[:])
-                    nc.sync.dma_start(out_rows(mt - 1, 2, last), res[:, mt - 1 : mt + 1, :])
+                    nc.vector.tensor_copy(to, acc[:])
+                if mt == 3:
+                    nc.sync.dma_start(out[2 * P :, HALF:].rearrange("(mt p) n -> p mt n", p=P), joint[:])
+            nc.sync.dma_start(out_rows(0, 2, last), res[:])
 
         gain_gpsimd(0, 2)
         nc.scalar.copy(
@@ -279,21 +285,22 @@ def tile_picked_tvdual_none_p_kernel(tc, x_words, x_scales, w1, dual, gn, w2, of
         nc.vector.quantize_mx(out=w2_codes[:].bitcast(FP8X4), scales=w2_scales[:], in_=w2_flat)
         inverse([(2, 1), (3, 1)], [span(2 * HALF), span(3 * HALF)], [span(0), late_row[:, PACK * HALF : (PACK + 1) * HALF]])
         quantise(0)
-        early_product(0, work[:, : PACK * CHUNK])
+        early_product(0, work[:, : PACK * CHUNK], 2)
         for t in range(2, PACK):
             numerator_vector(t, 0, CHUNK)
         quotient(1)
         for t in range(2, PACK):
             numerator_vector(t, CHUNK, HALF)
         quantise(1)
-        early_product(1, late_row[:, PACK * HALF :])
+        early_product(1, late_row[:, PACK * HALF :], 1)
         quotient(2)
         quotient(last, 0, CHUNK // 2)
         quantise(2)
         res, banks = third_product(2)
-        for u in range(2):
-            nc.scalar.copy(res[:, 2 * u : 2 * u + 2, :], banks[u][:])
-            nc.sync.dma_start(out_rows(2 * u, 2, 2), res[:, 2 * u : 2 * u + 2, :])
+        joint = keep.tile([P, 2, HALF], F32, name="joint")
+        nc.scalar.copy(res[:, :2, :], banks[0][:])
+        nc.sync.dma_start(out_rows(0, 2, 2), res[:, :2, :])
+        nc.scalar.copy(joint[:, :, :CHUNK], banks[1][:])
         quotient(last, CHUNK // 2, CHUNK)
         for lo in (0, CHUNK // 2):
             quantise(last, lo, lo + CHUNK // 2)

@@ -20,7 +20,7 @@ PACK = 4
 HALF = S // 2
 CHUNK = 128
 MH = P // 2
-W2_ON_SCALAR = 80
+W2_ON_SCALAR = 112
 
 
 def tile_picked_tvdual_none_p_kernel(tc, x_words, x_scales, w1, dual, gn, w2, offs, nb, out):
@@ -74,7 +74,7 @@ def tile_picked_tvdual_none_p_kernel(tc, x_words, x_scales, w1, dual, gn, w2, of
 
         early_bf = [keep.tile([P, 2, MH, PACK], BF16, name="early_bf%d" % u, tag="early_bf%d" % u, align_bytes=64) for u in range(2)]
         late_row = keep.tile([P, (PACK + 2) * HALF], F32, name="late_row", align_bytes=64)
-        gained = keep.tile([P, 7 * HALF], F32, name="gained", tag="w2_codes", align_bytes=64)
+        gained = keep.tile([P, 6 * HALF], F32, name="gained", tag="w2_codes", align_bytes=64)
         late_bf = gained[:, : P * PACK].bitcast(BF16).rearrange("p (t m j) -> p t m j", t=2, j=PACK)
         early_codes = [keep.tile([P, P], U32, name="early_codes%d" % t, align_bytes=64) for t in range(2)]
         early_scales = [keep.tile([P, P], U8, name="early_scales%d" % t, align_bytes=64) for t in range(2)]
@@ -106,6 +106,8 @@ def tile_picked_tvdual_none_p_kernel(tc, x_words, x_scales, w1, dual, gn, w2, of
         w1_scales = [early_scales[0][:], early_scales[1][:], late_scales[:, :P], late_scales[:, P:]]
         ginv = keep.tile([P, PACK], F32, name="ginv", tag="picked", align_bytes=64)
         nc.vector.reciprocal(ginv[:], gs[:])
+        recip = keep.tile([P, 2, PACK, HALF], F32, name="recip")
+        nc.vector.reciprocal(recip[:, 0, 0, 0:1], gs[:, 2:3])
 
         def first_product(t, c0, w, bank):
             y = psum.tile([P, w], F32, name="y", tag="bank%d" % bank)
@@ -139,7 +141,6 @@ def tile_picked_tvdual_none_p_kernel(tc, x_words, x_scales, w1, dual, gn, w2, of
         w2_scales = keep.tile([P, N], U8, name="w2_scales", align_bytes=64)
 
         diff = keep.tile([P, PACK * S], F32, name="diff")
-        recip = keep.tile([P, 2, PACK, HALF], F32, name="recip")
         fetched = {}
         early_row = keep.tile([P, PACK * HALF], F32, name="early_row")
         num = [row[:, : PACK * HALF].rearrange("p (t n) -> p t n", t=PACK) for row in (early_row, late_row)]
@@ -164,6 +165,10 @@ def tile_picked_tvdual_none_p_kernel(tc, x_words, x_scales, w1, dual, gn, w2, of
             for size, root in zip(sizes, roots):
                 nc.scalar.activation(root, size, ACT.Abs_reciprocal_sqrt, bias=ones[:])
 
+        def sizes_of(pieces, sizes):
+            for i, (t, h) in enumerate(pieces):
+                nc.scalar.activation(sizes[:, i, :], piece[t, h], ACT.Abs, scale=recip[:, 0, 0, 0:1] if (t, h) == (2, 0) else ginv[:, t : t + 1])
+
         def square(t, h, root):
             nc.scalar.activation(recip[:, h, t, :], root, ACT.Square)
 
@@ -173,7 +178,7 @@ def tile_picked_tvdual_none_p_kernel(tc, x_words, x_scales, w1, dual, gn, w2, of
                 square(t, h, root)
 
         def gain_gpsimd(t, halves):
-            both = gained[:, : 2 * PACK * HALF - HALF]
+            both = gained[:]
             if halves == 1:
                 to = late_row[:, :HALF]
                 src_t = dual_sb[t][:, :HALF]
@@ -194,8 +199,14 @@ def tile_picked_tvdual_none_p_kernel(tc, x_words, x_scales, w1, dual, gn, w2, of
         last = S // CHUNK - 1
         third_row = keep.tile([P, PACK * CHUNK], F32, name="third_row", align_bytes=64)
 
+        joint_row = keep.tile([P, S], F32, name="joint_row", align_bytes=64)
+        joint = joint_row[:].rearrange("p (m n) -> p m n", n=HALF)
+
         def rounded_tile(c):
-            zb[c] = keep.tile([P, CHUNK * PACK], BF16, name="zb%d" % c, align_bytes=64)[:]
+            if c == last:
+                zb[c] = joint_row[:, CHUNK : 3 * CHUNK].bitcast(BF16)
+            else:
+                zb[c] = keep.tile([P, CHUNK * PACK], BF16, name="zb%d" % c, align_bytes=64)[:]
             zc[c] = keep.tile([P, CHUNK], U32, name="zc%d" % c, align_bytes=64)
             zs[c] = keep.tile([P, CHUNK], U8, name="zs%d" % c, align_bytes=64)
 
@@ -253,7 +264,7 @@ def tile_picked_tvdual_none_p_kernel(tc, x_words, x_scales, w1, dual, gn, w2, of
                 else:
                     nc.vector.tensor_copy(to, acc[:])
                 if mt == 3:
-                    nc.sync.dma_start(out[2 * P :, HALF:].rearrange("(mt p) n -> p mt n", p=P), joint[:])
+                    nc.sync.dma_start(out[2 * P :, HALF:].rearrange("(mt p) n -> p mt n", p=P), joint)
             nc.sync.dma_start(out_rows(0, 2, last), res[:])
 
         gain_gpsimd(0, 2)
@@ -266,16 +277,21 @@ def tile_picked_tvdual_none_p_kernel(tc, x_words, x_scales, w1, dual, gn, w2, of
         differences((0, 0), (1, 0))
         add_gpsimd(0, 0, 2)
         held = [late_row[:, i * HALF : (i + 1) * HALF] for i in range(2)]
-        sizes_and_roots([(0, 0), (1, 0)], held, [span(4 * HALF), span(3 * HALF)])
+        roots = [keep.tile([P, 2, HALF], F32, name="roots%d" % i) for i in range(2)]
+        sizes_and_roots([(0, 0), (1, 0)], held, [roots[0][:, 0, :], roots[0][:, 1, :]])
         for t in range(2, PACK):
             nc.scalar.activation(held[t - 2], dual_sb[t][:, :HALF], ACT.Copy, scale=gn_sb[:, t : t + 1])
-        square(0, 0, span(4 * HALF))
-        square(1, 0, span(3 * HALF))
         differences((2, 0), (3, 0))
-        inverse([(2, 0), (3, 0)], [dual_sb[2][:, :HALF], dual_sb[3][:, :HALF]], [span(HALF // 2), gained[:, 6 * HALF :]])
+        spent = dual_hi[:, S:].rearrange("p (t n) -> p t n", t=2)[:, :, :HALF]
+        second = gained[:, 2 * HALF : 4 * HALF].rearrange("p (t n) -> p t n", t=2)
+        sizes_of([(2, 0), (3, 0)], spent)
+        nc.scalar.activation(recip[:, 0, :2, :], roots[0][:], ACT.Square)
+        nc.scalar.activation(second, spent, ACT.Abs_reciprocal_sqrt, bias=ones[:])
         add_gpsimd(2, 0, 2)
         differences((0, 1), (1, 1))
-        inverse([(0, 1), (1, 1)], [span(0), span(HALF)], [span(2 * HALF), span(3 * HALF)])
+        sizes_of([(0, 1), (1, 1)], roots[0][:])
+        nc.scalar.activation(recip[:, 0, 2:, :], second, ACT.Square)
+        nc.scalar.activation(roots[1][:], roots[0][:], ACT.Abs_reciprocal_sqrt, bias=ones[:])
         add_gpsimd(0, 1, 2)
         differences((2, 1), (3, 1))
         for c in range(last + 1):
@@ -283,7 +299,13 @@ def tile_picked_tvdual_none_p_kernel(tc, x_words, x_scales, w1, dual, gn, w2, of
         quotient(0)
         w2_codes = keep.tile([P, N], U32, name="w2_codes", tag="w2_codes", align_bytes=64)
         nc.vector.quantize_mx(out=w2_codes[:].bitcast(FP8X4), scales=w2_scales[:], in_=w2_flat)
-        inverse([(2, 1), (3, 1)], [span(2 * HALF), span(3 * HALF)], [span(0), late_row[:, PACK * HALF : (PACK + 1) * HALF]])
+        sizes_of([(2, 1), (3, 1)], spent)
+        nc.scalar.activation(recip[:, 1, :2, :], roots[1][:], ACT.Square)
+        last_roots = [span(HALF // 2), late_row[:, PACK * HALF : (PACK + 1) * HALF]]
+        for i in range(2):
+            nc.scalar.activation(last_roots[i], spent[:, i, :], ACT.Abs_reciprocal_sqrt, bias=ones[:])
+        for i in range(2):
+            square(2 + i, 1, last_roots[i])
         quantise(0)
         early_product(0, work[:, : PACK * CHUNK], 2)
         for t in range(2, PACK):
@@ -297,11 +319,10 @@ def tile_picked_tvdual_none_p_kernel(tc, x_words, x_scales, w1, dual, gn, w2, of
         quotient(last, 0, CHUNK // 2)
         quantise(2)
         res, banks = third_product(2)
-        joint = keep.tile([P, 2, HALF], F32, name="joint")
         nc.scalar.copy(res[:, :2, :], banks[0][:])
         nc.sync.dma_start(out_rows(0, 2, 2), res[:, :2, :])
-        nc.scalar.copy(joint[:, :, :CHUNK], banks[1][:])
         quotient(last, CHUNK // 2, CHUNK)
         for lo in (0, CHUNK // 2):
             quantise(last, lo, lo + CHUNK // 2)
+        nc.vector.tensor_copy(joint[:, :, :CHUNK], banks[1][:])
         last_product()

@@ -96,7 +96,7 @@ def tile_picked_tvdual_none_p_kernel(tc, x_words, x_scales, w1, dual, gn, w2, of
         nc.sync.dma_start(dual_hi[:], dual_rows[:, S:])
         dual_sb = [dual_lo[:]] + [dual_hi[:, i * S : (i + 1) * S] for i in range(3)]
         nc.scalar.copy(dst[1][0], src[1][:, :, :, 0:2])
-        nc.vector.tensor_copy(dst[1][1], src[1][:, :, :, 2:4])
+        nc.scalar.copy(dst[1][1], src[1][:, :, :, 2:4])
         for t in range(2):
             quantise_early(t, 1)
         late_codes = keep.tile([P, 2 * P], U32, name="late_codes", tag="early_bf1", align_bytes=64)

@@ -54,7 +54,7 @@ def tile_picked_tvdual_none_p_kernel(tc, x_words, x_scales, w1, dual, gn, w2, of
         nc.sync.dma_start(nb_sb[:], nb)
         nc.scalar.activation(warm[:], ones[:], ACT.Abs_reciprocal_sqrt, bias=ones[:])
 
-        picked = keep.tile([P, S], U8, name="picked", tag="picked", align_bytes=64)
+        picked = keep.tile([P, S], U8, name="picked", align_bytes=64)
         x_codes = keep.tile([P, S], U32, name="x_codes", align_bytes=64)
         nc.vector.tensor_copy(picked[:], bytes_win[:].indirect(offs_sb[:]))
         for q in range(4):
@@ -71,6 +71,10 @@ def tile_picked_tvdual_none_p_kernel(tc, x_words, x_scales, w1, dual, gn, w2, of
         nc.gpsimd.tensor_scalar(ngq[:], gn_sb[:], -0.25, None, ALU.mult)
         nc.gpsimd.tensor_scalar(gz[:], gn_sb[:], 0.0, None, ALU.is_equal)
         nc.gpsimd.tensor_tensor(gs[:], gz[:], gn_sb[:], ALU.add)
+        recip_row = keep.tile([P, 2 * PACK + PACK * S], F32, name="recip_row")
+        recip = recip_row[:, 2 * PACK :].rearrange("p (h t n) -> p h t n", h=2, t=PACK)
+        ginv = recip_row[:, PACK : 2 * PACK]
+        nc.gpsimd.tensor_scalar(ginv[:, 0:1], gn_sb[:, 0:1], 0.25, None, ALU.mult)
 
         early_bf = [keep.tile([P, 2, MH, PACK], BF16, name="early_bf%d" % u, tag="early_bf%d" % u, align_bytes=64) for u in range(2)]
         late_row = keep.tile([P, (PACK + 2) * HALF], F32, name="late_row", align_bytes=64)
@@ -104,10 +108,6 @@ def tile_picked_tvdual_none_p_kernel(tc, x_words, x_scales, w1, dual, gn, w2, of
         nc.vector.quantize_mx(out=late_codes[:].bitcast(FP8X4), scales=late_scales[:], in_=gained[:, : P * PACK].bitcast(BF16))
         w1_codes = [early_codes[0][:], early_codes[1][:], late_codes[:, :P], late_codes[:, P:]]
         w1_scales = [early_scales[0][:], early_scales[1][:], late_scales[:, :P], late_scales[:, P:]]
-        ginv = keep.tile([P, PACK], F32, name="ginv", tag="picked", align_bytes=64)
-        nc.vector.reciprocal(ginv[:], gs[:])
-        recip = keep.tile([P, 2, PACK, HALF], F32, name="recip")
-        nc.vector.reciprocal(recip[:, 0, 0, 0:1], gs[:, 2:3])
 
         def first_product(t, c0, w, bank):
             y = psum.tile([P, w], F32, name="y", tag="bank%d" % bank)
@@ -129,7 +129,9 @@ def tile_picked_tvdual_none_p_kernel(tc, x_words, x_scales, w1, dual, gn, w2, of
                 y_half[t, h] = first_product(t, h * HALF, HALF, 2 * t + h)[:]
         whole = {t: first_product(t, 0, S, t + 2) for t in range(2, PACK)}
         for t in range(2):
-            nc.vector.tensor_scalar(win[t][:, :HALF], y_half[t, 0], gq[:, t : t + 1], None, ALU.mult)
+            nc.vector.tensor_scalar(win[t][:, :HALF], y_half[t, 0], ginv[:, 0:1] if t == 0 else gq[:, 1:2], None, ALU.mult)
+            if t == 0:
+                nc.vector.reciprocal(recip_row[:, PACK : 3 * PACK].rearrange("p (r t) -> p r t", r=2), gs[:].unsqueeze(1).to_broadcast([P, 2, PACK]))
             nc.scalar.activation(win[t][:, HALF:], y_half[t, 1], ACT.Copy, scale=gq[:, t : t + 1])
         for t in range(2, PACK):
             nc.scalar.activation(win[t][:], whole[t][:], ACT.Copy, scale=gq[:, t : t + 1])
@@ -167,7 +169,7 @@ def tile_picked_tvdual_none_p_kernel(tc, x_words, x_scales, w1, dual, gn, w2, of
 
         def sizes_of(pieces, sizes):
             for i, (t, h) in enumerate(pieces):
-                nc.scalar.activation(sizes[:, i, :], piece[t, h], ACT.Abs, scale=recip[:, 0, 0, 0:1] if (t, h) == (2, 0) else ginv[:, t : t + 1])
+                nc.scalar.activation(sizes[:, i, :], piece[t, h], ACT.Abs, scale=recip[:, 0, 0, 2:3] if (t, h) == (2, 0) else ginv[:, t : t + 1])
 
         def square(t, h, root):
             nc.scalar.activation(recip[:, h, t, :], root, ACT.Square)

from contextlib import ExitStack

import concourse.mybir as mybir

K, T, S, H, N = 512, 2048, 512, 512, 512
FLOPS = 2 * K * H * S + 2 * H * N * S

F32 = mybir.dt.float32
BF16 = mybir.dt.bfloat16
I32 = mybir.dt.int32
U32 = mybir.dt.uint32
U16 = mybir.dt.uint16
U8 = mybir.dt.uint8
FP8X4 = mybir.dt.float8_e4m3fn_x4
ALU = mybir.AluOpType
ACT = mybir.ActivationFunctionType

P = 128
PACK = 4
HALF = S // 2
CHUNK = 128
MH = P // 2
W2_ON_SCALAR = 112


def tile_picked_tvdual_none_p_kernel(tc, x_words, x_scales, w1, dual, gn, w2, offs, nb, out):
    nc = tc.nc
    with ExitStack() as ctx:
        keep = ctx.enter_context(tc.tile_pool(name="keep", bufs=1))
        psum = ctx.enter_context(tc.psum_pool(name="psum", bufs=1))

        offs_sb = keep.tile([P, S // 16], U16, name="offs_sb")
        nb_sb = keep.tile([P, S // 16], U16, name="nb_sb")
        w1_raw = [keep.tile([P, PACK, H // 2], F32, name="w1_raw%d" % u, tag="w1_raw%d" % u) for u in range(2)]
        gn_sb = keep.tile([P, PACK], F32, name="gn_sb")
        words = keep.tile([P, T], I32, name="words", tag="words", align_bytes=64)
        bytes_win = keep.tile([P, T], U8, name="bytes_win", tag="bytes_win", align_bytes=64)
        ones = keep.tile([P, 1], F32, name="ones")
        warm = keep.tile([P, 1], F32, name="warm")

        for lo, hi in ((0, 16), (32, 64), (64, P)):
            nc.vector.memset(bytes_win[lo:hi, :].bitcast(I32), 0)
        nc.vector.memset(ones[:], 1.0)
        x_bytes = keep.tile([P, S], U8, name="x_bytes", align_bytes=64)
        nc.vector.memset(x_bytes[:].bitcast(I32), 0)

        nc.gpsimd.dma_start(gn_sb[:], gn.rearrange("(p t) o -> p (t o)", t=PACK))
        w1_rows = w1.rearrange("(p j) c -> p j c", j=PACK)
        nc.sync.dma_start(offs_sb[:], offs)
        nc.sync.dma_start(bytes_win[16:32, :].bitcast(I32), x_scales[0].bitcast(I32))
        nc.sync.dma_start(w1_raw[0][:], w1_rows[:, :, : H // 2])
        nc.sync.dma_start(words[:], x_words[0].rearrange("p n t -> p (n t)").bitcast(I32))
        nc.sync.dma_start(w1_raw[1][:], w1_rows[:, :, H // 2 :])
        nc.sync.dma_start(nb_sb[:], nb)
        nc.scalar.activation(warm[:], ones[:], ACT.Abs_reciprocal_sqrt, bias=ones[:])

        picked = keep.tile([P, S], U8, name="picked", align_bytes=64)
        x_codes = keep.tile([P, S], U32, name="x_codes", align_bytes=64)
        nc.vector.tensor_copy(picked[:], bytes_win[:].indirect(offs_sb[:]))
        for q in range(4):
            nc.sync.dma_start(x_bytes[32 * q : 32 * q + 4, :].bitcast(I32), picked[16 + 4 * q : 20 + 4 * q, :].bitcast(I32))
        dual_rows = dual.rearrange("(p t) n -> p (t n)", t=PACK)
        dual_lo = keep.tile([P, S], F32, name="dual_lo", tag="bytes_win", align_bytes=64)
        nc.sync.dma_start(dual_lo[:], dual_rows[:, :S])

        gq = keep.tile([P, PACK], F32, name="gq")
        ngq = keep.tile([P, PACK], F32, name="ngq")
        gz = keep.tile([P, PACK], F32, name="gz")
        gs = keep.tile([P, PACK], F32, name="gs")
        nc.gpsimd.tensor_scalar(gq[:], gn_sb[:], 0.25, None, ALU.mult)
        nc.gpsimd.tensor_scalar(ngq[:], gn_sb[:], -0.25, None, ALU.mult)
        nc.gpsimd.tensor_scalar(gz[:], gn_sb[:], 0.0, None, ALU.is_equal)
        nc.gpsimd.tensor_tensor(gs[:], gz[:], gn_sb[:], ALU.add)
        recip_row = keep.tile([P, 2 * PACK + PACK * S], F32, name="recip_row")
        recip = recip_row[:, 2 * PACK :].rearrange("p (h t n) -> p h t n", h=2, t=PACK)
        ginv = recip_row[:, PACK : 2 * PACK]
        nc.gpsimd.tensor_scalar(ginv[:, 0:1], gn_sb[:, 0:1], 0.25, None, ALU.mult)

        early_bf = [keep.tile([P, 2, MH, PACK], BF16, name="early_bf%d" % u, tag="early_bf%d" % u, align_bytes=64) for u in range(2)]
        late_row = keep.tile([P, (PACK + 2) * HALF], F32, name="late_row", align_bytes=64)
        gained = keep.tile([P, 6 * HALF], F32, name="gained", tag="w2_codes", align_bytes=64)
        late_bf = gained[:, : P * PACK].bitcast(BF16).rearrange("p (t m j) -> p t m j", t=2, j=PACK)
        early_codes = [keep.tile([P, P], U32, name="early_codes%d" % t, align_bytes=64) for t in range(2)]
        early_scales = [keep.tile([P, P], U8, name="early_scales%d" % t, align_bytes=64) for t in range(2)]
        src = [w1_raw[u][:].rearrange("p j (m t) -> p m j t", t=PACK) for u in range(2)]
        dst = [[early_bf[u][:].rearrange("p t m j -> p m j t"), late_bf[:, :, u * MH : (u + 1) * MH, :].rearrange("p t m j -> p m j t")] for u in range(2)]

        def quantise_early(t, u):
            cols = slice(u * MH, (u + 1) * MH)
            nc.vector.quantize_mx(out=early_codes[t][:, cols].bitcast(FP8X4), scales=early_scales[t][:, cols], in_=early_bf[u][:, t].rearrange("p m j -> p (m j)"))

        for g in range(2):
            nc.scalar.copy(dst[0][g], src[0][:, :, :, 2 * g : 2 * g + 2])
        for t in range(2):
            quantise_early(t, 0)
        w2_raw = keep.tile([P, PACK, N], F32, name="w2_raw", tag="early_bf0", align_bytes=64)
        nc.sync.dma_start(w2_raw[:], w2.rearrange("(p j) c -> p j c", j=PACK))
        nc.vector.tensor_copy(x_codes[:], words[:].bitcast(U32).indirect(offs_sb[:]))
        dual_hi = keep.tile([P, 3 * S], F32, name="dual_hi", tag="words", align_bytes=64)
        nc.sync.dma_start(dual_hi[:], dual_rows[:, S:])
        dual_sb = [dual_lo[:]] + [dual_hi[:, i * S : (i + 1) * S] for i in range(3)]
        nc.scalar.copy(dst[1][0], src[1][:, :, :, 0:2])
        nc.scalar.copy(dst[1][1], src[1][:, :, :, 2:4])
        for t in range(2):
            quantise_early(t, 1)
        late_codes = keep.tile([P, 2 * P], U32, name="late_codes", tag="early_bf1", align_bytes=64)
        late_scales = keep.tile([P, 2 * P], U8, name="late_scales", align_bytes=64)
        nc.vector.quantize_mx(out=late_codes[:].bitcast(FP8X4), scales=late_scales[:], in_=gained[:, : P * PACK].bitcast(BF16))
        w1_codes = [early_codes[0][:], early_codes[1][:], late_codes[:, :P], late_codes[:, P:]]
        w1_scales = [early_scales[0][:], early_scales[1][:], late_scales[:, :P], late_scales[:, P:]]

        def first_product(t, c0, w, bank):
            y = psum.tile([P, w], F32, name="y", tag="bank%d" % bank)
            nc.tensor.matmul_mx(
                out=y[:],
                lhsT=w1_codes[t].bitcast(FP8X4),
                lhsT_scale=w1_scales[t],
                rhs=x_codes[:, c0 : c0 + w].bitcast(FP8X4),
                rhs_scale=x_bytes[:, c0 : c0 + w],
                start=True,
                stop=True,
            )
            return y

        win = [keep.tile([P, S], F32, name="win%d" % t) for t in range(PACK)]
        y_half = {}
        for t in range(2):
            for h in range(2):
                y_half[t, h] = first_product(t, h * HALF, HALF, 2 * t + h)[:]
        whole = {t: first_product(t, 0, S, t + 2) for t in range(2, PACK)}
        for t in range(2):
            nc.vector.tensor_scalar(win[t][:, :HALF], y_half[t, 0], ginv[:, 0:1] if t == 0 else gq[:, 1:2], None, ALU.mult)
            if t == 0:
                nc.vector.reciprocal(recip_row[:, PACK : 3 * PACK].rearrange("p (r t) -> p r t", r=2), gs[:].unsqueeze(1).to_broadcast([P, 2, PACK]))
            nc.scalar.activation(win[t][:, HALF:], y_half[t, 1], ACT.Copy, scale=gq[:, t : t + 1])
        for t in range(2, PACK):
            nc.scalar.activation(win[t][:], whole[t][:], ACT.Copy, scale=gq[:, t : t + 1])
            for h in range(2):
                y_half[t, h] = whole[t][:, h * HALF : (h + 1) * HALF]

        w2_flat = late_row[:, 2 * HALF : 2 * HALF + N * PACK // 2].bitcast(BF16)
        w2_bf = w2_flat.rearrange("p (c j) -> p c j", j=PACK)
        w2_scales = keep.tile([P, N], U8, name="w2_scales", align_bytes=64)

        diff = keep.tile([P, PACK * S], F32, name="diff")
        fetched = {}
        early_row = keep.tile([P, PACK * HALF], F32, name="early_row")
        num = [row[:, : PACK * HALF].rearrange("p (t n) -> p t n", t=PACK) for row in (early_row, late_row)]
        zb, zc, zs = {}, {}, {}
        piece = {(t, h): diff[:, (h * PACK + t) * HALF : (h * PACK + t + 1) * HALF] for t in range(PACK) for h in range(2)}

        def differences(*pieces):
            for i, (t, h) in enumerate(pieces):
                fetched[t, h] = keep.tile([P, HALF], F32, name="fetched", tag="fetched%d" % i)
                nc.vector.tensor_copy(fetched[t, h][:], win[t][:].indirect(nb_sb[:, h * HALF // 16 : (h + 1) * HALF // 16]))
            for t, h in pieces:
                nc.vector.scalar_tensor_tensor(piece[t, h], y_half[t, h], ngq[:, t : t + 1], fetched[t, h][:], ALU.mult, ALU.add)

        work = keep.tile([P, 5 * HALF], F32, name="work")

        def span(first):
            return work[:, first : first + HALF]

        def sizes_and_roots(pieces, sizes, roots):
            for (t, h), size in zip(pieces, sizes):
                nc.scalar.activation(size, piece[t, h], ACT.Abs, scale=ginv[:, t : t + 1])
            for size, root in zip(sizes, roots):
                nc.scalar.activation(root, size, ACT.Abs_reciprocal_sqrt, bias=ones[:])

        def sizes_of(pieces, sizes):
            for i, (t, h) in enumerate(pieces):
                nc.scalar.activation(sizes[:, i, :], piece[t, h], ACT.Abs, scale=recip[:, 0, 0, 2:3] if (t, h) == (2, 0) else ginv[:, t : t + 1])

        def square(t, h, root):
            nc.scalar.activation(recip[:, h, t, :], root, ACT.Square)

        def inverse(pieces, sizes, roots):
            sizes_and_roots(pieces, sizes, roots)
            for (t, h), root in zip(pieces, roots):
                square(t, h, root)

        def gain_gpsimd(t, halves):
            both = gained[:]
            if halves == 1:
                to = late_row[:, :HALF]
                src_t = dual_sb[t][:, :HALF]
            else:
                to = both[:, t * HALF : (t + 5) * HALF].rearrange("p (h n) -> p h n", n=HALF)[:, 0:5:4, :]
                src_t = dual_sb[t].rearrange("p (h n) -> p h n", n=HALF)
            nc.gpsimd.tensor_scalar(to, src_t, gn_sb[:, t : t + 1], 0.0, ALU.mult, ALU.add)

        def add_gpsimd(t, h, planes):
            cols = slice((h * PACK + t) * HALF, (h * PACK + t + planes) * HALF)
            row = (early_row, late_row)[h]
            nc.gpsimd.tensor_tensor(row[:, t * HALF : (t + planes) * HALF], late_row[:, : 2 * HALF] if t == 2 else gained[:, cols], diff[:, cols], ALU.add)

        def numerator_vector(t, lo, hi):
            cols = slice(HALF + lo, HALF + hi)
            nc.vector.scalar_tensor_tensor(num[1][:, t, lo:hi], dual_sb[t][:, cols], gn_sb[:, t : t + 1], piece[t, 1][:, lo:hi], ALU.mult, ALU.add)

        last = S // CHUNK - 1
        third_row = keep.tile([P, PACK * CHUNK], F32, name="third_row", align_bytes=64)

        joint_row = keep.tile([P, S], F32, name="joint_row", align_bytes=64)
        joint = joint_row[:].rearrange("p (m n) -> p m n", n=HALF)

        def rounded_tile(c):
            if c == last:
                zb[c] = joint_row[:, CHUNK : 3 * CHUNK].bitcast(BF16)
            else:
                zb[c] = keep.tile([P, CHUNK * PACK], BF16, name="zb%d" % c, align_bytes=64)[:]
            zc[c] = keep.tile([P, CHUNK], U32, name="zc%d" % c, align_bytes=64)
            zs[c] = keep.tile([P, CHUNK], U8, name="zs%d" % c, align_bytes=64)

        def quotient(c, lo=0, hi=CHUNK):
            h, r0 = c * CHUNK // HALF, c * CHUNK % HALF
            nc.vector.tensor_tensor(
                zb[c][:, lo * PACK : hi * PACK].rearrange("p (c i t) -> p c t i", i=2, t=PACK),
                num[h][:, :, r0 + lo : r0 + hi].rearrange("p t (c i) -> p c t i", i=2),
                recip[:, h, :, r0 + lo : r0 + hi].rearrange("p t (c i) -> p c t i", i=2),
                ALU.mult,
            )

        def quantise(c, lo=0, hi=CHUNK):
            nc.vector.quantize_mx(out=zc[c][:, lo:hi].bitcast(FP8X4), scales=zs[c][:, lo:hi], in_=zb[c][:, lo * PACK : hi * PACK])

        def second_product(c, mt, acc):
            nc.tensor.matmul_mx(
                out=acc,
                lhsT=w2_codes[:, mt * P : (mt + 1) * P].bitcast(FP8X4),
                lhsT_scale=w2_scales[:, mt * P : (mt + 1) * P],
                rhs=zc[c][:].bitcast(FP8X4),
                rhs_scale=zs[c][:],
                start=True,
                stop=True,
            )

        def out_rows(mt0, n, c):
            return out[mt0 * P : (mt0 + n) * P, c * CHUNK : (c + 1) * CHUNK].rearrange("(mt p) n -> p mt n", p=P)

        def early_product(c, res, pieces):
            acc = psum.tile([P, PACK * CHUNK], F32, name="acc", tag="bank%d" % (6 + c))
            for mt in range(PACK):
                second_product(c, mt, acc[:, mt * CHUNK : (mt + 1) * CHUNK])
            tiles = PACK // pieces
            for mt in range(0, PACK, tiles):
                cols = slice(mt * CHUNK, (mt + tiles) * CHUNK)
                nc.scalar.copy(res[:, cols], acc[:, cols])
                nc.sync.dma_start(out_rows(mt, tiles, c), res[:, cols].rearrange("p (m n) -> p m n", n=CHUNK))

        def third_product(c):
            res = third_row[:].rearrange("p (m n) -> p m n", n=CHUNK)
            banks = [psum.tile([P, 2, CHUNK], F32, name="acc", tag="bank%d" % (5 * u)) for u in range(2)]
            for mt in range(PACK):
                second_product(c, mt, banks[mt // 2][:, mt % 2, :])
            return res, banks

        def last_product():
            res = keep.tile([P, 2, CHUNK], F32, name="res_last")
            for mt in (2, 3, 0, 1):
                acc = psum.tile([P, CHUNK], F32, name="acc", tag="bank%d" % (mt + 1))
                second_product(last, mt, acc[:])
                to = res[:, mt, :] if mt < 2 else joint[:, mt - 2, CHUNK:]
                if mt % 2 == 0:
                    nc.scalar.copy(to, acc[:])
                else:
                    nc.vector.tensor_copy(to, acc[:])
                if mt == 3:
                    nc.sync.dma_start(out[2 * P :, HALF:].rearrange("(mt p) n -> p mt n", p=P), joint)
            nc.sync.dma_start(out_rows(0, 2, last), res[:])

        gain_gpsimd(0, 2)
        nc.scalar.copy(
            w2_bf[:, :W2_ON_SCALAR, :].rearrange("p (c i) j -> p c j i", i=2),
            w2_raw[:, :, :W2_ON_SCALAR].rearrange("p j (c i) -> p c j i", i=2),
        )
        nc.gpsimd.tensor_scalar(w2_bf[:, W2_ON_SCALAR:, :], w2_raw[:, :, W2_ON_SCALAR:].rearrange("p j c -> p c j"), 1.0, 0.0, ALU.mult, ALU.add)
        gain_gpsimd(1, 2)
        differences((0, 0), (1, 0))
        add_gpsimd(0, 0, 2)
        held = [late_row[:, i * HALF : (i + 1) * HALF] for i in range(2)]
        roots = [keep.tile([P, 2, HALF], F32, name="roots%d" % i) for i in range(2)]
        sizes_and_roots([(0, 0), (1, 0)], held, [roots[0][:, 0, :], roots[0][:, 1, :]])
        for t in range(2, PACK):
            nc.scalar.activation(held[t - 2], dual_sb[t][:, :HALF], ACT.Copy, scale=gn_sb[:, t : t + 1])
        differences((2, 0), (3, 0))
        spent = dual_hi[:, S:].rearrange("p (t n) -> p t n", t=2)[:, :, :HALF]
        second = gained[:, 2 * HALF : 4 * HALF].rearrange("p (t n) -> p t n", t=2)
        sizes_of([(2, 0), (3, 0)], spent)
        nc.scalar.activation(recip[:, 0, :2, :], roots[0][:], ACT.Square)
        nc.scalar.activation(second, spent, ACT.Abs_reciprocal_sqrt, bias=ones[:])
        add_gpsimd(2, 0, 2)
        differences((0, 1), (1, 1))
        sizes_of([(0, 1), (1, 1)], roots[0][:])
        nc.scalar.activation(recip[:, 0, 2:, :], second, ACT.Square)
        nc.scalar.activation(roots[1][:], roots[0][:], ACT.Abs_reciprocal_sqrt, bias=ones[:])
        add_gpsimd(0, 1, 2)
        differences((2, 1), (3, 1))
        for c in range(last + 1):
            rounded_tile(c)
        quotient(0)
        w2_codes = keep.tile([P, N], U32, name="w2_codes", tag="w2_codes", align_bytes=64)
        nc.vector.quantize_mx(out=w2_codes[:].bitcast(FP8X4), scales=w2_scales[:], in_=w2_flat)
        sizes_of([(2, 1), (3, 1)], spent)
        nc.scalar.activation(recip[:, 1, :2, :], roots[1][:], ACT.Square)
        last_roots = [span(HALF // 2), late_row[:, PACK * HALF : (PACK + 1) * HALF]]
        for i in range(2):
            nc.scalar.activation(last_roots[i], spent[:, i, :], ACT.Abs_reciprocal_sqrt, bias=ones[:])
        for i in range(2):
            square(2 + i, 1, last_roots[i])
        quantise(0)
        early_product(0, work[:, : PACK * CHUNK], 2)
        for t in range(2, PACK):
            numerator_vector(t, 0, CHUNK)
        quotient(1)
        for t in range(2, PACK):
            numerator_vector(t, CHUNK, HALF)
        quantise(1)
        early_product(1, late_row[:, PACK * HALF :], 1)
        quotient(2)
        quotient(last, 0, CHUNK // 2)
        quantise(2)
        res, banks = third_product(2)
        nc.scalar.copy(res[:, :2, :], banks[0][:])
        nc.sync.dma_start(out_rows(0, 2, 2), res[:, :2, :])
        quotient(last, CHUNK // 2, CHUNK)
        for lo in (0, CHUNK // 2):
            quantise(last, lo, lo + CHUNK // 2)
        nc.vector.tensor_copy(joint[:, :, :CHUNK], banks[1][:])
        last_product()
